import numpy as np
import ml_dtypes


def mxq(x, axis, fmt="e4m3"):
    dtype, down = {"e4m3": (ml_dtypes.float8_e4m3fn, 7), "e5m2": (ml_dtypes.float8_e5m2, 14)}[fmt]
    v = np.moveaxis(np.asarray(x, np.float32).astype(ml_dtypes.bfloat16).astype(np.float64), axis, -1)
    blocks = v.reshape(v.shape[:-1] + (-1, 32))
    amax = np.abs(blocks).max(-1, keepdims=True)
    byte = np.maximum(np.where(amax > 0, np.frexp(amax)[1] - 1 + 127, 0) - down, 1)
    scale = np.exp2(byte - 127.0)
    codes = (blocks / scale).astype(np.float32).astype(dtype).astype(np.float64)
    return np.moveaxis((codes * scale).reshape(v.shape), -1, axis)


WIDE = False


def mx_kscale(k):
    if not WIDE:
        return np.ones(k)
    levels = np.array([10, -10, 5, -5, 0])
    if k % 512:
        return np.exp2(np.random.permutation(np.resize(levels, k // 32))).repeat(32)
    a = np.empty((k // 512, 16))
    for p in range(k // 512):
        a[p, :8] = np.random.permutation(np.resize(levels, 8))
        for g in range(8):
            far = levels[np.abs(levels - a[p, g]) >= 10]
            a[p, g + 8] = far[np.random.randint(len(far))]
    return np.exp2(a.ravel()).repeat(32)


def f64(x):
    return np.asarray(x).astype(np.float64)


def striped(idx):
    return np.tile(idx.reshape(-1, 16).T, (8, 1)).astype(np.uint16)


def unstriped(offs):
    return offs[:16].T.reshape(-1).astype(np.int64)


E2M1 = np.array([0.0, 0.5, 1.0, 1.5, 2.0, 3.0, 4.0, 6.0, -0.0, -0.5, -1.0, -1.5, -2.0, -3.0, -4.0, -6.0])


def pack_weight(w, fmt):
    k, n = w.shape
    w = f64(np.asarray(w, np.float32).astype(ml_dtypes.bfloat16)).reshape(k // 32, 32, n)
    amax = np.abs(w).max(1)
    if fmt == "e4m3":
        byte = np.frexp(amax)[1] - 1 + 127 - 7
    else:
        mant, ex = np.frexp(amax / 6.0)
        byte = np.where(mant > 0.5, ex, ex - 1) + 127
    byte = np.clip(np.where(amax > 0, byte, 1), 1, 254)
    scaled = (w * np.exp2(127.0 - byte)[:, None, :]).reshape(k, n).astype(np.float32)
    by_word = np.ascontiguousarray(scaled.reshape(k // 512, 128, 4, n).transpose(0, 1, 3, 2))
    if fmt == "e4m3":
        words = by_word.astype(ml_dtypes.float8_e4m3fn).view(np.uint8)
    else:
        c = by_word.astype(ml_dtypes.float4_e2m1fn).view(np.uint8) & 0xF
        words = (c[..., 0::2] | (c[..., 1::2] << 4)).reshape(k // 512, 128, 2 * n)
    return np.ascontiguousarray(words), np.ascontiguousarray(byte.astype(np.uint8).reshape(k // 512, 16, n))


def unpack_weight(words, scales, fmt):
    g, _, n = scales.shape
    words = np.ascontiguousarray(words).reshape(g, 128, n, -1)
    if fmt == "e4m3":
        vals = words.view(ml_dtypes.float8_e4m3fn).astype(np.float64)
    else:
        nib = np.empty((g, 128, n, 4), np.uint8)
        nib[..., 0::2] = words & 0xF
        nib[..., 1::2] = words >> 4
        vals = E2M1[nib]
    vals = vals * np.repeat(np.exp2(scales.astype(np.float64) - 127.0), 8, axis=1)[..., None]
    return vals.transpose(0, 1, 3, 2).reshape(g * 512, n)


def planes(y):
    n, m = y.shape
    v = y.astype(np.float32).astype(ml_dtypes.bfloat16).astype(np.float64).reshape(n // 32, 32, m)
    top = np.abs(v).max(1)
    byte = np.clip(np.where(top > 0, np.frexp(top)[1] - 1 + 127 - 7, 1), 1, 254)
    codes = (v * np.exp2(127.0 - byte)[:, None, :]).reshape(n, m).astype(np.float32).astype(ml_dtypes.float8_e4m3fn).view(np.uint8)
    words = codes.reshape(n // 512, 128, 4, m).transpose(0, 1, 3, 2)
    return np.ascontiguousarray(words), np.ascontiguousarray(byte.astype(np.uint8).reshape(n // 512, 16, m))


def gelu(v):
    return 0.5 * v * (1.0 + np.tanh(np.sqrt(2.0 / np.pi) * (v + 0.044715 * v**3)))


K, T, E, B, H, N = 512, 768, 8, 6, 512, 512


def setup_inputs():
    n = np.random.standard_normal
    s = mx_kscale(K)
    u = mx_kscale(H)
    slot_token = np.random.permutation(T)[:128 * B]
    block = np.sort(np.random.randint(E, size=B))
    x = pack_weight(n((K, T)) * s[:, None], "e4m3")
    w = pack_weight(n((K, N)) / np.sqrt(K) / s[:, None], "e2m1")
    wa = pack_weight(n((K, E * H)) / np.sqrt(K) / s[:, None] * np.tile(u, E), "e4m3")
    wb = pack_weight(n((H, E * N)) / np.sqrt(H) / u[:, None], "e4m3")
    return {
        "x_words": x[0],
        "x_scales": x[1],
        "w_words": w[0],
        "w_scales": w[1],
        "wa_words": wa[0],
        "wa_scales": wa[1],
        "wb_words": wb[0],
        "wb_scales": wb[1],
        "gate": (np.tile(np.random.uniform(0.2, 1.0, 128 * B), (128, 1))).astype(np.float32),
        "offs": striped(slot_token),
        "offs2": striped((block[:, None] * H + np.arange(H)).reshape(-1)),
        "offs3": striped((block[:, None] * N + np.arange(N)).reshape(-1)),
    }


def reference(x_words, x_scales, w_words, w_scales, wa_words, wa_scales, wb_words, wb_scales, gate, offs, offs2, offs3):
    w = unpack_weight(w_words, w_scales, "e2m1")
    idx, idx2, idx3 = unstriped(offs), unstriped(offs2), unstriped(offs3)
    x = unpack_weight(x_words, x_scales, "e4m3")
    out = w.T @ x
    wa = unpack_weight(wa_words, wa_scales, "e4m3")[:, idx2]
    wb = unpack_weight(wb_words, wb_scales, "e4m3")[:, idx3]
    xq = x[:, idx]
    h = np.concatenate([wa[:, m * H:(m + 1) * H].T @ xq[:, 128 * m:128 * m + 128] for m in range(B)], axis=1)
    hq = mxq(gelu(h), 0, "e4m3")
    y = np.concatenate([wb[:, m * N:(m + 1) * N].T @ hq[:, 128 * m:128 * m + 128] for m in range(B)], axis=1)
    out[:, idx] += f64(gate[:1]) * y
    out_0 = out
    return (out_0,) + planes(out_0)

@@ -1,0 +1,244 @@
+from contextlib import ExitStack
+
+import concourse.mybir as mybir
+from concourse.masks import make_identity
+
+K, T, E, B, H, N = 512, 768, 8, 6, 512, 512
+FLOPS = 2 * K * N * T + 2 * K * H * T + 2 * H * N * T
+
+F32 = mybir.dt.float32
+BF16 = mybir.dt.bfloat16
+I32 = mybir.dt.int32
+U32 = mybir.dt.uint32
+U16 = mybir.dt.uint16
+U8 = mybir.dt.uint8
+FP8X4 = mybir.dt.float8_e4m3fn_x4
+FP4X4 = mybir.dt.float4_e2m1fn_x4
+ACT = mybir.ActivationFunctionType
+ADD = mybir.AluOpType.add
+
+P = 128
+POOL = E * H
+PER_COL = 16
+
+
+def tile_moe_dyl_gelu_kernel(
+    tc, x_words, x_scales, w_words, w_scales, wa_words, wa_scales, wb_words, wb_scales,
+    gate, offs, offs2, offs3, out_0, out_1, out_2,
+):
+    nc = tc.nc
+    with ExitStack() as ctx:
+        lists = ctx.enter_context(tc.tile_pool(name="lists", bufs=1))
+        keep = ctx.enter_context(tc.tile_pool(name="keep", bufs=1))
+        ring = ctx.enter_context(tc.tile_pool(name="ring", bufs=3))
+        psum = ctx.enter_context(tc.psum_pool(name="psum", bufs=3))
+        psum_keep = ctx.enter_context(tc.psum_pool(name="psum_keep", bufs=1))
+
+        tok_list = lists.tile([P, T // PER_COL], U16, name="tok_list")
+        a_list = lists.tile([P, B * H // PER_COL], U16, name="a_list")
+        b_list = lists.tile([P, B * N // PER_COL], U16, name="b_list")
+
+        x_w = keep.tile([P, T], I32, name="x_w", align_bytes=64)
+        x_s = keep.tile([P, T], U8, name="x_s", align_bytes=64)
+        w_w = keep.tile([P, 2 * N], U8, name="w_w", align_bytes=64)
+        w_s = keep.tile([P, N], U8, name="w_s", align_bytes=64)
+        wa_w = keep.tile([P, POOL], I32, name="wa_w", align_bytes=64)
+        wa_s = keep.tile([P, POOL], U8, name="wa_s", align_bytes=64)
+        wb_w = keep.tile([P, POOL], I32, name="wb_w", align_bytes=64)
+        wb_s = keep.tile([P, POOL], U8, name="wb_s", tag="wb_s_then_h", align_bytes=64)
+        gate_col = keep.tile([P, B], F32, name="gate_col")
+        ident = keep.tile([P, P], F32, name="ident")
+
+        def load_words(tile, words):
+            nc.sync.dma_start(out=tile[:], in_=words[0].rearrange("p c d -> p (c d)").bitcast(I32))
+
+        def load_scales(tile, scales):
+            rows = scales[0].bitcast(I32).rearrange("(q r) c -> r q c", r=4)
+            for r in range(4):
+                nc.sync.dma_start(out=tile[:].bitcast(I32)[r:P:32, :], in_=rows[r])
+
+        nc.vector.memset(wa_s[:].bitcast(I32), 0)
+        nc.vector.memset(x_s[:].bitcast(I32), 0)
+        nc.vector.memset(w_s[:].bitcast(I32), 0)
+        nc.gpsimd.memset(wb_s[:].bitcast(I32), 0)
+        make_identity(nc, ident[:])
+
+        load_words(x_w, x_words)
+        nc.sync.dma_start(tok_list[:], offs)
+        nc.sync.dma_start(a_list[:], offs2)
+        load_scales(wa_s, wa_scales)
+        load_scales(x_s, x_scales)
+        load_words(wa_w, wa_words)
+        nc.sync.dma_start(out=w_w[:].bitcast(I32), in_=w_words[0].bitcast(I32))
+        load_scales(w_s, w_scales)
+        nc.sync.dma_start(b_list[:], offs3)
+        load_scales(wb_s, wb_scales)
+        load_words(wb_w, wb_words)
+        nc.sync.dma_start(
+            out=gate_col[:], in_=gate[0].rearrange("(m p) -> p m", p=P), allow_slow_non_contiguous=True
+        )
+
+        def gather(dst, window, offsets, start, stop):
+            nc.vector.tensor_copy(
+                dst[:, start:stop], window.indirect(offsets[:, start // PER_COL : stop // PER_COL])
+            )
+
+        xg_w = keep.tile([P, T], U32, name="xg_w", align_bytes=64)
+        xg_s = keep.tile([P, T], U8, name="xg_s", align_bytes=64)
+        ag_w = keep.tile([P, B * H], U32, name="ag_w", align_bytes=64)
+        ag_s = keep.tile([P, B * H], U8, name="ag_s", align_bytes=64)
+        bg_w = keep.tile([P, B * N], U32, name="bg_w", align_bytes=64)
+        bg_s = keep.tile([P, B * N], U8, name="bg_s", align_bytes=64)
+
+        for start in range(0, T, T // 2):
+            gather(xg_w, x_w[:].bitcast(U32), tok_list, start, start + T // 2)
+        for start in range(0, B * H, 3 * H):
+            gather(ag_s, wa_s[:], a_list, start, start + 3 * H)
+        for start in range(0, T, T // 2):
+            gather(xg_s, x_s[:], tok_list, start, start + T // 2)
+        for start in range(0, B * H, 2 * H):
+            gather(ag_w, wa_w[:].bitcast(U32), a_list, start, start + 2 * H)
+        for start in range(0, B * N, 3 * N):
+            gather(bg_s, wb_s[:], b_list, start, start + 3 * N)
+
+        h_in = []
+        for pair in range(B // 2):
+            turned = psum.tile([P, 2, 2, P], F32, name="turned", tag="turn")
+            for side in range(2):
+                m = 2 * pair + side
+                slots = slice(m * P, (m + 1) * P)
+                cols = slice(m * H, (m + 1) * H)
+                acc = psum.tile([P, H], F32, name="acc", tag="acc")
+                nc.tensor.matmul_mx(
+                    out=acc[:], lhsT=xg_w[:, slots].bitcast(FP8X4), lhsT_scale=xg_s[:, slots],
+                    rhs=ag_w[:, cols].bitcast(FP8X4), rhs_scale=ag_s[:, cols], start=True, stop=True,
+                )
+                h_rows = ring.tile([P, H], BF16, name="h_rows", align_bytes=64)
+                nc.scalar.activation(
+                    h_rows[:].rearrange("j (u p e) -> j u p e", u=2, e=2),
+                    acc[:].rearrange("j (p u e) -> j u p e", u=2, e=2),
+                    ACT.Gelu_apprx_tanh,
+                )
+                for u in range(2):
+                    nc.tensor.transpose(
+                        turned[:, side, u, :], h_rows[:].bitcast(F32)[:, u * P : (u + 1) * P], ident[:]
+                    )
+            grouped = ring.tile([P, 2 * P * 4], BF16, name="grouped", align_bytes=64)
+            nc.scalar.copy(
+                grouped[:].bitcast(F32).rearrange("p (s j u) -> p s j u", s=2, u=2),
+                turned[:].rearrange("p s u j -> p s j u"),
+            )
+            h_in.append(grouped)
+
+        base_rows = keep.tile([P, B, 4, P], F32, name="base_rows")
+        for b in range(B):
+            toks = slice(b * P, (b + 1) * P)
+            acc = psum.tile([P, N], F32, name="acc", tag="acc")
+            nc.tensor.matmul_mx(
+                out=acc[:], lhsT=x_w[:, toks].bitcast(FP8X4), lhsT_scale=x_s[:, toks],
+                rhs=w_w[:].bitcast(FP4X4), rhs_scale=w_s[:], start=True, stop=True,
+            )
+            nc.scalar.copy(base_rows[:, b, :, :], acc[:].rearrange("j (p t) -> j t p", t=4))
+        base_last = [
+            psum_keep.tile([P, 4 * P], F32, name="base_last_a"),
+            psum_keep.tile([P, 2 * P], F32, name="base_last_b"),
+        ]
+        for b in range(B):
+            nc.tensor.transpose(
+                base_last[b // 4][:, (b % 4) * P : (b % 4 + 1) * P], base_rows[:, b, 3, :], ident[:]
+            )
+
+        h_w = keep.tile([P, T], U32, name="h_w", tag="wb_s_then_h", align_bytes=64)
+        h_s = keep.tile([P, T], U8, name="h_s", align_bytes=64)
+        for pair in range(B // 2):
+            slots = slice(2 * pair * P, 2 * (pair + 1) * P)
+            nc.vector.quantize_mx(out=h_w[:, slots].bitcast(FP8X4), scales=h_s[:, slots], in_=h_in[pair][:])
+        for start in range(0, B * N, 2 * N):
+            gather(bg_w, wb_w[:].bitcast(U32), b_list, start, start + 2 * N)
+
+        y = keep.tile([P, 4, T], F32, name="y")
+        for m in range(B):
+            slots = slice(m * P, (m + 1) * P)
+            cols = slice(m * N, (m + 1) * N)
+            acc = psum.tile([P, N], F32, name="acc", tag="acc")
+            nc.tensor.matmul_mx(
+                out=acc[:], lhsT=h_w[:, slots].bitcast(FP8X4), lhsT_scale=h_s[:, slots],
+                rhs=bg_w[:, cols].bitcast(FP8X4), rhs_scale=bg_s[:, cols], start=True, stop=True,
+            )
+            y_rows = ring.tile([P, 4, P], F32, name="y_rows")
+            nc.scalar.activation(
+                y_rows[:], acc[:].rearrange("j (p t) -> j t p", t=4), ACT.Copy, scale=gate_col[:, m : m + 1]
+            )
+            turned = psum.tile([P, 4, P], F32, name="turned", tag="turn")
+            for t in range(4):
+                nc.tensor.transpose(turned[:, t, :], y_rows[:, t, :], ident[:])
+            nc.scalar.copy(y[:, :, slots], turned[:])
+
+        placed = [
+            keep.tile([P, T if t < 2 else 1024], F32, name="placed%d" % t) for t in range(4)
+        ]
+
+        def scatter(t, start, stop):
+            nc.vector.tensor_copy(
+                placed[t][:].indirect(tok_list[:, start // PER_COL : stop // PER_COL]), y[:, t, start:stop]
+            )
+
+        for start, stop in ((0, 2 * P), (2 * P, T)):
+            for t in range(2):
+                scatter(t, start, stop)
+        for t in range(2, 4):
+            scatter(t, 0, T)
+
+        result = [keep.tile([P, 2, T], F32, name="result%d" % u) for u in range(2)]
+        out_rows = out_0.rearrange("(p t) c -> p t c", t=4)
+        out_in = [keep.tile([P, 2 * P, 4], BF16, name="out_in%d" % c, align_bytes=64) for c in range(3)]
+
+        def pair_views(u, c):
+            toks = slice(2 * c * P, 2 * (c + 1) * P)
+            return out_in[c][:, :, 2 * u : 2 * u + 2], result[u][:, :, toks].rearrange("p e j -> p j e")
+
+        for t in range(3):
+            for half in range(2):
+                acc = psum.tile([P, 3, P], F32, name="acc", tag="acc")
+                for i in range(3):
+                    b = 3 * half + i
+                    nc.tensor.transpose(acc[:, i, :], placed[t][:, b * P : (b + 1) * P], ident[:])
+                placed_rows = ring.tile([P, 3, P], F32, name="placed_rows")
+                nc.scalar.copy(placed_rows[:], acc[:])
+                total = psum.tile([P, 3 * P], F32, name="total", tag="turn")
+                for i in range(3):
+                    b = 3 * half + i
+                    dst = total[:, i * P : (i + 1) * P]
+                    nc.tensor.matmul(dst, base_rows[:, b, t, :], ident[:], start=True, stop=False, is_transpose=True)
+                    nc.tensor.matmul(dst, placed_rows[:, i, :], ident[:], start=False, stop=True, is_transpose=True)
+                nc.scalar.copy(result[t // 2][:, t % 2, 3 * half * P : 3 * (half + 1) * P], total[:])
+            nc.sync.dma_start(out=out_rows[:, t, :], in_=result[t // 2][:, t % 2, :])
+            if t == 1:
+                for c in range(3):
+                    nc.scalar.copy(*pair_views(0, c))
+
+        for c in range(3):
+            toks = slice(2 * c * P, 2 * (c + 1) * P)
+            nc.vector.tensor_tensor(
+                result[1][:, 1, toks], base_last[c // 2][:, (c % 2) * 2 * P : (c % 2 + 1) * 2 * P],
+                placed[3][:, toks], ADD,
+            )
+        nc.sync.dma_start(out=out_rows[:, 3, :], in_=result[1][:, 1, :])
+        nc.scalar.copy(*pair_views(1, 0))
+        nc.vector.tensor_copy(*pair_views(1, 1))
+        nc.vector.tensor_copy(*pair_views(1, 2))
+
+        out_w = keep.tile([P, T], U32, name="out_w", align_bytes=64)
+        out_s = keep.tile([P, T], U8, name="out_s", align_bytes=64)
+        word_rows = out_1[0].rearrange("p c d -> p (c d)").bitcast(I32)
+        for c in (0, 1, 2):
+            toks = slice(2 * c * P, 2 * (c + 1) * P)
+            nc.vector.quantize_mx(
+                out=out_w[:, toks].bitcast(FP8X4), scales=out_s[:, toks],
+                in_=out_in[c][:].rearrange("p j d -> p (j d)"),
+            )
+            nc.sync.dma_start(out=word_rows[:, toks], in_=out_w[:, toks].bitcast(I32))
+        scale_rows = out_2[0].bitcast(I32)
+        for q in range(4):
+            eng = nc.scalar if q % 2 else nc.sync
+            eng.dma_start(out=scale_rows[4 * q : 4 * q + 4, :], in_=out_s[:].bitcast(I32)[32 * q : 32 * q + 4, :])

@@ -20,6 +20,7 @@ ADD = mybir.AluOpType.add
 P = 128
 POOL = E * H
 PER_COL = 16
+BLOCK_RUNS = ((0, 1), (1, 3), (3, 6))
 
 
 def tile_moe_dyl_gelu_kernel(
@@ -57,21 +58,21 @@ def tile_moe_dyl_gelu_kernel(
             for r in range(4):
                 nc.sync.dma_start(out=tile[:].bitcast(I32)[r:P:32, :], in_=rows[r])
 
-        nc.vector.memset(wa_s[:].bitcast(I32), 0)
         nc.vector.memset(x_s[:].bitcast(I32), 0)
+        nc.vector.memset(wa_s[:].bitcast(I32), 0)
         nc.vector.memset(w_s[:].bitcast(I32), 0)
         nc.gpsimd.memset(wb_s[:].bitcast(I32), 0)
         make_identity(nc, ident[:])
 
-        load_words(x_w, x_words)
         nc.sync.dma_start(tok_list[:], offs)
         nc.sync.dma_start(a_list[:], offs2)
-        load_scales(wa_s, wa_scales)
+        nc.sync.dma_start(b_list[:], offs3)
         load_scales(x_s, x_scales)
+        load_words(x_w, x_words)
+        load_scales(wa_s, wa_scales)
         load_words(wa_w, wa_words)
         nc.sync.dma_start(out=w_w[:].bitcast(I32), in_=w_words[0].bitcast(I32))
         load_scales(w_s, w_scales)
-        nc.sync.dma_start(b_list[:], offs3)
         load_scales(wb_s, wb_scales)
         load_words(wb_w, wb_words)
         nc.sync.dma_start(
@@ -91,13 +92,13 @@ def tile_moe_dyl_gelu_kernel(
         bg_s = keep.tile([P, B * N], U8, name="bg_s", align_bytes=64)
 
         for start in range(0, T, T // 2):
+            gather(xg_s, x_s[:], tok_list, start, start + T // 2)
+        for start in range(0, T, T // 2):
             gather(xg_w, x_w[:].bitcast(U32), tok_list, start, start + T // 2)
         for start in range(0, B * H, 3 * H):
             gather(ag_s, wa_s[:], a_list, start, start + 3 * H)
-        for start in range(0, T, T // 2):
-            gather(xg_s, x_s[:], tok_list, start, start + T // 2)
-        for start in range(0, B * H, 2 * H):
-            gather(ag_w, wa_w[:].bitcast(U32), a_list, start, start + 2 * H)
+        for first, last in BLOCK_RUNS:
+            gather(ag_w, wa_w[:].bitcast(U32), a_list, first * H, last * H)
         for start in range(0, B * N, 3 * N):
             gather(bg_s, wb_s[:], b_list, start, start + 3 * N)
 
@@ -153,8 +154,8 @@ def tile_moe_dyl_gelu_kernel(
         for pair in range(B // 2):
             slots = slice(2 * pair * P, 2 * (pair + 1) * P)
             nc.vector.quantize_mx(out=h_w[:, slots].bitcast(FP8X4), scales=h_s[:, slots], in_=h_in[pair][:])
-        for start in range(0, B * N, 2 * N):
-            gather(bg_w, wb_w[:].bitcast(U32), b_list, start, start + 2 * N)
+        for first, last in BLOCK_RUNS:
+            gather(bg_w, wb_w[:].bitcast(U32), b_list, first * N, last * N)
 
         y = keep.tile([P, 4, T], F32, name="y")
         for m in range(B):
@@ -183,9 +184,9 @@ def tile_moe_dyl_gelu_kernel(
                 placed[t][:].indirect(tok_list[:, start // PER_COL : stop // PER_COL]), y[:, t, start:stop]
             )
 
-        for start, stop in ((0, 2 * P), (2 * P, T)):
+        for first, last in BLOCK_RUNS:
             for t in range(2):
-                scatter(t, start, stop)
+                scatter(t, first * P, last * P)
         for t in range(2, 4):
             scatter(t, 0, T)
 
@@ -198,19 +199,28 @@ def tile_moe_dyl_gelu_kernel(
             return out_in[c][:, :, 2 * u : 2 * u + 2], result[u][:, :, toks].rearrange("p e j -> p j e")
 
         for t in range(3):
+            totals = []
             for half in range(2):
+                total = psum.tile([P, 3 * P], F32, name="total", tag="turn")
+                for i in range(3):
+                    nc.tensor.matmul(
+                        total[:, i * P : (i + 1) * P], base_rows[:, 3 * half + i, t, :], ident[:],
+                        start=(i == 0), stop=False, is_transpose=True,
+                    )
+                totals.append(total)
+            for half in range(2):
+                total = totals[half]
                 acc = psum.tile([P, 3, P], F32, name="acc", tag="acc")
                 for i in range(3):
                     b = 3 * half + i
                     nc.tensor.transpose(acc[:, i, :], placed[t][:, b * P : (b + 1) * P], ident[:])
                 placed_rows = ring.tile([P, 3, P], F32, name="placed_rows")
                 nc.scalar.copy(placed_rows[:], acc[:])
-                total = psum.tile([P, 3 * P], F32, name="total", tag="turn")
                 for i in range(3):
-                    b = 3 * half + i
-                    dst = total[:, i * P : (i + 1) * P]
-                    nc.tensor.matmul(dst, base_rows[:, b, t, :], ident[:], start=True, stop=False, is_transpose=True)
-                    nc.tensor.matmul(dst, placed_rows[:, i, :], ident[:], start=False, stop=True, is_transpose=True)
+                    nc.tensor.matmul(
+                        total[:, i * P : (i + 1) * P], placed_rows[:, i, :], ident[:],
+                        start=False, stop=(i == 2), is_transpose=True,
+                    )
                 nc.scalar.copy(result[t // 2][:, t % 2, 3 * half * P : 3 * (half + 1) * P], total[:])
             nc.sync.dma_start(out=out_rows[:, t, :], in_=result[t // 2][:, t % 2, :])
             if t == 1:
@@ -225,13 +235,13 @@ def tile_moe_dyl_gelu_kernel(
             )
         nc.sync.dma_start(out=out_rows[:, 3, :], in_=result[1][:, 1, :])
         nc.scalar.copy(*pair_views(1, 0))
-        nc.vector.tensor_copy(*pair_views(1, 1))
+        nc.scalar.copy(*pair_views(1, 1))
         nc.vector.tensor_copy(*pair_views(1, 2))
 
         out_w = keep.tile([P, T], U32, name="out_w", align_bytes=64)
         out_s = keep.tile([P, T], U8, name="out_s", align_bytes=64)
         word_rows = out_1[0].rearrange("p c d -> p (c d)").bitcast(I32)
-        for c in (0, 1, 2):
+        for c in (0, 2, 1):
             toks = slice(2 * c * P, 2 * (c + 1) * P)
             nc.vector.quantize_mx(
                 out=out_w[:, toks].bitcast(FP8X4), scales=out_s[:, toks],

@@ -20,7 +20,11 @@ ADD = mybir.AluOpType.add
 P = 128
 POOL = E * H
 PER_COL = 16
-BLOCK_RUNS = ((0, 1), (1, 3), (3, 6))
+WIDE = 1024
+HALVES = ((0, 3), (3, 6))
+B_RUNS = ((0, 2), (2, 3), (3, 6))
+SUM_BANK = (0, 1, 2, 2, 3, 4)
+TURN_AFTER = {1: (3, 0, 2), 2: (4, 2, 3), 4: (0, 3, 5), 5: (1, 5, 6)}
 
 
 def tile_moe_dyl_gelu_kernel(
@@ -32,15 +36,17 @@ def tile_moe_dyl_gelu_kernel(
         lists = ctx.enter_context(tc.tile_pool(name="lists", bufs=1))
         keep = ctx.enter_context(tc.tile_pool(name="keep", bufs=1))
         ring = ctx.enter_context(tc.tile_pool(name="ring", bufs=3))
-        psum = ctx.enter_context(tc.psum_pool(name="psum", bufs=3))
-        psum_keep = ctx.enter_context(tc.psum_pool(name="psum_keep", bufs=1))
+        psum = ctx.enter_context(tc.psum_pool(name="psum", bufs=1))
+
+        def bank(number, shape):
+            return psum.tile(shape, F32, name="bank%d" % number)
 
         tok_list = lists.tile([P, T // PER_COL], U16, name="tok_list")
         a_list = lists.tile([P, B * H // PER_COL], U16, name="a_list")
         b_list = lists.tile([P, B * N // PER_COL], U16, name="b_list")
 
-        x_w = keep.tile([P, T], I32, name="x_w", align_bytes=64)
-        x_s = keep.tile([P, T], U8, name="x_s", align_bytes=64)
+        x_w = keep.tile([P, WIDE], I32, name="x_w", align_bytes=64)
+        x_s = keep.tile([P, WIDE], U8, name="x_s", align_bytes=64)
         w_w = keep.tile([P, 2 * N], U8, name="w_w", align_bytes=64)
         w_s = keep.tile([P, N], U8, name="w_s", align_bytes=64)
         wa_w = keep.tile([P, POOL], I32, name="wa_w", align_bytes=64)
@@ -51,33 +57,37 @@ def tile_moe_dyl_gelu_kernel(
         ident = keep.tile([P, P], F32, name="ident")
 
         def load_words(tile, words):
-            nc.sync.dma_start(out=tile[:], in_=words[0].rearrange("p c d -> p (c d)").bitcast(I32))
+            nc.sync.dma_start(out=tile, in_=words[0].rearrange("p c d -> p (c d)").bitcast(I32))
 
-        def load_scales(tile, scales):
+        def load_scales(tile, scales, queues=(nc.sync,) * 4):
             rows = scales[0].bitcast(I32).rearrange("(q r) c -> r q c", r=4)
             for r in range(4):
-                nc.sync.dma_start(out=tile[:].bitcast(I32)[r:P:32, :], in_=rows[r])
+                queues[r].dma_start(out=tile.bitcast(I32)[r:P:32, :], in_=rows[r])
 
-        nc.vector.memset(x_s[:].bitcast(I32), 0)
-        nc.vector.memset(wa_s[:].bitcast(I32), 0)
+        nc.gpsimd.memset(x_s[:].bitcast(I32), 0)
+        nc.vector.memset(wa_s[:, : POOL // 2].bitcast(I32), 0)
+        nc.gpsimd.memset(wa_s[:, POOL // 2 :].bitcast(I32), 0)
         nc.vector.memset(w_s[:].bitcast(I32), 0)
-        nc.gpsimd.memset(wb_s[:].bitcast(I32), 0)
+        nc.vector.memset(wb_s[:].bitcast(I32), 0)
         make_identity(nc, ident[:])
 
         nc.sync.dma_start(tok_list[:], offs)
+        load_scales(x_s[:, :T], x_scales, (nc.sync, nc.scalar, nc.sync, nc.scalar))
+        load_words(x_w[:, :T], x_words)
         nc.sync.dma_start(a_list[:], offs2)
-        nc.sync.dma_start(b_list[:], offs3)
-        load_scales(x_s, x_scales)
-        load_words(x_w, x_words)
-        load_scales(wa_s, wa_scales)
-        load_words(wa_w, wa_words)
+        load_scales(wa_s[:], wa_scales)
+        load_words(wa_w[:], wa_words)
         nc.sync.dma_start(out=w_w[:].bitcast(I32), in_=w_words[0].bitcast(I32))
-        load_scales(w_s, w_scales)
-        load_scales(wb_s, wb_scales)
-        load_words(wb_w, wb_words)
+        load_scales(w_s[:], w_scales)
+        nc.sync.dma_start(b_list[:], offs3)
+        load_scales(wb_s[:], wb_scales)
+        load_words(wb_w[:], wb_words)
         nc.sync.dma_start(
             out=gate_col[:], in_=gate[0].rearrange("(m p) -> p m", p=P), allow_slow_non_contiguous=True
         )
+
+        warm = keep.tile([P, 1], F32, name="warm")
+        nc.scalar.activation(warm[:], ident[:, 0:1], ACT.Gelu_apprx_tanh)
 
         def gather(dst, window, offsets, start, stop):
             nc.vector.tensor_copy(
@@ -91,100 +101,125 @@ def tile_moe_dyl_gelu_kernel(
         bg_w = keep.tile([P, B * N], U32, name="bg_w", align_bytes=64)
         bg_s = keep.tile([P, B * N], U8, name="bg_s", align_bytes=64)
 
-        for start in range(0, T, T // 2):
-            gather(xg_s, x_s[:], tok_list, start, start + T // 2)
-        for start in range(0, T, T // 2):
-            gather(xg_w, x_w[:].bitcast(U32), tok_list, start, start + T // 2)
+        gather(xg_s, x_s[:], tok_list, 0, T)
+        gather(xg_w, x_w[:].bitcast(U32), tok_list, 0, T)
         for start in range(0, B * H, 3 * H):
             gather(ag_s, wa_s[:], a_list, start, start + 3 * H)
-        for first, last in BLOCK_RUNS:
+        for first, last in HALVES:
             gather(ag_w, wa_w[:].bitcast(U32), a_list, first * H, last * H)
         for start in range(0, B * N, 3 * N):
             gather(bg_s, wb_s[:], b_list, start, start + 3 * N)
 
-        h_in = []
-        for pair in range(B // 2):
-            turned = psum.tile([P, 2, 2, P], F32, name="turned", tag="turn")
-            for side in range(2):
-                m = 2 * pair + side
-                slots = slice(m * P, (m + 1) * P)
-                cols = slice(m * H, (m + 1) * H)
-                acc = psum.tile([P, H], F32, name="acc", tag="acc")
-                nc.tensor.matmul_mx(
-                    out=acc[:], lhsT=xg_w[:, slots].bitcast(FP8X4), lhsT_scale=xg_s[:, slots],
-                    rhs=ag_w[:, cols].bitcast(FP8X4), rhs_scale=ag_s[:, cols], start=True, stop=True,
-                )
-                h_rows = ring.tile([P, H], BF16, name="h_rows", align_bytes=64)
-                nc.scalar.activation(
-                    h_rows[:].rearrange("j (u p e) -> j u p e", u=2, e=2),
-                    acc[:].rearrange("j (p u e) -> j u p e", u=2, e=2),
-                    ACT.Gelu_apprx_tanh,
-                )
-                for u in range(2):
-                    nc.tensor.transpose(
-                        turned[:, side, u, :], h_rows[:].bitcast(F32)[:, u * P : (u + 1) * P], ident[:]
-                    )
-            grouped = ring.tile([P, 2 * P * 4], BF16, name="grouped", align_bytes=64)
-            nc.scalar.copy(
-                grouped[:].bitcast(F32).rearrange("p (s j u) -> p s j u", s=2, u=2),
-                turned[:].rearrange("p s u j -> p s j u"),
-            )
-            h_in.append(grouped)
-
         base_rows = keep.tile([P, B, 4, P], F32, name="base_rows")
         for b in range(B):
             toks = slice(b * P, (b + 1) * P)
-            acc = psum.tile([P, N], F32, name="acc", tag="acc")
+            acc = bank(b % 3, [P, N])
             nc.tensor.matmul_mx(
                 out=acc[:], lhsT=x_w[:, toks].bitcast(FP8X4), lhsT_scale=x_s[:, toks],
                 rhs=w_w[:].bitcast(FP4X4), rhs_scale=w_s[:], start=True, stop=True,
             )
             nc.scalar.copy(base_rows[:, b, :, :], acc[:].rearrange("j (p t) -> j t p", t=4))
-        base_last = [
-            psum_keep.tile([P, 4 * P], F32, name="base_last_a"),
-            psum_keep.tile([P, 2 * P], F32, name="base_last_b"),
-        ]
+        base_last = [bank(6, [P, 4 * P]), bank(7, [P, 2 * P])]
         for b in range(B):
             nc.tensor.transpose(
                 base_last[b // 4][:, (b % 4) * P : (b % 4 + 1) * P], base_rows[:, b, 3, :], ident[:]
             )
 
-        h_w = keep.tile([P, T], U32, name="h_w", tag="wb_s_then_h", align_bytes=64)
-        h_s = keep.tile([P, T], U8, name="h_s", align_bytes=64)
-        for pair in range(B // 2):
-            slots = slice(2 * pair * P, 2 * (pair + 1) * P)
-            nc.vector.quantize_mx(out=h_w[:, slots].bitcast(FP8X4), scales=h_s[:, slots], in_=h_in[pair][:])
-        for first, last in BLOCK_RUNS:
-            gather(bg_w, wb_w[:].bitcast(U32), b_list, first * N, last * N)
+        h_rows = keep.tile([P, B, H], BF16, name="h_rows", align_bytes=64)
+        h_in = keep.tile([P, 4 * T], BF16, name="h_in", align_bytes=64)
 
-        y = keep.tile([P, 4, T], F32, name="y")
+        def turn_h(number, first, last):
+            turned = bank(number, [P, last - first, 2, P])
+            for m in range(first, last):
+                for u in range(2):
+                    nc.tensor.transpose(
+                        turned[:, m - first, u, :], h_rows[:, m, :].bitcast(F32)[:, u * P : (u + 1) * P], ident[:]
+                    )
+            nc.scalar.copy(
+                h_in[:, 4 * first * P : 4 * last * P].bitcast(F32).rearrange("p (s j u) -> p s j u", j=P, u=2),
+                turned[:].rearrange("p s u j -> p s j u"),
+            )
+
         for m in range(B):
             slots = slice(m * P, (m + 1) * P)
-            cols = slice(m * N, (m + 1) * N)
-            acc = psum.tile([P, N], F32, name="acc", tag="acc")
+            cols = slice(m * H, (m + 1) * H)
+            acc = bank(SUM_BANK[m], [P, H])
             nc.tensor.matmul_mx(
-                out=acc[:], lhsT=h_w[:, slots].bitcast(FP8X4), lhsT_scale=h_s[:, slots],
-                rhs=bg_w[:, cols].bitcast(FP8X4), rhs_scale=bg_s[:, cols], start=True, stop=True,
+                out=acc[:], lhsT=xg_w[:, slots].bitcast(FP8X4), lhsT_scale=xg_s[:, slots],
+                rhs=ag_w[:, cols].bitcast(FP8X4), rhs_scale=ag_s[:, cols], start=True, stop=True,
             )
-            y_rows = ring.tile([P, 4, P], F32, name="y_rows")
             nc.scalar.activation(
-                y_rows[:], acc[:].rearrange("j (p t) -> j t p", t=4), ACT.Copy, scale=gate_col[:, m : m + 1]
+                h_rows[:, m, :].rearrange("j (u p e) -> j u p e", u=2, e=2),
+                acc[:].rearrange("j (p u e) -> j u p e", u=2, e=2),
+                ACT.Gelu_apprx_tanh,
             )
-            turned = psum.tile([P, 4, P], F32, name="turned", tag="turn")
-            for t in range(4):
-                nc.tensor.transpose(turned[:, t, :], y_rows[:, t, :], ident[:])
-            nc.scalar.copy(y[:, :, slots], turned[:])
+            if m in TURN_AFTER:
+                turn_h(*TURN_AFTER[m])
+
+        h_w = keep.tile([P, T], U32, name="h_w", tag="wb_s_then_h", align_bytes=64)
+        h_s = keep.tile([P, T], U8, name="h_s", align_bytes=64)
+        for first, last in ((0, 4), (4, 6)):
+            slots = slice(first * P, last * P)
+            nc.vector.quantize_mx(
+                out=h_w[:, slots].bitcast(FP8X4), scales=h_s[:, slots], in_=h_in[:, 4 * first * P : 4 * last * P]
+            )
+        for first, last in B_RUNS:
+            gather(bg_w, wb_w[:].bitcast(U32), b_list, first * N, last * N)
+
+        y = [keep.tile([P, 2, T], F32, name="y%d" % u) for u in range(2)]
+
+        def gate_rows(u, half, sums):
+            rows = keep.tile([P, 3, 2, P], F32, name="y_rows%d" % half)
+            for i in range(3):
+                m = 3 * half + i
+                nc.scalar.activation(
+                    rows[:, i, :, :], sums[i][:].rearrange("j (p t) -> j t p", t=4)[:, 2 * u : 2 * u + 2, :],
+                    ACT.Copy, scale=gate_col[:, m : m + 1],
+                )
+            return rows
+
+        def turn_y(u, half, rows, banks):
+            for number, first, last in ((banks[0], 0, 2), (banks[1], 2, 3)):
+                turned = bank(number, [P, last - first, 2, P])
+                for i in range(first, last):
+                    for e in range(2):
+                        nc.tensor.transpose(turned[:, i - first, e, :], rows[:, i, e, :], ident[:])
+                cols = slice((3 * half + first) * P, (3 * half + last) * P)
+                nc.scalar.copy(y[u][:, :, cols].rearrange("p e (m j) -> p m e j", j=P), turned[:])
+
+        def second_layer(half, banks):
+            sums = []
+            for i in range(3):
+                m = 3 * half + i
+                slots = slice(m * P, (m + 1) * P)
+                cols = slice(m * N, (m + 1) * N)
+                acc = bank(banks[i], [P, N])
+                nc.tensor.matmul_mx(
+                    out=acc[:], lhsT=h_w[:, slots].bitcast(FP8X4), lhsT_scale=h_s[:, slots],
+                    rhs=bg_w[:, cols].bitcast(FP8X4), rhs_scale=bg_s[:, cols], start=True, stop=True,
+                )
+                sums.append(acc)
+            return sums
+
+        sums_a = second_layer(0, (0, 1, 2))
+        turn_y(0, 0, gate_rows(0, 0, sums_a), (3, 4))
+        high_a = gate_rows(1, 0, sums_a)
+        sums_b = second_layer(1, (4, 0, 1))
+        turn_y(0, 1, gate_rows(0, 1, sums_b), (3, 5))
+        turn_y(1, 0, high_a, (2, 5))
+        turn_y(1, 1, gate_rows(1, 1, sums_b), (3, 2))
 
         placed = [
-            keep.tile([P, T if t < 2 else 1024], F32, name="placed%d" % t) for t in range(4)
+            keep.tile([P, T if t < 2 else WIDE], F32, name="placed%d" % t) for t in range(4)
         ]
 
         def scatter(t, start, stop):
             nc.vector.tensor_copy(
-                placed[t][:].indirect(tok_list[:, start // PER_COL : stop // PER_COL]), y[:, t, start:stop]
+                placed[t][:].indirect(tok_list[:, start // PER_COL : stop // PER_COL]),
+                y[t // 2][:, t % 2, start:stop],
             )
 
-        for first, last in BLOCK_RUNS:
+        for first, last in HALVES:
             for t in range(2):
                 scatter(t, first * P, last * P)
         for t in range(2, 4):
@@ -201,7 +236,7 @@ def tile_moe_dyl_gelu_kernel(
         for t in range(3):
             totals = []
             for half in range(2):
-                total = psum.tile([P, 3 * P], F32, name="total", tag="turn")
+                total = bank((0, 4, 0)[t] + half, [P, 3 * P])
                 for i in range(3):
                     nc.tensor.matmul(
                         total[:, i * P : (i + 1) * P], base_rows[:, 3 * half + i, t, :], ident[:],
@@ -210,7 +245,7 @@ def tile_moe_dyl_gelu_kernel(
                 totals.append(total)
             for half in range(2):
                 total = totals[half]
-                acc = psum.tile([P, 3, P], F32, name="acc", tag="acc")
+                acc = bank(3 - half, [P, 3, P])
                 for i in range(3):
                     b = 3 * half + i
                     nc.tensor.transpose(acc[:, i, :], placed[t][:, b * P : (b + 1) * P], ident[:])
@@ -222,18 +257,18 @@ def tile_moe_dyl_gelu_kernel(
                         start=False, stop=(i == 2), is_transpose=True,
                     )
                 nc.scalar.copy(result[t // 2][:, t % 2, 3 * half * P : 3 * (half + 1) * P], total[:])
-            nc.sync.dma_start(out=out_rows[:, t, :], in_=result[t // 2][:, t % 2, :])
+            nc.scalar.dma_start(out=out_rows[:, t, :], in_=result[t // 2][:, t % 2, :])
             if t == 1:
                 for c in range(3):
                     nc.scalar.copy(*pair_views(0, c))
 
-        for c in range(3):
+        for c in (0, 2, 1):
             toks = slice(2 * c * P, 2 * (c + 1) * P)
             nc.vector.tensor_tensor(
                 result[1][:, 1, toks], base_last[c // 2][:, (c % 2) * 2 * P : (c % 2 + 1) * 2 * P],
                 placed[3][:, toks], ADD,
             )
-        nc.sync.dma_start(out=out_rows[:, 3, :], in_=result[1][:, 1, :])
+            nc.sync.dma_start(out=out_rows[:, 3, toks], in_=result[1][:, 1, toks])
         nc.scalar.copy(*pair_views(1, 0))
         nc.scalar.copy(*pair_views(1, 1))
         nc.vector.tensor_copy(*pair_views(1, 2))

@@ -22,7 +22,7 @@ POOL = E * H
 PER_COL = 16
 WIDE = 1024
 HALVES = ((0, 3), (3, 6))
-B_RUNS = ((0, 2), (2, 3), (3, 6))
+B_RUNS = ((0, 1), (1, 3), (3, 6))
 SUM_BANK = (0, 1, 2, 2, 3, 4)
 TURN_AFTER = {1: (3, 0, 2), 2: (4, 2, 3), 4: (0, 3, 5), 5: (1, 5, 6)}
 
@@ -52,7 +52,7 @@ def tile_moe_dyl_gelu_kernel(
         wa_w = keep.tile([P, POOL], I32, name="wa_w", align_bytes=64)
         wa_s = keep.tile([P, POOL], U8, name="wa_s", align_bytes=64)
         wb_w = keep.tile([P, POOL], I32, name="wb_w", align_bytes=64)
-        wb_s = keep.tile([P, POOL], U8, name="wb_s", tag="wb_s_then_h", align_bytes=64)
+        wb_s = keep.tile([P, POOL], U8, name="wb_s", align_bytes=64)
         gate_col = keep.tile([P, B], F32, name="gate_col")
         ident = keep.tile([P, P], F32, name="ident")
 
@@ -77,17 +77,14 @@ def tile_moe_dyl_gelu_kernel(
         nc.sync.dma_start(a_list[:], offs2)
         load_scales(wa_s[:], wa_scales)
         load_words(wa_w[:], wa_words)
-        nc.sync.dma_start(out=w_w[:].bitcast(I32), in_=w_words[0].bitcast(I32))
-        load_scales(w_s[:], w_scales)
+        nc.scalar.dma_start(out=w_w[:].bitcast(I32), in_=w_words[0].bitcast(I32))
+        load_scales(w_s[:], w_scales, (nc.scalar,) * 4)
         nc.sync.dma_start(b_list[:], offs3)
         load_scales(wb_s[:], wb_scales)
         load_words(wb_w[:], wb_words)
         nc.sync.dma_start(
             out=gate_col[:], in_=gate[0].rearrange("(m p) -> p m", p=P), allow_slow_non_contiguous=True
         )
-
-        warm = keep.tile([P, 1], F32, name="warm")
-        nc.scalar.activation(warm[:], ident[:, 0:1], ACT.Gelu_apprx_tanh)
 
         def gather(dst, window, offsets, start, stop):
             nc.vector.tensor_copy(
@@ -156,7 +153,7 @@ def tile_moe_dyl_gelu_kernel(
             if m in TURN_AFTER:
                 turn_h(*TURN_AFTER[m])
 
-        h_w = keep.tile([P, T], U32, name="h_w", tag="wb_s_then_h", align_bytes=64)
+        h_w = keep.tile([P, T], U32, name="h_w", align_bytes=64)
         h_s = keep.tile([P, T], U8, name="h_s", align_bytes=64)
         for first, last in ((0, 4), (4, 6)):
             slots = slice(first * P, last * P)
@@ -179,7 +176,7 @@ def tile_moe_dyl_gelu_kernel(
             return rows
 
         def turn_y(u, half, rows, banks):
-            for number, first, last in ((banks[0], 0, 2), (banks[1], 2, 3)):
+            for number, first, last in ((banks[0], 0, 1), (banks[1], 1, 3)):
                 turned = bank(number, [P, last - first, 2, P])
                 for i in range(first, last):
                     for e in range(2):
@@ -219,7 +216,7 @@ def tile_moe_dyl_gelu_kernel(
                 y[t // 2][:, t % 2, start:stop],
             )
 
-        for first, last in HALVES:
+        for first, last in B_RUNS:
             for t in range(2):
                 scatter(t, first * P, last * P)
         for t in range(2, 4):

@@ -21,6 +21,7 @@ P = 128
 POOL = E * H
 PER_COL = 16
 WIDE = 1024
+ZERO_SPLIT = 3072
 HALVES = ((0, 3), (3, 6))
 B_RUNS = ((0, 1), (1, 3), (3, 6))
 SUM_BANK = (0, 1, 2, 2, 3, 4)
@@ -56,32 +57,34 @@ def tile_moe_dyl_gelu_kernel(
         gate_col = keep.tile([P, B], F32, name="gate_col")
         ident = keep.tile([P, P], F32, name="ident")
 
-        def load_words(tile, words):
-            nc.sync.dma_start(out=tile, in_=words[0].rearrange("p c d -> p (c d)").bitcast(I32))
+        def load_words(tile, words, start, stop):
+            rows = words[0].rearrange("p c d -> p (c d)").bitcast(I32)
+            nc.sync.dma_start(out=tile[:, start:stop], in_=rows[:, start:stop])
 
         def load_scales(tile, scales, queues=(nc.sync,) * 4):
             rows = scales[0].bitcast(I32).rearrange("(q r) c -> r q c", r=4)
             for r in range(4):
                 queues[r].dma_start(out=tile.bitcast(I32)[r:P:32, :], in_=rows[r])
 
+        nc.gpsimd.memset(wa_s[:, :ZERO_SPLIT].bitcast(I32), 0)
+        nc.vector.memset(wa_s[:, ZERO_SPLIT:].bitcast(I32), 0)
         nc.gpsimd.memset(x_s[:].bitcast(I32), 0)
-        nc.vector.memset(wa_s[:, : POOL // 2].bitcast(I32), 0)
-        nc.gpsimd.memset(wa_s[:, POOL // 2 :].bitcast(I32), 0)
-        nc.vector.memset(w_s[:].bitcast(I32), 0)
         nc.vector.memset(wb_s[:].bitcast(I32), 0)
+        nc.vector.memset(w_s[:].bitcast(I32), 0)
         make_identity(nc, ident[:])
 
         nc.sync.dma_start(tok_list[:], offs)
-        load_scales(x_s[:, :T], x_scales, (nc.sync, nc.scalar, nc.sync, nc.scalar))
-        load_words(x_w[:, :T], x_words)
+        load_words(x_w, x_words, 0, T)
         nc.sync.dma_start(a_list[:], offs2)
         load_scales(wa_s[:], wa_scales)
-        load_words(wa_w[:], wa_words)
-        nc.scalar.dma_start(out=w_w[:].bitcast(I32), in_=w_words[0].bitcast(I32))
-        load_scales(w_s[:], w_scales, (nc.scalar,) * 4)
+        load_words(wa_w, wa_words, 0, POOL // 2)
+        load_scales(x_s[:, :T], x_scales)
+        load_words(wa_w, wa_words, POOL // 2, POOL)
         nc.sync.dma_start(b_list[:], offs3)
         load_scales(wb_s[:], wb_scales)
-        load_words(wb_w[:], wb_words)
+        nc.sync.dma_start(out=w_w[:].bitcast(I32), in_=w_words[0].bitcast(I32))
+        load_scales(w_s[:], w_scales)
+        load_words(wb_w, wb_words, 0, POOL)
         nc.sync.dma_start(
             out=gate_col[:], in_=gate[0].rearrange("(m p) -> p m", p=P), allow_slow_non_contiguous=True
         )
@@ -98,29 +101,27 @@ def tile_moe_dyl_gelu_kernel(
         bg_w = keep.tile([P, B * N], U32, name="bg_w", align_bytes=64)
         bg_s = keep.tile([P, B * N], U8, name="bg_s", align_bytes=64)
 
-        gather(xg_s, x_s[:], tok_list, 0, T)
         gather(xg_w, x_w[:].bitcast(U32), tok_list, 0, T)
         for start in range(0, B * H, 3 * H):
             gather(ag_s, wa_s[:], a_list, start, start + 3 * H)
+        gather(xg_s, x_s[:], tok_list, 0, T)
         for first, last in HALVES:
             gather(ag_w, wa_w[:].bitcast(U32), a_list, first * H, last * H)
         for start in range(0, B * N, 3 * N):
             gather(bg_s, wb_s[:], b_list, start, start + 3 * N)
 
         base_rows = keep.tile([P, B, 4, P], F32, name="base_rows")
-        for b in range(B):
-            toks = slice(b * P, (b + 1) * P)
-            acc = bank(b % 3, [P, N])
-            nc.tensor.matmul_mx(
-                out=acc[:], lhsT=x_w[:, toks].bitcast(FP8X4), lhsT_scale=x_s[:, toks],
-                rhs=w_w[:].bitcast(FP4X4), rhs_scale=w_s[:], start=True, stop=True,
-            )
-            nc.scalar.copy(base_rows[:, b, :, :], acc[:].rearrange("j (p t) -> j t p", t=4))
-        base_last = [bank(6, [P, 4 * P]), bank(7, [P, 2 * P])]
-        for b in range(B):
-            nc.tensor.transpose(
-                base_last[b // 4][:, (b % 4) * P : (b % 4 + 1) * P], base_rows[:, b, 3, :], ident[:]
-            )
+
+        def frozen_layer(half, banks):
+            for i in range(3):
+                b = 3 * half + i
+                toks = slice(b * P, (b + 1) * P)
+                acc = bank(banks[i], [P, N])
+                nc.tensor.matmul_mx(
+                    out=acc[:], lhsT=x_w[:, toks].bitcast(FP8X4), lhsT_scale=x_s[:, toks],
+                    rhs=w_w[:].bitcast(FP4X4), rhs_scale=w_s[:], start=True, stop=True,
+                )
+                nc.scalar.copy(base_rows[:, b, :, :], acc[:].rearrange("j (p t) -> j t p", t=4))
 
         h_rows = keep.tile([P, B, H], BF16, name="h_rows", align_bytes=64)
         h_in = keep.tile([P, 4 * T], BF16, name="h_in", align_bytes=64)
@@ -152,6 +153,8 @@ def tile_moe_dyl_gelu_kernel(
             )
             if m in TURN_AFTER:
                 turn_h(*TURN_AFTER[m])
+
+        frozen_layer(0, (0, 1, 0))
 
         h_w = keep.tile([P, T], U32, name="h_w", align_bytes=64)
         h_s = keep.tile([P, T], U8, name="h_s", align_bytes=64)
@@ -205,6 +208,13 @@ def tile_moe_dyl_gelu_kernel(
         turn_y(0, 1, gate_rows(0, 1, sums_b), (3, 5))
         turn_y(1, 0, high_a, (2, 5))
         turn_y(1, 1, gate_rows(1, 1, sums_b), (3, 2))
+
+        frozen_layer(1, (3, 2, 3))
+        base_last = [bank(6, [P, 4 * P]), bank(7, [P, 2 * P])]
+        for b in range(B):
+            nc.tensor.transpose(
+                base_last[b // 4][:, (b % 4) * P : (b % 4 + 1) * P], base_rows[:, b, 3, :], ident[:]
+            )
 
         placed = [
             keep.tile([P, T if t < 2 else WIDE], F32, name="placed%d" % t) for t in range(4)

@@ -24,8 +24,7 @@ WIDE = 1024
 ZERO_SPLIT = 3072
 HALVES = ((0, 3), (3, 6))
 B_RUNS = ((0, 1), (1, 3), (3, 6))
-SUM_BANK = (0, 1, 2, 2, 3, 4)
-TURN_AFTER = {1: (3, 0, 2), 2: (4, 2, 3), 4: (0, 3, 5), 5: (1, 5, 6)}
+SUM_BANK = (0, 1, 2, 2, 3, 2)
 
 
 def tile_moe_dyl_gelu_kernel(
@@ -54,6 +53,7 @@ def tile_moe_dyl_gelu_kernel(
         wa_s = keep.tile([P, POOL], U8, name="wa_s", align_bytes=64)
         wb_w = keep.tile([P, POOL], I32, name="wb_w", align_bytes=64)
         wb_s = keep.tile([P, POOL], U8, name="wb_s", align_bytes=64)
+        gate_by_block = keep.tile([P, P], F32, name="gate_by_block")
         gate_col = keep.tile([P, B], F32, name="gate_col")
         ident = keep.tile([P, P], F32, name="ident")
 
@@ -61,20 +61,21 @@ def tile_moe_dyl_gelu_kernel(
             rows = words[0].rearrange("p c d -> p (c d)").bitcast(I32)
             nc.sync.dma_start(out=tile[:, start:stop], in_=rows[:, start:stop])
 
-        def load_scales(tile, scales, queues=(nc.sync,) * 4):
+        def load_scales(tile, scales):
             rows = scales[0].bitcast(I32).rearrange("(q r) c -> r q c", r=4)
             for r in range(4):
-                queues[r].dma_start(out=tile.bitcast(I32)[r:P:32, :], in_=rows[r])
+                nc.sync.dma_start(out=tile.bitcast(I32)[r:P:32, :], in_=rows[r])
 
         nc.gpsimd.memset(wa_s[:, :ZERO_SPLIT].bitcast(I32), 0)
         nc.vector.memset(wa_s[:, ZERO_SPLIT:].bitcast(I32), 0)
         nc.gpsimd.memset(x_s[:].bitcast(I32), 0)
         nc.vector.memset(wb_s[:].bitcast(I32), 0)
         nc.vector.memset(w_s[:].bitcast(I32), 0)
+        nc.vector.memset(gate_by_block[:], 0.0)
         make_identity(nc, ident[:])
 
-        nc.sync.dma_start(tok_list[:], offs)
         load_words(x_w, x_words, 0, T)
+        nc.sync.dma_start(tok_list[:], offs)
         nc.sync.dma_start(a_list[:], offs2)
         load_scales(wa_s[:], wa_scales)
         load_words(wa_w, wa_words, 0, POOL // 2)
@@ -85,9 +86,7 @@ def tile_moe_dyl_gelu_kernel(
         nc.sync.dma_start(out=w_w[:].bitcast(I32), in_=w_words[0].bitcast(I32))
         load_scales(w_s[:], w_scales)
         load_words(wb_w, wb_words, 0, POOL)
-        nc.sync.dma_start(
-            out=gate_col[:], in_=gate[0].rearrange("(m p) -> p m", p=P), allow_slow_non_contiguous=True
-        )
+        nc.sync.dma_start(out=gate_by_block[:B, :], in_=gate[0].rearrange("(m p) -> m p", p=P))
 
         def gather(dst, window, offsets, start, stop):
             nc.vector.tensor_copy(
@@ -105,7 +104,7 @@ def tile_moe_dyl_gelu_kernel(
         for start in range(0, B * H, 3 * H):
             gather(ag_s, wa_s[:], a_list, start, start + 3 * H)
         gather(xg_s, x_s[:], tok_list, 0, T)
-        for first, last in HALVES:
+        for first, last in B_RUNS:
             gather(ag_w, wa_w[:].bitcast(U32), a_list, first * H, last * H)
         for start in range(0, B * N, 3 * N):
             gather(bg_s, wb_s[:], b_list, start, start + 3 * N)
@@ -123,46 +122,44 @@ def tile_moe_dyl_gelu_kernel(
                 )
                 nc.scalar.copy(base_rows[:, b, :, :], acc[:].rearrange("j (p t) -> j t p", t=4))
 
-        h_rows = keep.tile([P, B, H], BF16, name="h_rows", align_bytes=64)
-        h_in = keep.tile([P, 4 * T], BF16, name="h_in", align_bytes=64)
-
-        def turn_h(number, first, last):
-            turned = bank(number, [P, last - first, 2, P])
-            for m in range(first, last):
+        h_in = [keep.tile([P, 4 * count * P], BF16, name="h_in%d" % count, align_bytes=64) for count in (4, 2)]
+        for pair in range(B // 2):
+            turned = bank(3 + pair, [P, 2, 2, P])
+            for side in range(2):
+                m = 2 * pair + side
+                slots = slice(m * P, (m + 1) * P)
+                cols = slice(m * H, (m + 1) * H)
+                acc = bank(SUM_BANK[m], [P, H])
+                nc.tensor.matmul_mx(
+                    out=acc[:], lhsT=xg_w[:, slots].bitcast(FP8X4), lhsT_scale=xg_s[:, slots],
+                    rhs=ag_w[:, cols].bitcast(FP8X4), rhs_scale=ag_s[:, cols], start=True, stop=True,
+                )
+                h_rows = keep.tile([P, H], BF16, name="h_rows%d" % m, align_bytes=64)
+                nc.scalar.activation(
+                    h_rows[:].rearrange("j (u p e) -> j u p e", u=2, e=2),
+                    acc[:].rearrange("j (p u e) -> j u p e", u=2, e=2),
+                    ACT.Gelu_apprx_tanh,
+                )
                 for u in range(2):
                     nc.tensor.transpose(
-                        turned[:, m - first, u, :], h_rows[:, m, :].bitcast(F32)[:, u * P : (u + 1) * P], ident[:]
+                        turned[:, side, u, :], h_rows[:].bitcast(F32)[:, u * P : (u + 1) * P], ident[:]
                     )
+            start = (pair % 2) * 8 * P
             nc.scalar.copy(
-                h_in[:, 4 * first * P : 4 * last * P].bitcast(F32).rearrange("p (s j u) -> p s j u", j=P, u=2),
+                h_in[pair // 2][:, start : start + 8 * P].bitcast(F32).rearrange("p (s j u) -> p s j u", s=2, u=2),
                 turned[:].rearrange("p s u j -> p s j u"),
             )
 
-        for m in range(B):
-            slots = slice(m * P, (m + 1) * P)
-            cols = slice(m * H, (m + 1) * H)
-            acc = bank(SUM_BANK[m], [P, H])
-            nc.tensor.matmul_mx(
-                out=acc[:], lhsT=xg_w[:, slots].bitcast(FP8X4), lhsT_scale=xg_s[:, slots],
-                rhs=ag_w[:, cols].bitcast(FP8X4), rhs_scale=ag_s[:, cols], start=True, stop=True,
-            )
-            nc.scalar.activation(
-                h_rows[:, m, :].rearrange("j (u p e) -> j u p e", u=2, e=2),
-                acc[:].rearrange("j (p u e) -> j u p e", u=2, e=2),
-                ACT.Gelu_apprx_tanh,
-            )
-            if m in TURN_AFTER:
-                turn_h(*TURN_AFTER[m])
-
-        frozen_layer(0, (0, 1, 0))
+        frozen_layer(0, (4, 5, 4))
+        gate_turned = bank(5, [P, P])
+        nc.tensor.transpose(gate_turned[:], gate_by_block[:], ident[:])
+        nc.scalar.copy(gate_col[:], gate_turned[:, :B])
 
         h_w = keep.tile([P, T], U32, name="h_w", align_bytes=64)
         h_s = keep.tile([P, T], U8, name="h_s", align_bytes=64)
-        for first, last in ((0, 4), (4, 6)):
+        for part, (first, last) in enumerate(((0, 4), (4, 6))):
             slots = slice(first * P, last * P)
-            nc.vector.quantize_mx(
-                out=h_w[:, slots].bitcast(FP8X4), scales=h_s[:, slots], in_=h_in[:, 4 * first * P : 4 * last * P]
-            )
+            nc.vector.quantize_mx(out=h_w[:, slots].bitcast(FP8X4), scales=h_s[:, slots], in_=h_in[part][:])
         for first, last in B_RUNS:
             gather(bg_w, wb_w[:].bitcast(U32), b_list, first * N, last * N)
 
@@ -178,14 +175,16 @@ def tile_moe_dyl_gelu_kernel(
                 )
             return rows
 
-        def turn_y(u, half, rows, banks):
-            for number, first, last in ((banks[0], 0, 1), (banks[1], 1, 3)):
-                turned = bank(number, [P, last - first, 2, P])
+        def turn_y(u, half, rows, pieces):
+            for number, first, last, planes in pieces:
+                turned = bank(number, [P, last - first, len(planes), P])
                 for i in range(first, last):
-                    for e in range(2):
-                        nc.tensor.transpose(turned[:, i - first, e, :], rows[:, i, e, :], ident[:])
+                    for e in planes:
+                        nc.tensor.transpose(turned[:, i - first, e - planes[0], :], rows[:, i, e, :], ident[:])
                 cols = slice((3 * half + first) * P, (3 * half + last) * P)
-                nc.scalar.copy(y[u][:, :, cols].rearrange("p e (m j) -> p m e j", j=P), turned[:])
+                nc.scalar.copy(
+                    y[u][:, planes[0] : planes[-1] + 1, cols].rearrange("p e (m j) -> p m e j", j=P), turned[:]
+                )
 
         def second_layer(half, banks):
             sums = []
@@ -201,15 +200,15 @@ def tile_moe_dyl_gelu_kernel(
                 sums.append(acc)
             return sums
 
+        both = (0, 1)
         sums_a = second_layer(0, (0, 1, 2))
-        turn_y(0, 0, gate_rows(0, 0, sums_a), (3, 4))
-        high_a = gate_rows(1, 0, sums_a)
-        sums_b = second_layer(1, (4, 0, 1))
-        turn_y(0, 1, gate_rows(0, 1, sums_b), (3, 5))
-        turn_y(1, 0, high_a, (2, 5))
-        turn_y(1, 1, gate_rows(1, 1, sums_b), (3, 2))
+        turn_y(0, 0, gate_rows(0, 0, sums_a), ((3, 0, 1, both), (3, 1, 2, both), (4, 2, 3, (0,)), (5, 2, 3, (1,))))
+        sums_b = second_layer(1, (3, 4, 5))
+        turn_y(0, 1, gate_rows(0, 1, sums_b), ((6, 0, 2, both), (7, 2, 3, both)))
+        turn_y(1, 0, gate_rows(1, 0, sums_a), ((0, 0, 1, both), (1, 1, 3, both)))
+        turn_y(1, 1, gate_rows(1, 1, sums_b), ((2, 0, 1, both), (0, 1, 3, both)))
 
-        frozen_layer(1, (3, 2, 3))
+        frozen_layer(1, (2, 0, 2))
         base_last = [bank(6, [P, 4 * P]), bank(7, [P, 2 * P])]
         for b in range(B):
             nc.tensor.transpose(
@@ -243,7 +242,7 @@ def tile_moe_dyl_gelu_kernel(
         for t in range(3):
             totals = []
             for half in range(2):
-                total = bank((0, 4, 0)[t] + half, [P, 3 * P])
+                total = bank(((3, 4), (5, 1), (3, 4))[t][half], [P, 3 * P])
                 for i in range(3):
                     nc.tensor.matmul(
                         total[:, i * P : (i + 1) * P], base_rows[:, 3 * half + i, t, :], ident[:],
@@ -252,7 +251,7 @@ def tile_moe_dyl_gelu_kernel(
                 totals.append(total)
             for half in range(2):
                 total = totals[half]
-                acc = bank(3 - half, [P, 3, P])
+                acc = bank(2 * half, [P, 3, P])
                 for i in range(3):
                     b = 3 * half + i
                     nc.tensor.transpose(acc[:, i, :], placed[t][:, b * P : (b + 1) * P], ident[:])
@@ -275,7 +274,7 @@ def tile_moe_dyl_gelu_kernel(
                 result[1][:, 1, toks], base_last[c // 2][:, (c % 2) * 2 * P : (c % 2 + 1) * 2 * P],
                 placed[3][:, toks], ADD,
             )
-            nc.sync.dma_start(out=out_rows[:, 3, toks], in_=result[1][:, 1, toks])
+        nc.sync.dma_start(out=out_rows[:, 3, :], in_=result[1][:, 1, :])
         nc.scalar.copy(*pair_views(1, 0))
         nc.scalar.copy(*pair_views(1, 1))
         nc.vector.tensor_copy(*pair_views(1, 2))

@@ -20,11 +20,10 @@ ADD = mybir.AluOpType.add
 P = 128
 POOL = E * H
 PER_COL = 16
+HALF = 3
 WIDE = 1024
 ZERO_SPLIT = 3072
-HALVES = ((0, 3), (3, 6))
-B_RUNS = ((0, 1), (1, 3), (3, 6))
-SUM_BANK = (0, 1, 2, 2, 3, 2)
+RUNS = ((0, 1), (1, 3), (3, 6))
 
 
 def tile_moe_dyl_gelu_kernel(
@@ -89,31 +88,28 @@ def tile_moe_dyl_gelu_kernel(
         nc.sync.dma_start(out=gate_by_block[:B, :], in_=gate[0].rearrange("(m p) -> m p", p=P))
 
         def gather(dst, window, offsets, start, stop):
-            nc.vector.tensor_copy(
-                dst[:, start:stop], window.indirect(offsets[:, start // PER_COL : stop // PER_COL])
-            )
+            nc.vector.tensor_copy(dst, window.indirect(offsets[:, start // PER_COL : stop // PER_COL]))
 
         xg_w = keep.tile([P, T], U32, name="xg_w", align_bytes=64)
         xg_s = keep.tile([P, T], U8, name="xg_s", align_bytes=64)
         ag_w = keep.tile([P, B * H], U32, name="ag_w", align_bytes=64)
         ag_s = keep.tile([P, B * H], U8, name="ag_s", align_bytes=64)
-        bg_w = keep.tile([P, B * N], U32, name="bg_w", align_bytes=64)
         bg_s = keep.tile([P, B * N], U8, name="bg_s", align_bytes=64)
 
-        gather(xg_w, x_w[:].bitcast(U32), tok_list, 0, T)
-        for start in range(0, B * H, 3 * H):
-            gather(ag_s, wa_s[:], a_list, start, start + 3 * H)
-        gather(xg_s, x_s[:], tok_list, 0, T)
-        for first, last in B_RUNS:
-            gather(ag_w, wa_w[:].bitcast(U32), a_list, first * H, last * H)
-        for start in range(0, B * N, 3 * N):
-            gather(bg_s, wb_s[:], b_list, start, start + 3 * N)
+        gather(xg_w[:], x_w[:].bitcast(U32), tok_list, 0, T)
+        for start in range(0, B * H, HALF * H):
+            gather(ag_s[:, start : start + HALF * H], wa_s[:], a_list, start, start + HALF * H)
+        gather(xg_s[:], x_s[:], tok_list, 0, T)
+        for first, last in RUNS:
+            gather(ag_w[:, first * H : last * H], wa_w[:].bitcast(U32), a_list, first * H, last * H)
+        for start in range(0, B * N, HALF * N):
+            gather(bg_s[:, start : start + HALF * N], wb_s[:], b_list, start, start + HALF * N)
 
         base_rows = keep.tile([P, B, 4, P], F32, name="base_rows")
 
         def frozen_layer(half, banks):
-            for i in range(3):
-                b = 3 * half + i
+            for i in range(HALF):
+                b = HALF * half + i
                 toks = slice(b * P, (b + 1) * P)
                 acc = bank(banks[i], [P, N])
                 nc.tensor.matmul_mx(
@@ -122,6 +118,7 @@ def tile_moe_dyl_gelu_kernel(
                 )
                 nc.scalar.copy(base_rows[:, b, :, :], acc[:].rearrange("j (p t) -> j t p", t=4))
 
+        first_banks = (0, 1, 2, 2, 3, 2)
         h_in = [keep.tile([P, 4 * count * P], BF16, name="h_in%d" % count, align_bytes=64) for count in (4, 2)]
         for pair in range(B // 2):
             turned = bank(3 + pair, [P, 2, 2, P])
@@ -129,7 +126,7 @@ def tile_moe_dyl_gelu_kernel(
                 m = 2 * pair + side
                 slots = slice(m * P, (m + 1) * P)
                 cols = slice(m * H, (m + 1) * H)
-                acc = bank(SUM_BANK[m], [P, H])
+                acc = bank(first_banks[m], [P, H])
                 nc.tensor.matmul_mx(
                     out=acc[:], lhsT=xg_w[:, slots].bitcast(FP8X4), lhsT_scale=xg_s[:, slots],
                     rhs=ag_w[:, cols].bitcast(FP8X4), rhs_scale=ag_s[:, cols], start=True, stop=True,
@@ -155,20 +152,41 @@ def tile_moe_dyl_gelu_kernel(
         nc.tensor.transpose(gate_turned[:], gate_by_block[:], ident[:])
         nc.scalar.copy(gate_col[:], gate_turned[:, :B])
 
-        h_w = keep.tile([P, T], U32, name="h_w", align_bytes=64)
+        h_w = {0: keep.tile([P, 4 * P], U32, name="h_w0", align_bytes=64)}
         h_s = keep.tile([P, T], U8, name="h_s", align_bytes=64)
-        for part, (first, last) in enumerate(((0, 4), (4, 6))):
-            slots = slice(first * P, last * P)
-            nc.vector.quantize_mx(out=h_w[:, slots].bitcast(FP8X4), scales=h_s[:, slots], in_=h_in[part][:])
-        for first, last in B_RUNS:
-            gather(bg_w, wb_w[:].bitcast(U32), b_list, first * N, last * N)
+        nc.vector.quantize_mx(out=h_w[0][:].bitcast(FP8X4), scales=h_s[:, : 4 * P], in_=h_in[0][:])
+        bg_w = {
+            0: keep.tile([P, N], U32, name="bg_w0", tag="bg_w0_then_h", align_bytes=64),
+            1: keep.tile([P, 2 * N], U32, name="bg_w1", align_bytes=64),
+            3: keep.tile([P, 3 * N], U32, name="bg_w3", align_bytes=64),
+        }
+        for first, last in RUNS:
+            gather(bg_w[first][:], wb_w[:].bitcast(U32), b_list, first * N, last * N)
 
         y = [keep.tile([P, 2, T], F32, name="y%d" % u) for u in range(2)]
 
+        def second_layer(half, banks):
+            sums = []
+            for i in range(HALF):
+                m = HALF * half + i
+                slots = slice(m * P, (m + 1) * P)
+                cols = slice(m * N, (m + 1) * N)
+                run = max(first for first in bg_w if first <= m)
+                part = max(first for first in h_w if first <= m)
+                acc = bank(banks[i], [P, N])
+                nc.tensor.matmul_mx(
+                    out=acc[:], lhsT=h_w[part][:, (m - part) * P : (m - part + 1) * P].bitcast(FP8X4),
+                    lhsT_scale=h_s[:, slots],
+                    rhs=bg_w[run][:, (m - run) * N : (m - run + 1) * N].bitcast(FP8X4), rhs_scale=bg_s[:, cols],
+                    start=True, stop=True,
+                )
+                sums.append(acc)
+            return sums
+
         def gate_rows(u, half, sums):
-            rows = keep.tile([P, 3, 2, P], F32, name="y_rows%d" % half)
-            for i in range(3):
-                m = 3 * half + i
+            rows = keep.tile([P, HALF, 2, P], F32, name="y_rows%d" % half)
+            for i in range(HALF):
+                m = HALF * half + i
                 nc.scalar.activation(
                     rows[:, i, :, :], sums[i][:].rearrange("j (p t) -> j t p", t=4)[:, 2 * u : 2 * u + 2, :],
                     ACT.Copy, scale=gate_col[:, m : m + 1],
@@ -181,28 +199,16 @@ def tile_moe_dyl_gelu_kernel(
                 for i in range(first, last):
                     for e in planes:
                         nc.tensor.transpose(turned[:, i - first, e - planes[0], :], rows[:, i, e, :], ident[:])
-                cols = slice((3 * half + first) * P, (3 * half + last) * P)
+                slots = slice((HALF * half + first) * P, (HALF * half + last) * P)
                 nc.scalar.copy(
-                    y[u][:, planes[0] : planes[-1] + 1, cols].rearrange("p e (m j) -> p m e j", j=P), turned[:]
+                    y[u][:, planes[0] : planes[-1] + 1, slots].rearrange("p e (m j) -> p m e j", j=P), turned[:]
                 )
-
-        def second_layer(half, banks):
-            sums = []
-            for i in range(3):
-                m = 3 * half + i
-                slots = slice(m * P, (m + 1) * P)
-                cols = slice(m * N, (m + 1) * N)
-                acc = bank(banks[i], [P, N])
-                nc.tensor.matmul_mx(
-                    out=acc[:], lhsT=h_w[:, slots].bitcast(FP8X4), lhsT_scale=h_s[:, slots],
-                    rhs=bg_w[:, cols].bitcast(FP8X4), rhs_scale=bg_s[:, cols], start=True, stop=True,
-                )
-                sums.append(acc)
-            return sums
 
         both = (0, 1)
         sums_a = second_layer(0, (0, 1, 2))
         turn_y(0, 0, gate_rows(0, 0, sums_a), ((3, 0, 1, both), (3, 1, 2, both), (4, 2, 3, (0,)), (5, 2, 3, (1,))))
+        h_w[4] = keep.tile([P, 2 * P], U32, name="h_w4", tag="bg_w0_then_h", align_bytes=64)
+        nc.vector.quantize_mx(out=h_w[4][:].bitcast(FP8X4), scales=h_s[:, 4 * P :], in_=h_in[1][:])
         sums_b = second_layer(1, (3, 4, 5))
         turn_y(0, 1, gate_rows(0, 1, sums_b), ((6, 0, 2, both), (7, 2, 3, both)))
         turn_y(1, 0, gate_rows(1, 0, sums_a), ((0, 0, 1, both), (1, 1, 3, both)))
@@ -215,9 +221,7 @@ def tile_moe_dyl_gelu_kernel(
                 base_last[b // 4][:, (b % 4) * P : (b % 4 + 1) * P], base_rows[:, b, 3, :], ident[:]
             )
 
-        placed = [
-            keep.tile([P, T if t < 2 else WIDE], F32, name="placed%d" % t) for t in range(4)
-        ]
+        placed = [keep.tile([P, T if t < 2 else WIDE], F32, name="placed%d" % t) for t in range(4)]
 
         def scatter(t, start, stop):
             nc.vector.tensor_copy(
@@ -225,7 +229,7 @@ def tile_moe_dyl_gelu_kernel(
                 y[t // 2][:, t % 2, start:stop],
             )
 
-        for first, last in B_RUNS:
+        for first, last in RUNS:
             for t in range(2):
                 scatter(t, first * P, last * P)
         for t in range(2, 4):
@@ -239,36 +243,38 @@ def tile_moe_dyl_gelu_kernel(
             toks = slice(2 * c * P, 2 * (c + 1) * P)
             return out_in[c][:, :, 2 * u : 2 * u + 2], result[u][:, :, toks].rearrange("p e j -> p j e")
 
+        group_banks = ((3, 4), (5, 1), (3, 4))
         for t in range(3):
             totals = []
             for half in range(2):
-                total = bank(((3, 4), (5, 1), (3, 4))[t][half], [P, 3 * P])
-                for i in range(3):
+                total = bank(group_banks[t][half], [P, HALF * P])
+                for i in range(HALF):
                     nc.tensor.matmul(
-                        total[:, i * P : (i + 1) * P], base_rows[:, 3 * half + i, t, :], ident[:],
+                        total[:, i * P : (i + 1) * P], base_rows[:, HALF * half + i, t, :], ident[:],
                         start=(i == 0), stop=False, is_transpose=True,
                     )
                 totals.append(total)
             for half in range(2):
                 total = totals[half]
-                acc = bank(2 * half, [P, 3, P])
-                for i in range(3):
-                    b = 3 * half + i
-                    nc.tensor.transpose(acc[:, i, :], placed[t][:, b * P : (b + 1) * P], ident[:])
-                placed_rows = ring.tile([P, 3, P], F32, name="placed_rows")
-                nc.scalar.copy(placed_rows[:], acc[:])
-                for i in range(3):
+                turned = bank(2 * half, [P, HALF, P])
+                for i in range(HALF):
+                    b = HALF * half + i
+                    nc.tensor.transpose(turned[:, i, :], placed[t][:, b * P : (b + 1) * P], ident[:])
+                placed_rows = ring.tile([P, HALF, P], F32, name="placed_rows")
+                nc.scalar.copy(placed_rows[:], turned[:])
+                for i in range(HALF):
                     nc.tensor.matmul(
                         total[:, i * P : (i + 1) * P], placed_rows[:, i, :], ident[:],
-                        start=False, stop=(i == 2), is_transpose=True,
+                        start=False, stop=(i == HALF - 1), is_transpose=True,
                     )
-                nc.scalar.copy(result[t // 2][:, t % 2, 3 * half * P : 3 * (half + 1) * P], total[:])
+                nc.scalar.copy(result[t // 2][:, t % 2, HALF * half * P : HALF * (half + 1) * P], total[:])
             nc.scalar.dma_start(out=out_rows[:, t, :], in_=result[t // 2][:, t % 2, :])
             if t == 1:
                 for c in range(3):
                     nc.scalar.copy(*pair_views(0, c))
 
-        for c in (0, 2, 1):
+        chunk_order = (0, 2, 1)
+        for c in chunk_order:
             toks = slice(2 * c * P, 2 * (c + 1) * P)
             nc.vector.tensor_tensor(
                 result[1][:, 1, toks], base_last[c // 2][:, (c % 2) * 2 * P : (c % 2 + 1) * 2 * P],
@@ -282,7 +288,7 @@ def tile_moe_dyl_gelu_kernel(
         out_w = keep.tile([P, T], U32, name="out_w", align_bytes=64)
         out_s = keep.tile([P, T], U8, name="out_s", align_bytes=64)
         word_rows = out_1[0].rearrange("p c d -> p (c d)").bitcast(I32)
-        for c in (0, 2, 1):
+        for c in chunk_order:
             toks = slice(2 * c * P, 2 * (c + 1) * P)
             nc.vector.quantize_mx(
                 out=out_w[:, toks].bitcast(FP8X4), scales=out_s[:, toks],
@@ -291,5 +297,5 @@ def tile_moe_dyl_gelu_kernel(
             nc.sync.dma_start(out=word_rows[:, toks], in_=out_w[:, toks].bitcast(I32))
         scale_rows = out_2[0].bitcast(I32)
         for q in range(4):
-            eng = nc.scalar if q % 2 else nc.sync
-            eng.dma_start(out=scale_rows[4 * q : 4 * q + 4, :], in_=out_s[:].bitcast(I32)[32 * q : 32 * q + 4, :])
+            queue = nc.scalar if q % 2 else nc.sync
+            queue.dma_start(out=scale_rows[4 * q : 4 * q + 4, :], in_=out_s[:].bitcast(I32)[32 * q : 32 * q + 4, :])

@@ -84,8 +84,8 @@ def tile_moe_dyl_gelu_kernel(
         load_scales(wb_s[:], wb_scales)
         nc.sync.dma_start(out=w_w[:].bitcast(I32), in_=w_words[0].bitcast(I32))
         load_scales(w_s[:], w_scales)
-        load_words(wb_w, wb_words, 0, POOL)
         nc.sync.dma_start(out=gate_by_block[:B, :], in_=gate[0].rearrange("(m p) -> m p", p=P))
+        load_words(wb_w, wb_words, 0, POOL)
 
         def gather(dst, window, offsets, start, stop):
             nc.vector.tensor_copy(dst, window.indirect(offsets[:, start // PER_COL : stop // PER_COL]))
@@ -147,8 +147,7 @@ def tile_moe_dyl_gelu_kernel(
                 turned[:].rearrange("p s u j -> p s j u"),
             )
 
-        frozen_layer(0, (4, 5, 4))
-        gate_turned = bank(5, [P, P])
+        gate_turned = bank(6, [P, P])
         nc.tensor.transpose(gate_turned[:], gate_by_block[:], ident[:])
         nc.scalar.copy(gate_col[:], gate_turned[:, :B])
 
@@ -214,7 +213,8 @@ def tile_moe_dyl_gelu_kernel(
         turn_y(1, 0, gate_rows(1, 0, sums_a), ((0, 0, 1, both), (1, 1, 3, both)))
         turn_y(1, 1, gate_rows(1, 1, sums_b), ((2, 0, 1, both), (0, 1, 3, both)))
 
-        frozen_layer(1, (2, 0, 2))
+        frozen_layer(0, (1, 2, 0))
+        frozen_layer(1, (1, 2, 0))
         base_last = [bank(6, [P, 4 * P]), bank(7, [P, 2 * P])]
         for b in range(B):
             nc.tensor.transpose(

@@ -22,7 +22,7 @@ POOL = E * H
 PER_COL = 16
 HALF = 3
 WIDE = 1024
-ZERO_SPLIT = 3072
+ZERO_SPLIT = 2048
 RUNS = ((0, 1), (1, 3), (3, 6))
 
 
@@ -67,10 +67,9 @@ def tile_moe_dyl_gelu_kernel(
 
         nc.gpsimd.memset(wa_s[:, :ZERO_SPLIT].bitcast(I32), 0)
         nc.vector.memset(wa_s[:, ZERO_SPLIT:].bitcast(I32), 0)
-        nc.gpsimd.memset(x_s[:].bitcast(I32), 0)
+        nc.gpsimd.memset(x_s[:, :T].bitcast(I32), 0)
         nc.vector.memset(wb_s[:].bitcast(I32), 0)
-        nc.vector.memset(w_s[:].bitcast(I32), 0)
-        nc.vector.memset(gate_by_block[:], 0.0)
+        nc.gpsimd.memset(gate_by_block[:], 0.0)
         make_identity(nc, ident[:])
 
         load_words(x_w, x_words, 0, T)
@@ -104,19 +103,6 @@ def tile_moe_dyl_gelu_kernel(
             gather(ag_w[:, first * H : last * H], wa_w[:].bitcast(U32), a_list, first * H, last * H)
         for start in range(0, B * N, HALF * N):
             gather(bg_s[:, start : start + HALF * N], wb_s[:], b_list, start, start + HALF * N)
-
-        base_rows = keep.tile([P, B, 4, P], F32, name="base_rows")
-
-        def frozen_layer(half, banks):
-            for i in range(HALF):
-                b = HALF * half + i
-                toks = slice(b * P, (b + 1) * P)
-                acc = bank(banks[i], [P, N])
-                nc.tensor.matmul_mx(
-                    out=acc[:], lhsT=x_w[:, toks].bitcast(FP8X4), lhsT_scale=x_s[:, toks],
-                    rhs=w_w[:].bitcast(FP4X4), rhs_scale=w_s[:], start=True, stop=True,
-                )
-                nc.scalar.copy(base_rows[:, b, :, :], acc[:].rearrange("j (p t) -> j t p", t=4))
 
         first_banks = (0, 1, 2, 2, 3, 2)
         h_in = [keep.tile([P, 4 * count * P], BF16, name="h_in%d" % count, align_bytes=64) for count in (4, 2)]
@@ -213,8 +199,15 @@ def tile_moe_dyl_gelu_kernel(
         turn_y(1, 0, gate_rows(1, 0, sums_a), ((0, 0, 1, both), (1, 1, 3, both)))
         turn_y(1, 1, gate_rows(1, 1, sums_b), ((2, 0, 1, both), (0, 1, 3, both)))
 
-        frozen_layer(0, (1, 2, 0))
-        frozen_layer(1, (1, 2, 0))
+        base_rows = keep.tile([P, B, 4, P], F32, name="base_rows")
+        for b in range(B):
+            toks = slice(b * P, (b + 1) * P)
+            acc = bank((b + 1) % HALF, [P, N])
+            nc.tensor.matmul_mx(
+                out=acc[:], lhsT=x_w[:, toks].bitcast(FP8X4), lhsT_scale=x_s[:, toks],
+                rhs=w_w[:].bitcast(FP4X4), rhs_scale=w_s[:], start=True, stop=True,
+            )
+            nc.scalar.copy(base_rows[:, b, :, :], acc[:].rearrange("j (p t) -> j t p", t=4))
         base_last = [bank(6, [P, 4 * P]), bank(7, [P, 2 * P])]
         for b in range(B):
             nc.tensor.transpose(

@@ -24,6 +24,8 @@ HALF = 3
 WIDE = 1024
 ZERO_SPLIT = 2048
 RUNS = ((0, 1), (1, 3), (3, 6))
+GROUPS = ((0, 1), (1, 3), (3, 4), (4, 6))
+EARLY = 4
 
 
 def tile_moe_dyl_gelu_kernel(
@@ -76,46 +78,51 @@ def tile_moe_dyl_gelu_kernel(
         nc.sync.dma_start(tok_list[:], offs)
         nc.sync.dma_start(a_list[:], offs2)
         load_scales(wa_s[:], wa_scales)
-        load_words(wa_w, wa_words, 0, POOL // 2)
         load_scales(x_s[:, :T], x_scales)
-        load_words(wa_w, wa_words, POOL // 2, POOL)
+        load_words(wa_w, wa_words, 0, POOL // 2)
         nc.sync.dma_start(b_list[:], offs3)
         load_scales(wb_s[:], wb_scales)
+        load_words(wa_w, wa_words, POOL // 2, POOL)
+        load_words(wb_w, wb_words, 0, POOL)
+        nc.sync.dma_start(out=gate_by_block[:B, :], in_=gate[0].rearrange("(m p) -> m p", p=P))
         nc.sync.dma_start(out=w_w[:].bitcast(I32), in_=w_words[0].bitcast(I32))
         load_scales(w_s[:], w_scales)
-        nc.sync.dma_start(out=gate_by_block[:B, :], in_=gate[0].rearrange("(m p) -> m p", p=P))
-        load_words(wb_w, wb_words, 0, POOL)
 
         def gather(dst, window, offsets, start, stop):
             nc.vector.tensor_copy(dst, window.indirect(offsets[:, start // PER_COL : stop // PER_COL]))
 
         xg_w = keep.tile([P, T], U32, name="xg_w", align_bytes=64)
         xg_s = keep.tile([P, T], U8, name="xg_s", align_bytes=64)
-        ag_w = keep.tile([P, B * H], U32, name="ag_w", align_bytes=64)
+        ag_w = {
+            first: keep.tile([P, (last - first) * H], U32, name="ag_w%d" % first, align_bytes=64)
+            for first, last in RUNS
+        }
         ag_s = keep.tile([P, B * H], U8, name="ag_s", align_bytes=64)
-        bg_s = keep.tile([P, B * N], U8, name="bg_s", align_bytes=64)
+        bg_s = {0: keep.tile([P, EARLY * N], U8, name="bg_s0", align_bytes=64)}
 
         gather(xg_w[:], x_w[:].bitcast(U32), tok_list, 0, T)
         for start in range(0, B * H, HALF * H):
             gather(ag_s[:, start : start + HALF * H], wa_s[:], a_list, start, start + HALF * H)
         gather(xg_s[:], x_s[:], tok_list, 0, T)
+        gather(bg_s[0][:], wb_s[:], b_list, 0, EARLY * N)
         for first, last in RUNS:
-            gather(ag_w[:, first * H : last * H], wa_w[:].bitcast(U32), a_list, first * H, last * H)
-        for start in range(0, B * N, HALF * N):
-            gather(bg_s[:, start : start + HALF * N], wb_s[:], b_list, start, start + HALF * N)
+            gather(ag_w[first][:], wa_w[:].bitcast(U32), a_list, first * H, last * H)
 
-        first_banks = (0, 1, 2, 2, 3, 2)
-        h_in = [keep.tile([P, 4 * count * P], BF16, name="h_in%d" % count, align_bytes=64) for count in (4, 2)]
-        for pair in range(B // 2):
-            turned = bank(3 + pair, [P, 2, 2, P])
-            for side in range(2):
-                m = 2 * pair + side
+        first_banks = (0, 1, 2, 3, 1, 2)
+        turn_banks = (3, 4, 5, 4)
+        h_in = {}
+        for group, (first, last) in enumerate(GROUPS):
+            count = last - first
+            turned = bank(turn_banks[group], [P, count, 2, P])
+            for m in range(first, last):
                 slots = slice(m * P, (m + 1) * P)
                 cols = slice(m * H, (m + 1) * H)
+                run = max(start for start in ag_w if start <= m)
                 acc = bank(first_banks[m], [P, H])
                 nc.tensor.matmul_mx(
                     out=acc[:], lhsT=xg_w[:, slots].bitcast(FP8X4), lhsT_scale=xg_s[:, slots],
-                    rhs=ag_w[:, cols].bitcast(FP8X4), rhs_scale=ag_s[:, cols], start=True, stop=True,
+                    rhs=ag_w[run][:, (m - run) * H : (m - run + 1) * H].bitcast(FP8X4), rhs_scale=ag_s[:, cols],
+                    start=True, stop=True,
                 )
                 h_rows = keep.tile([P, H], BF16, name="h_rows%d" % m, align_bytes=64)
                 nc.scalar.activation(
@@ -125,11 +132,11 @@ def tile_moe_dyl_gelu_kernel(
                 )
                 for u in range(2):
                     nc.tensor.transpose(
-                        turned[:, side, u, :], h_rows[:].bitcast(F32)[:, u * P : (u + 1) * P], ident[:]
+                        turned[:, m - first, u, :], h_rows[:].bitcast(F32)[:, u * P : (u + 1) * P], ident[:]
                     )
-            start = (pair % 2) * 8 * P
+            h_in[first] = keep.tile([P, 4 * count * P], BF16, name="h_in%d" % first, align_bytes=64)
             nc.scalar.copy(
-                h_in[pair // 2][:, start : start + 8 * P].bitcast(F32).rearrange("p (s j u) -> p s j u", s=2, u=2),
+                h_in[first][:].bitcast(F32).rearrange("p (s j u) -> p s j u", s=count, u=2),
                 turned[:].rearrange("p s u j -> p s j u"),
             )
 
@@ -137,16 +144,32 @@ def tile_moe_dyl_gelu_kernel(
         nc.tensor.transpose(gate_turned[:], gate_by_block[:], ident[:])
         nc.scalar.copy(gate_col[:], gate_turned[:, :B])
 
-        h_w = {0: keep.tile([P, 4 * P], U32, name="h_w0", align_bytes=64)}
         h_s = keep.tile([P, T], U8, name="h_s", align_bytes=64)
-        nc.vector.quantize_mx(out=h_w[0][:].bitcast(FP8X4), scales=h_s[:, : 4 * P], in_=h_in[0][:])
-        bg_w = {
-            0: keep.tile([P, N], U32, name="bg_w0", tag="bg_w0_then_h", align_bytes=64),
-            1: keep.tile([P, 2 * N], U32, name="bg_w1", align_bytes=64),
-            3: keep.tile([P, 3 * N], U32, name="bg_w3", align_bytes=64),
-        }
-        for first, last in RUNS:
+        h_w = {}
+        bg_w = {}
+
+        def quantise_h(run, first, last):
+            nc.vector.quantize_mx(
+                out=h_w[run][:, (first - run) * P : (last - run) * P].bitcast(FP8X4),
+                scales=h_s[:, first * P : last * P], in_=h_in[first][:],
+            )
+
+        def gather_wb(first, last, tag):
+            bg_w[first] = keep.tile([P, (last - first) * N], U32, name="bg_w%d" % first, tag=tag, align_bytes=64)
             gather(bg_w[first][:], wb_w[:].bitcast(U32), b_list, first * N, last * N)
+
+        bg_s[EARLY] = keep.tile([P, (B - EARLY) * N], U8, name="bg_s1", tag="ag_w0", align_bytes=64)
+        gather(bg_s[EARLY][:], wb_s[:], b_list, EARLY * N, B * N)
+        h_w[0] = keep.tile([P, P], U32, name="h_w0", align_bytes=64)
+        quantise_h(0, 0, 1)
+        gather_wb(0, 1, "bg_w0")
+        gather_wb(1, 3, "bg_w1")
+        h_w[1] = keep.tile([P, 2 * P], U32, name="h_w1", align_bytes=64)
+        quantise_h(1, 1, 3)
+        h_w[3] = keep.tile([P, 3 * P], U32, name="h_w3", align_bytes=64)
+        quantise_h(3, 3, 4)
+        gather_wb(3, 6, "h_rows4")
+        quantise_h(3, 4, 6)
 
         y = [keep.tile([P, 2, T], F32, name="y%d" % u) for u in range(2)]
 
@@ -155,14 +178,15 @@ def tile_moe_dyl_gelu_kernel(
             for i in range(HALF):
                 m = HALF * half + i
                 slots = slice(m * P, (m + 1) * P)
-                cols = slice(m * N, (m + 1) * N)
+                scale_run = max(first for first in bg_s if first <= m)
                 run = max(first for first in bg_w if first <= m)
                 part = max(first for first in h_w if first <= m)
                 acc = bank(banks[i], [P, N])
                 nc.tensor.matmul_mx(
                     out=acc[:], lhsT=h_w[part][:, (m - part) * P : (m - part + 1) * P].bitcast(FP8X4),
                     lhsT_scale=h_s[:, slots],
-                    rhs=bg_w[run][:, (m - run) * N : (m - run + 1) * N].bitcast(FP8X4), rhs_scale=bg_s[:, cols],
+                    rhs=bg_w[run][:, (m - run) * N : (m - run + 1) * N].bitcast(FP8X4),
+                    rhs_scale=bg_s[scale_run][:, (m - scale_run) * N : (m - scale_run + 1) * N],
                     start=True, stop=True,
                 )
                 sums.append(acc)
@@ -192,8 +216,6 @@ def tile_moe_dyl_gelu_kernel(
         both = (0, 1)
         sums_a = second_layer(0, (0, 1, 2))
         turn_y(0, 0, gate_rows(0, 0, sums_a), ((3, 0, 1, both), (3, 1, 2, both), (4, 2, 3, (0,)), (5, 2, 3, (1,))))
-        h_w[4] = keep.tile([P, 2 * P], U32, name="h_w4", tag="bg_w0_then_h", align_bytes=64)
-        nc.vector.quantize_mx(out=h_w[4][:].bitcast(FP8X4), scales=h_s[:, 4 * P :], in_=h_in[1][:])
         sums_b = second_layer(1, (3, 4, 5))
         turn_y(0, 1, gate_rows(0, 1, sums_b), ((6, 0, 2, both), (7, 2, 3, both)))
         turn_y(1, 0, gate_rows(1, 0, sums_a), ((0, 0, 1, both), (1, 1, 3, both)))
@@ -214,7 +236,11 @@ def tile_moe_dyl_gelu_kernel(
                 base_last[b // 4][:, (b % 4) * P : (b % 4 + 1) * P], base_rows[:, b, 3, :], ident[:]
             )
 
-        placed = [keep.tile([P, T if t < 2 else WIDE], F32, name="placed%d" % t) for t in range(4)]
+        placed_tags = ("placed0", "placed1", "placed2", "placed3")
+        placed = [
+            keep.tile([P, T if t < 2 else WIDE], F32, name="placed%d" % t, tag=placed_tags[t], align_bytes=64)
+            for t in range(4)
+        ]
 
         def scatter(t, start, stop):
             nc.vector.tensor_copy(

@@ -26,6 +26,7 @@ ZERO_SPLIT = 2048
 RUNS = ((0, 1), (1, 3), (3, 6))
 GROUPS = ((0, 1), (1, 3), (3, 4), (4, 6))
 EARLY = 4
+CHUNKS = ((0, P), (P, 3 * P), (3 * P, 4 * P), (4 * P, 6 * P))
 
 
 def tile_moe_dyl_gelu_kernel(
@@ -256,10 +257,12 @@ def tile_moe_dyl_gelu_kernel(
 
         result = [keep.tile([P, 2, T], F32, name="result%d" % u) for u in range(2)]
         out_rows = out_0.rearrange("(p t) c -> p t c", t=4)
-        out_in = [keep.tile([P, 2 * P, 4], BF16, name="out_in%d" % c, align_bytes=64) for c in range(3)]
+        out_in = [
+            keep.tile([P, stop - start, 4], BF16, name="out_in%d" % start, align_bytes=64) for start, stop in CHUNKS
+        ]
 
         def pair_views(u, c):
-            toks = slice(2 * c * P, 2 * (c + 1) * P)
+            toks = slice(*CHUNKS[c])
             return out_in[c][:, :, 2 * u : 2 * u + 2], result[u][:, :, toks].rearrange("p e j -> p j e")
 
         group_banks = ((3, 4), (5, 1), (3, 4))
@@ -289,31 +292,33 @@ def tile_moe_dyl_gelu_kernel(
                 nc.scalar.copy(result[t // 2][:, t % 2, HALF * half * P : HALF * (half + 1) * P], total[:])
             nc.scalar.dma_start(out=out_rows[:, t, :], in_=result[t // 2][:, t % 2, :])
             if t == 1:
-                for c in range(3):
+                for c in range(len(CHUNKS)):
                     nc.scalar.copy(*pair_views(0, c))
 
-        chunk_order = (0, 2, 1)
-        for c in chunk_order:
-            toks = slice(2 * c * P, 2 * (c + 1) * P)
+        for c in (0, 1, 3, 2):
+            start, stop = CHUNKS[c]
+            first = start // (4 * P) * 4 * P
             nc.vector.tensor_tensor(
-                result[1][:, 1, toks], base_last[c // 2][:, (c % 2) * 2 * P : (c % 2 + 1) * 2 * P],
-                placed[3][:, toks], ADD,
+                result[1][:, 1, start:stop], base_last[start // (4 * P)][:, start - first : stop - first],
+                placed[3][:, start:stop], ADD,
             )
         nc.sync.dma_start(out=out_rows[:, 3, :], in_=result[1][:, 1, :])
-        nc.scalar.copy(*pair_views(1, 0))
-        nc.scalar.copy(*pair_views(1, 1))
-        nc.vector.tensor_copy(*pair_views(1, 2))
+        for c in range(3):
+            nc.scalar.copy(*pair_views(1, c))
+        nc.vector.tensor_copy(*pair_views(1, 3))
 
         out_w = keep.tile([P, T], U32, name="out_w", align_bytes=64)
         out_s = keep.tile([P, T], U8, name="out_s", align_bytes=64)
         word_rows = out_1[0].rearrange("p c d -> p (c d)").bitcast(I32)
-        for c in chunk_order:
-            toks = slice(2 * c * P, 2 * (c + 1) * P)
+        for c in (0, 3, 1, 2):
+            toks = slice(*CHUNKS[c])
             nc.vector.quantize_mx(
                 out=out_w[:, toks].bitcast(FP8X4), scales=out_s[:, toks],
                 in_=out_in[c][:].rearrange("p j d -> p (j d)"),
             )
-            nc.sync.dma_start(out=word_rows[:, toks], in_=out_w[:, toks].bitcast(I32))
+            if c > 0:
+                stored = slice(0 if c == 1 else toks.start, toks.stop)
+                nc.sync.dma_start(out=word_rows[:, stored], in_=out_w[:, stored].bitcast(I32))
         scale_rows = out_2[0].bitcast(I32)
         for q in range(4):
             queue = nc.scalar if q % 2 else nc.sync

@@ -37,7 +37,6 @@ def tile_moe_dyl_gelu_kernel(
     with ExitStack() as ctx:
         lists = ctx.enter_context(tc.tile_pool(name="lists", bufs=1))
         keep = ctx.enter_context(tc.tile_pool(name="keep", bufs=1))
-        ring = ctx.enter_context(tc.tile_pool(name="ring", bufs=3))
         psum = ctx.enter_context(tc.psum_pool(name="psum", bufs=1))
 
         def bank(number, shape):
@@ -73,6 +72,7 @@ def tile_moe_dyl_gelu_kernel(
         nc.gpsimd.memset(x_s[:, :T].bitcast(I32), 0)
         nc.vector.memset(wb_s[:].bitcast(I32), 0)
         nc.gpsimd.memset(gate_by_block[:], 0.0)
+        nc.gpsimd.memset(w_s[:].bitcast(I32), 0)
         make_identity(nc, ident[:])
 
         load_words(x_w, x_words, 0, T)
@@ -172,88 +172,84 @@ def tile_moe_dyl_gelu_kernel(
         gather_wb(3, 6, "h_rows4")
         quantise_h(3, 4, 6)
 
-        y = [keep.tile([P, 2, T], F32, name="y%d" % u) for u in range(2)]
+        y = [keep.tile([P, 4, 2 * P], F32, name="y%d" % g) for g in range(B // 2)]
+        sum_banks = (0, 1, 2, 2, 5, 2)
+        y_banks = (6, 7, 5, 0, 1, 6)
+        placed = {}
 
-        def second_layer(half, banks):
-            sums = []
-            for i in range(HALF):
-                m = HALF * half + i
-                slots = slice(m * P, (m + 1) * P)
-                scale_run = max(first for first in bg_s if first <= m)
-                run = max(first for first in bg_w if first <= m)
-                part = max(first for first in h_w if first <= m)
-                acc = bank(banks[i], [P, N])
-                nc.tensor.matmul_mx(
-                    out=acc[:], lhsT=h_w[part][:, (m - part) * P : (m - part + 1) * P].bitcast(FP8X4),
-                    lhsT_scale=h_s[:, slots],
-                    rhs=bg_w[run][:, (m - run) * N : (m - run + 1) * N].bitcast(FP8X4),
-                    rhs_scale=bg_s[scale_run][:, (m - scale_run) * N : (m - scale_run + 1) * N],
-                    start=True, stop=True,
-                )
-                sums.append(acc)
-            return sums
-
-        def gate_rows(u, half, sums):
-            rows = keep.tile([P, HALF, 2, P], F32, name="y_rows%d" % half)
-            for i in range(HALF):
-                m = HALF * half + i
-                nc.scalar.activation(
-                    rows[:, i, :, :], sums[i][:].rearrange("j (p t) -> j t p", t=4)[:, 2 * u : 2 * u + 2, :],
-                    ACT.Copy, scale=gate_col[:, m : m + 1],
-                )
+        def second_layer(m):
+            slots = slice(m * P, (m + 1) * P)
+            scale_run = max(first for first in bg_s if first <= m)
+            run = max(first for first in bg_w if first <= m)
+            part = max(first for first in h_w if first <= m)
+            acc = bank(sum_banks[m], [P, N])
+            nc.tensor.matmul_mx(
+                out=acc[:], lhsT=h_w[part][:, (m - part) * P : (m - part + 1) * P].bitcast(FP8X4),
+                lhsT_scale=h_s[:, slots],
+                rhs=bg_w[run][:, (m - run) * N : (m - run + 1) * N].bitcast(FP8X4),
+                rhs_scale=bg_s[scale_run][:, (m - scale_run) * N : (m - scale_run + 1) * N],
+                start=True, stop=True,
+            )
+            rows = keep.tile([P, 4, P], F32, name="y_rows%d" % m, align_bytes=64)
+            nc.scalar.activation(
+                rows[:], acc[:].rearrange("j (p t) -> j t p", t=4), ACT.Copy, scale=gate_col[:, m : m + 1]
+            )
             return rows
 
-        def turn_y(u, half, rows, pieces):
-            for number, first, last, planes in pieces:
-                turned = bank(number, [P, last - first, len(planes), P])
-                for i in range(first, last):
-                    for e in planes:
-                        nc.tensor.transpose(turned[:, i - first, e - planes[0], :], rows[:, i, e, :], ident[:])
-                slots = slice((HALF * half + first) * P, (HALF * half + last) * P)
-                nc.scalar.copy(
-                    y[u][:, planes[0] : planes[-1] + 1, slots].rearrange("p e (m j) -> p m e j", j=P), turned[:]
+        def turn_y(m, rows):
+            turned = bank(y_banks[m], [P, 4, P])
+            for t in range(4):
+                nc.tensor.transpose(turned[:, t, :], rows[:, t, :], ident[:])
+            nc.scalar.copy(y[m // 2][:, :, m % 2 * P : (m % 2 + 1) * P], turned[:])
+
+        def scatter(t, g):
+            if t not in placed:
+                tag = "y_rows5" if t == 3 else "placed%d" % t
+                placed[t] = keep.tile([P, T], F32, name="placed%d" % t, tag=tag, align_bytes=64)
+            window = placed[t][:].indirect(tok_list[:, 2 * P * g // PER_COL : 2 * P * (g + 1) // PER_COL])
+            if t < 2:
+                nc.vector.tensor_copy(window, y[g][:, t, :])
+            else:
+                nc.scalar.activation(window, y[g][:, t, :], ACT.Copy)
+
+        rows = [second_layer(0), second_layer(1)]
+        turn_y(0, rows[0])
+        rows.append(second_layer(2))
+        turn_y(1, rows[1])
+        turn_y(2, rows[2])
+        scatter(2, 0)
+        rows.append(second_layer(3))
+        rows.append(second_layer(4))
+        turn_y(3, rows[3])
+        rows.append(second_layer(5))
+        turn_y(4, rows[4])
+        turn_y(5, rows[5])
+        for g in range(3):
+            scatter(0, g)
+            scatter(1, g)
+        scatter(2, 1)
+        scatter(2, 2)
+        for g in range(3):
+            scatter(3, g)
+
+        wd_w = keep.tile([P, N], U16, name="wd_w", align_bytes=64)
+        wd_s = keep.tile([P, N], U8, name="wd_s", align_bytes=64)
+        nc.scalar.copy(wd_w[:].rearrange("k (t p) -> k t p", t=4), w_w[:].bitcast(U16).rearrange("k (p t) -> k t p", t=4))
+        nc.vector.tensor_copy(wd_s[:].rearrange("k (t p) -> k p t", t=4), w_s[:].rearrange("k (p t) -> k p t", t=4))
+        wide_banks = (3, 7, 0, 1)
+        rest_banks = (4, 5)
+        base = []
+        for t in range(4):
+            if t % 2 == 0:
+                rest = bank(rest_banks[t // 2], [P, 2, T - 4 * P])
+            wide = bank(wide_banks[t], [P, 4 * P])
+            for out, toks in ((wide[:], slice(0, 4 * P)), (rest[:, t % 2, :], slice(4 * P, T))):
+                nc.tensor.matmul_mx(
+                    out=out, lhsT=wd_w[:, t * P : (t + 1) * P].bitcast(U8).bitcast(FP4X4),
+                    lhsT_scale=wd_s[:, t * P : (t + 1) * P],
+                    rhs=x_w[:, toks].bitcast(FP8X4), rhs_scale=x_s[:, toks], start=True, stop=True,
                 )
-
-        both = (0, 1)
-        sums_a = second_layer(0, (0, 1, 2))
-        turn_y(0, 0, gate_rows(0, 0, sums_a), ((3, 0, 1, both), (3, 1, 2, both), (4, 2, 3, (0,)), (5, 2, 3, (1,))))
-        sums_b = second_layer(1, (3, 4, 5))
-        turn_y(0, 1, gate_rows(0, 1, sums_b), ((6, 0, 2, both), (7, 2, 3, both)))
-        turn_y(1, 0, gate_rows(1, 0, sums_a), ((0, 0, 1, both), (1, 1, 3, both)))
-        turn_y(1, 1, gate_rows(1, 1, sums_b), ((2, 0, 1, both), (0, 1, 3, both)))
-
-        base_rows = keep.tile([P, B, 4, P], F32, name="base_rows")
-        for b in range(B):
-            toks = slice(b * P, (b + 1) * P)
-            acc = bank((b + 1) % HALF, [P, N])
-            nc.tensor.matmul_mx(
-                out=acc[:], lhsT=x_w[:, toks].bitcast(FP8X4), lhsT_scale=x_s[:, toks],
-                rhs=w_w[:].bitcast(FP4X4), rhs_scale=w_s[:], start=True, stop=True,
-            )
-            nc.scalar.copy(base_rows[:, b, :, :], acc[:].rearrange("j (p t) -> j t p", t=4))
-        base_last = [bank(6, [P, 4 * P]), bank(7, [P, 2 * P])]
-        for b in range(B):
-            nc.tensor.transpose(
-                base_last[b // 4][:, (b % 4) * P : (b % 4 + 1) * P], base_rows[:, b, 3, :], ident[:]
-            )
-
-        placed_tags = ("placed0", "placed1", "placed2", "placed3")
-        placed = [
-            keep.tile([P, T if t < 2 else WIDE], F32, name="placed%d" % t, tag=placed_tags[t], align_bytes=64)
-            for t in range(4)
-        ]
-
-        def scatter(t, start, stop):
-            nc.vector.tensor_copy(
-                placed[t][:].indirect(tok_list[:, start // PER_COL : stop // PER_COL]),
-                y[t // 2][:, t % 2, start:stop],
-            )
-
-        for first, last in RUNS:
-            for t in range(2):
-                scatter(t, first * P, last * P)
-        for t in range(2, 4):
-            scatter(t, 0, T)
+            base.append((wide, rest))
 
         result = [keep.tile([P, 2, T], F32, name="result%d" % u) for u in range(2)]
         out_rows = out_0.rearrange("(p t) c -> p t c", t=4)
@@ -265,59 +261,34 @@ def tile_moe_dyl_gelu_kernel(
             toks = slice(*CHUNKS[c])
             return out_in[c][:, :, 2 * u : 2 * u + 2], result[u][:, :, toks].rearrange("p e j -> p j e")
 
-        group_banks = ((3, 4), (5, 1), (3, 4))
-        for t in range(3):
-            totals = []
-            for half in range(2):
-                total = bank(group_banks[t][half], [P, HALF * P])
-                for i in range(HALF):
-                    nc.tensor.matmul(
-                        total[:, i * P : (i + 1) * P], base_rows[:, HALF * half + i, t, :], ident[:],
-                        start=(i == 0), stop=False, is_transpose=True,
-                    )
-                totals.append(total)
-            for half in range(2):
-                total = totals[half]
-                turned = bank(2 * half, [P, HALF, P])
-                for i in range(HALF):
-                    b = HALF * half + i
-                    nc.tensor.transpose(turned[:, i, :], placed[t][:, b * P : (b + 1) * P], ident[:])
-                placed_rows = ring.tile([P, HALF, P], F32, name="placed_rows")
-                nc.scalar.copy(placed_rows[:], turned[:])
-                for i in range(HALF):
-                    nc.tensor.matmul(
-                        total[:, i * P : (i + 1) * P], placed_rows[:, i, :], ident[:],
-                        start=False, stop=(i == HALF - 1), is_transpose=True,
-                    )
-                nc.scalar.copy(result[t // 2][:, t % 2, HALF * half * P : HALF * (half + 1) * P], total[:])
-            nc.scalar.dma_start(out=out_rows[:, t, :], in_=result[t // 2][:, t % 2, :])
-            if t == 1:
-                for c in range(len(CHUNKS)):
-                    nc.scalar.copy(*pair_views(0, c))
+        def add(t, start, stop):
+            wide, rest = base[t]
+            sums = wide[:, start:stop] if stop <= 4 * P else rest[:, t % 2, start - 4 * P : stop - 4 * P]
+            nc.vector.tensor_tensor(result[t // 2][:, t % 2, start:stop], sums, placed[t][:, start:stop], ADD)
 
-        for c in (0, 1, 3, 2):
-            start, stop = CHUNKS[c]
-            first = start // (4 * P) * 4 * P
-            nc.vector.tensor_tensor(
-                result[1][:, 1, start:stop], base_last[start // (4 * P)][:, start - first : stop - first],
-                placed[3][:, start:stop], ADD,
-            )
+        for t in range(3):
+            add(t, 0, 4 * P)
+            add(t, 4 * P, T)
+            nc.sync.dma_start(out=out_rows[:, t, :], in_=result[t // 2][:, t % 2, :])
+        for c in range(len(CHUNKS)):
+            nc.scalar.copy(*pair_views(0, c))
+        for start, stop in CHUNKS:
+            add(3, start, stop)
         nc.sync.dma_start(out=out_rows[:, 3, :], in_=result[1][:, 1, :])
-        for c in range(3):
-            nc.scalar.copy(*pair_views(1, c))
-        nc.vector.tensor_copy(*pair_views(1, 3))
 
         out_w = keep.tile([P, T], U32, name="out_w", align_bytes=64)
         out_s = keep.tile([P, T], U8, name="out_s", align_bytes=64)
         word_rows = out_1[0].rearrange("p c d -> p (c d)").bitcast(I32)
-        for c in (0, 3, 1, 2):
+        for c in range(len(CHUNKS)):
+            nc.vector.tensor_copy(*pair_views(1, c))
+        for c in range(len(CHUNKS)):
             toks = slice(*CHUNKS[c])
             nc.vector.quantize_mx(
                 out=out_w[:, toks].bitcast(FP8X4), scales=out_s[:, toks],
                 in_=out_in[c][:].rearrange("p j d -> p (j d)"),
             )
-            if c > 0:
-                stored = slice(0 if c == 1 else toks.start, toks.stop)
+            if c % 2:
+                stored = slice(CHUNKS[c - 1][0], toks.stop)
                 nc.sync.dma_start(out=word_rows[:, stored], in_=out_w[:, stored].bitcast(I32))
         scale_rows = out_2[0].bitcast(I32)
         for q in range(4):

@@ -16,6 +16,7 @@ FP8X4 = mybir.dt.float8_e4m3fn_x4
 FP4X4 = mybir.dt.float4_e2m1fn_x4
 ACT = mybir.ActivationFunctionType
 ADD = mybir.AluOpType.add
+MULT = mybir.AluOpType.mult
 
 P = 128
 POOL = E * H
@@ -23,9 +24,9 @@ PER_COL = 16
 HALF = 3
 WIDE = 1024
 ZERO_SPLIT = 2048
-RUNS = ((0, 1), (1, 3), (3, 6))
-GROUPS = ((0, 1), (1, 3), (3, 4), (4, 6))
-EARLY = 4
+A_ROW = 0
+B_ROW = 0
+BANK = 512
 CHUNKS = ((0, P), (P, 3 * P), (3 * P, 4 * P), (4 * P, 6 * P))
 
 
@@ -37,258 +38,268 @@ def tile_moe_dyl_gelu_kernel(
     with ExitStack() as ctx:
         lists = ctx.enter_context(tc.tile_pool(name="lists", bufs=1))
         keep = ctx.enter_context(tc.tile_pool(name="keep", bufs=1))
+        reuse = ctx.enter_context(tc.tile_pool(name="reuse", bufs=1))
         psum = ctx.enter_context(tc.psum_pool(name="psum", bufs=1))
 
         def bank(number, shape):
             return psum.tile(shape, F32, name="bank%d" % number)
 
+        def sbuf(shape, dtype, name, tag=None):
+            if isinstance(tag, int):
+                return reuse.tile(shape, dtype, name=name, offset=tag, align_bytes=64)
+            return keep.tile(shape, dtype, name=name, tag=tag or name, align_bytes=64)
+
         tok_list = lists.tile([P, T // PER_COL], U16, name="tok_list")
         a_list = lists.tile([P, B * H // PER_COL], U16, name="a_list")
         b_list = lists.tile([P, B * N // PER_COL], U16, name="b_list")
 
-        x_w = keep.tile([P, WIDE], I32, name="x_w", align_bytes=64)
-        x_s = keep.tile([P, WIDE], U8, name="x_s", align_bytes=64)
-        w_w = keep.tile([P, 2 * N], U8, name="w_w", align_bytes=64)
-        w_s = keep.tile([P, N], U8, name="w_s", align_bytes=64)
-        wa_w = keep.tile([P, POOL], I32, name="wa_w", align_bytes=64)
-        wa_s = keep.tile([P, POOL], U8, name="wa_s", align_bytes=64)
-        wb_w = keep.tile([P, POOL], I32, name="wb_w", align_bytes=64)
-        wb_s = keep.tile([P, POOL], U8, name="wb_s", align_bytes=64)
-        gate_by_block = keep.tile([P, P], F32, name="gate_by_block")
-        gate_col = keep.tile([P, B], F32, name="gate_col")
-        ident = keep.tile([P, P], F32, name="ident")
+        x_w = sbuf([P, WIDE], I32, "x_w")
+        x_s = sbuf([P, WIDE], U8, "x_s")
+        w_w = sbuf([P, 2 * N], U8, "w_w")
+        w_s = sbuf([P, N], U8, "w_s")
+        wa_w = sbuf([P, POOL], I32, "wa_w")
+        wa_s = sbuf([P, POOL], U8, "wa_s")
+        wb_w = sbuf([P, POOL], I32, "wb_w")
+        wb_s = sbuf([P, POOL], U8, "wb_s")
+        gate_rows = sbuf([P, HALF * P], F32, "gate_rows")
+        gate_col = sbuf([P, HALF, 2], F32, "gate_col")
+        ident = sbuf([P, P], F32, "ident")
 
         def load_words(tile, words, start, stop):
             rows = words[0].rearrange("p c d -> p (c d)").bitcast(I32)
             nc.sync.dma_start(out=tile[:, start:stop], in_=rows[:, start:stop])
 
-        def load_scales(tile, scales):
+        def load_scales(queue, tile, scales, first_row):
             rows = scales[0].bitcast(I32).rearrange("(q r) c -> r q c", r=4)
             for r in range(4):
-                nc.sync.dma_start(out=tile.bitcast(I32)[r:P:32, :], in_=rows[r])
+                queue.dma_start(out=tile.bitcast(I32)[first_row + r : P : 32, :], in_=rows[r])
 
         nc.gpsimd.memset(wa_s[:, :ZERO_SPLIT].bitcast(I32), 0)
         nc.vector.memset(wa_s[:, ZERO_SPLIT:].bitcast(I32), 0)
         nc.gpsimd.memset(x_s[:, :T].bitcast(I32), 0)
         nc.vector.memset(wb_s[:].bitcast(I32), 0)
-        nc.gpsimd.memset(gate_by_block[:], 0.0)
+        nc.gpsimd.memset(gate_rows[:], 0.0)
         nc.gpsimd.memset(w_s[:].bitcast(I32), 0)
         make_identity(nc, ident[:])
 
         load_words(x_w, x_words, 0, T)
         nc.sync.dma_start(tok_list[:], offs)
         nc.sync.dma_start(a_list[:], offs2)
-        load_scales(wa_s[:], wa_scales)
-        load_scales(x_s[:, :T], x_scales)
+        load_scales(nc.sync, wa_s[:], wa_scales, A_ROW)
         load_words(wa_w, wa_words, 0, POOL // 2)
-        nc.sync.dma_start(b_list[:], offs3)
-        load_scales(wb_s[:], wb_scales)
+        load_scales(nc.sync, x_s[:, :T], x_scales, 0)
         load_words(wa_w, wa_words, POOL // 2, POOL)
-        load_words(wb_w, wb_words, 0, POOL)
-        nc.sync.dma_start(out=gate_by_block[:B, :], in_=gate[0].rearrange("(m p) -> m p", p=P))
+        load_words(wb_w, wb_words, 0, POOL // 2)
+        nc.sync.dma_start(b_list[:], offs3)
+        nc.sync.dma_start(out=gate_rows[:2, :], in_=gate[0].rearrange("(q c) -> q c", q=2))
+        load_scales(nc.sync, wb_s[:], wb_scales, B_ROW)
+        load_words(wb_w, wb_words, POOL // 2, POOL)
         nc.sync.dma_start(out=w_w[:].bitcast(I32), in_=w_words[0].bitcast(I32))
-        load_scales(w_s[:], w_scales)
+        load_scales(nc.sync, w_s[:], w_scales, 0)
 
-        def gather(dst, window, offsets, start, stop):
-            nc.vector.tensor_copy(dst, window.indirect(offsets[:, start // PER_COL : stop // PER_COL]))
+        def gather(name, tag, dtype, window, offsets, start, stop):
+            dst = sbuf([P, stop - start], dtype, name, tag)
+            nc.vector.tensor_copy(dst[:], window.indirect(offsets[:, start // PER_COL : stop // PER_COL]))
+            return dst
 
-        xg_w = keep.tile([P, T], U32, name="xg_w", align_bytes=64)
-        xg_s = keep.tile([P, T], U8, name="xg_s", align_bytes=64)
-        ag_w = {
-            first: keep.tile([P, (last - first) * H], U32, name="ag_w%d" % first, align_bytes=64)
-            for first, last in RUNS
-        }
-        ag_s = keep.tile([P, B * H], U8, name="ag_s", align_bytes=64)
-        bg_s = {0: keep.tile([P, EARLY * N], U8, name="bg_s0", align_bytes=64)}
+        def columns(tiles, m, width):
+            first = max(f for f in tiles if f <= m)
+            return tiles[first][:, (m - first) * width : (m - first + 1) * width]
 
-        gather(xg_w[:], x_w[:].bitcast(U32), tok_list, 0, T)
-        for start in range(0, B * H, HALF * H):
-            gather(ag_s[:, start : start + HALF * H], wa_s[:], a_list, start, start + HALF * H)
-        gather(xg_s[:], x_s[:], tok_list, 0, T)
-        gather(bg_s[0][:], wb_s[:], b_list, 0, EARLY * N)
-        for first, last in RUNS:
-            gather(ag_w[first][:], wa_w[:].bitcast(U32), a_list, first * H, last * H)
+        ag_w, ag_s, bg_w, bg_s, h_in, h_w, h_s, h_rows, h_turned, y_rows = {}, {}, {}, {}, {}, {}, {}, {}, {}, {}
+        y = sbuf([P, 4, T], F32, "y")
+        placed = {}
 
-        first_banks = (0, 1, 2, 3, 1, 2)
-        turn_banks = (3, 4, 5, 4)
-        h_in = {}
-        for group, (first, last) in enumerate(GROUPS):
+        def gather_a_words(first, last, tag=None):
+            ag_w[first] = gather("ag_w%d" % first, tag, U32, wa_w[:].bitcast(U32), a_list, first * H, last * H)
+
+        def gather_a_scales(first, last, tag=None):
+            for f in range(first, last, HALF):
+                ag_s[f] = gather("ag_s%d" % f, tag, U8, wa_s[:], a_list, f * H, (f + HALF) * H)
+
+        def gather_b_words(first, last, tag=None):
+            bg_w[first] = gather("bg_w%d" % first, tag, U32, wb_w[:].bitcast(U32), b_list, first * N, last * N)
+
+        def gather_b_scales(first, last, tag=None):
+            bg_s[first] = gather("bg_s%d" % first, tag, U8, wb_s[:], b_list, first * N, last * N)
+
+        def first_layer(m, number):
+            slots = slice(m * P, (m + 1) * P)
+            acc = bank(number, [P, H])
+            nc.tensor.matmul_mx(
+                out=acc[:], lhsT=xg_w[:, slots].bitcast(FP8X4), lhsT_scale=xg_s[:, slots],
+                rhs=columns(ag_w, m, H).bitcast(FP8X4), rhs_scale=columns(ag_s, m, H)[A_ROW:, :],
+                start=True, stop=True,
+            )
+            h_rows[m] = sbuf([P, H], BF16, "h_rows%d" % m)
+            nc.scalar.activation(
+                h_rows[m][:].rearrange("j (u p e) -> j u p e", u=2, e=2),
+                acc[:].rearrange("j (p u e) -> j u p e", u=2, e=2),
+                ACT.Gelu_apprx_tanh,
+            )
+
+        def turn_h(first, last, number):
             count = last - first
-            turned = bank(turn_banks[group], [P, count, 2, P])
+            turned = bank(number, [P, count, 2, P])
             for m in range(first, last):
-                slots = slice(m * P, (m + 1) * P)
-                cols = slice(m * H, (m + 1) * H)
-                run = max(start for start in ag_w if start <= m)
-                acc = bank(first_banks[m], [P, H])
-                nc.tensor.matmul_mx(
-                    out=acc[:], lhsT=xg_w[:, slots].bitcast(FP8X4), lhsT_scale=xg_s[:, slots],
-                    rhs=ag_w[run][:, (m - run) * H : (m - run + 1) * H].bitcast(FP8X4), rhs_scale=ag_s[:, cols],
-                    start=True, stop=True,
-                )
-                h_rows = keep.tile([P, H], BF16, name="h_rows%d" % m, align_bytes=64)
-                nc.scalar.activation(
-                    h_rows[:].rearrange("j (u p e) -> j u p e", u=2, e=2),
-                    acc[:].rearrange("j (p u e) -> j u p e", u=2, e=2),
-                    ACT.Gelu_apprx_tanh,
-                )
                 for u in range(2):
                     nc.tensor.transpose(
-                        turned[:, m - first, u, :], h_rows[:].bitcast(F32)[:, u * P : (u + 1) * P], ident[:]
+                        turned[:, m - first, u, :], h_rows[m][:].bitcast(F32)[:, u * P : (u + 1) * P], ident[:]
                     )
-            h_in[first] = keep.tile([P, 4 * count * P], BF16, name="h_in%d" % first, align_bytes=64)
+            pair = first - first % HALF
+            if pair not in h_in:
+                h_in[pair] = sbuf([P, 4 * HALF * P], BF16, "h_in%d" % pair)
             nc.scalar.copy(
-                h_in[first][:].bitcast(F32).rearrange("p (s j u) -> p s j u", s=count, u=2),
+                h_in[pair][:, (first - pair) * 4 * P : (last - pair) * 4 * P]
+                .bitcast(F32).rearrange("p (s j u) -> p s j u", s=count, u=2),
                 turned[:].rearrange("p s u j -> p s j u"),
             )
 
-        gate_turned = bank(6, [P, P])
-        nc.tensor.transpose(gate_turned[:], gate_by_block[:], ident[:])
-        nc.scalar.copy(gate_col[:], gate_turned[:, :B])
+        def quantise_h(first, last, tag=None):
+            h_w[first] = sbuf([P, (last - first) * P], U32, "h_w%d" % first)
+            h_s[first] = sbuf([P, (last - first) * P], U8, "h_s%d" % first, tag)
+            nc.vector.quantize_mx(out=h_w[first][:].bitcast(FP8X4), scales=h_s[first][:], in_=h_in[first][:])
 
-        h_s = keep.tile([P, T], U8, name="h_s", align_bytes=64)
-        h_w = {}
-        bg_w = {}
-
-        def quantise_h(run, first, last):
-            nc.vector.quantize_mx(
-                out=h_w[run][:, (first - run) * P : (last - run) * P].bitcast(FP8X4),
-                scales=h_s[:, first * P : last * P], in_=h_in[first][:],
-            )
-
-        def gather_wb(first, last, tag):
-            bg_w[first] = keep.tile([P, (last - first) * N], U32, name="bg_w%d" % first, tag=tag, align_bytes=64)
-            gather(bg_w[first][:], wb_w[:].bitcast(U32), b_list, first * N, last * N)
-
-        bg_s[EARLY] = keep.tile([P, (B - EARLY) * N], U8, name="bg_s1", tag="ag_w0", align_bytes=64)
-        gather(bg_s[EARLY][:], wb_s[:], b_list, EARLY * N, B * N)
-        h_w[0] = keep.tile([P, P], U32, name="h_w0", align_bytes=64)
-        quantise_h(0, 0, 1)
-        gather_wb(0, 1, "bg_w0")
-        gather_wb(1, 3, "bg_w1")
-        h_w[1] = keep.tile([P, 2 * P], U32, name="h_w1", align_bytes=64)
-        quantise_h(1, 1, 3)
-        h_w[3] = keep.tile([P, 3 * P], U32, name="h_w3", align_bytes=64)
-        quantise_h(3, 3, 4)
-        gather_wb(3, 6, "h_rows4")
-        quantise_h(3, 4, 6)
-
-        y = [keep.tile([P, 4, 2 * P], F32, name="y%d" % g) for g in range(B // 2)]
-        sum_banks = (0, 1, 2, 2, 5, 2)
-        y_banks = (6, 7, 5, 0, 1, 6)
-        placed = {}
-
-        def second_layer(m):
-            slots = slice(m * P, (m + 1) * P)
-            scale_run = max(first for first in bg_s if first <= m)
-            run = max(first for first in bg_w if first <= m)
-            part = max(first for first in h_w if first <= m)
-            acc = bank(sum_banks[m], [P, N])
+        def second_layer(m, number):
+            acc = bank(number, [P, N])
             nc.tensor.matmul_mx(
-                out=acc[:], lhsT=h_w[part][:, (m - part) * P : (m - part + 1) * P].bitcast(FP8X4),
-                lhsT_scale=h_s[:, slots],
-                rhs=bg_w[run][:, (m - run) * N : (m - run + 1) * N].bitcast(FP8X4),
-                rhs_scale=bg_s[scale_run][:, (m - scale_run) * N : (m - scale_run + 1) * N],
+                out=acc[:], lhsT=columns(h_w, m, P).bitcast(FP8X4), lhsT_scale=columns(h_s, m, P),
+                rhs=columns(bg_w, m, N).bitcast(FP8X4), rhs_scale=columns(bg_s, m, N)[B_ROW:, :],
                 start=True, stop=True,
             )
-            rows = keep.tile([P, 4, P], F32, name="y_rows%d" % m, align_bytes=64)
-            nc.scalar.activation(
-                rows[:], acc[:].rearrange("j (p t) -> j t p", t=4), ACT.Copy, scale=gate_col[:, m : m + 1]
-            )
-            return rows
+            y_rows[m] = sbuf([P, 4, P], F32, "y_rows%d" % m)
+            sums = acc[:].rearrange("j (p t) -> j t p", t=4)
+            factor = gate_col[:, m % HALF, m // HALF : m // HALF + 1]
+            nc.scalar.activation(y_rows[m][:], sums, ACT.Copy, scale=factor)
 
-        def turn_y(m, rows):
-            turned = bank(y_banks[m], [P, 4, P])
+        def turn_y(m, number):
+            turned = bank(number, [P, 4, P])
             for t in range(4):
-                nc.tensor.transpose(turned[:, t, :], rows[:, t, :], ident[:])
-            nc.scalar.copy(y[m // 2][:, :, m % 2 * P : (m % 2 + 1) * P], turned[:])
+                nc.tensor.transpose(turned[:, t, :], y_rows[m][:, t, :], ident[:])
+            nc.scalar.copy(y[:, :, m * P : (m + 1) * P], turned[:])
 
-        def scatter(t, g):
+        def scatter(engine, t, first, last, tag=None):
             if t not in placed:
-                tag = "y_rows5" if t == 3 else "placed%d" % t
-                placed[t] = keep.tile([P, T], F32, name="placed%d" % t, tag=tag, align_bytes=64)
-            window = placed[t][:].indirect(tok_list[:, 2 * P * g // PER_COL : 2 * P * (g + 1) // PER_COL])
-            if t < 2:
-                nc.vector.tensor_copy(window, y[g][:, t, :])
+                placed[t] = sbuf([P, T], F32, "placed%d" % t, tag)
+            window = placed[t][:].indirect(tok_list[:, first * P // PER_COL : last * P // PER_COL])
+            values = y[:, t, first * P : last * P]
+            if engine == "vector":
+                nc.vector.tensor_copy(window, values)
             else:
-                nc.scalar.activation(window, y[g][:, t, :], ACT.Copy)
+                nc.scalar.activation(window, values, ACT.Copy)
 
-        rows = [second_layer(0), second_layer(1)]
-        turn_y(0, rows[0])
-        rows.append(second_layer(2))
-        turn_y(1, rows[1])
-        turn_y(2, rows[2])
-        scatter(2, 0)
-        rows.append(second_layer(3))
-        rows.append(second_layer(4))
-        turn_y(3, rows[3])
-        rows.append(second_layer(5))
-        turn_y(4, rows[4])
-        turn_y(5, rows[5])
-        for g in range(3):
-            scatter(0, g)
-            scatter(1, g)
-        scatter(2, 1)
-        scatter(2, 2)
-        for g in range(3):
-            scatter(3, g)
+        xg_w = gather("xg_w", None, U32, x_w[:].bitcast(U32), tok_list, 0, T)
+        early = 9216
+        gather_a_scales(0, 3)
+        xg_s = gather("xg_s", None, U8, x_s[:], tok_list, 0, T)
+        gather_a_words(0, 1, early + 1472)
+        gather_a_words(1, 3)
+        first_layer(0, 0)
+        gather_a_scales(3, 6, early)
+        gather_a_words(3, 4, early + 1536 + 4096)
+        gather_a_words(4, 6, early + 1536)
+        turn_h(0, 1, 2)
+        first_layer(1, 1)
+        first_layer(2, 3)
+        turn_h(1, 3, 4)
+        first_layer(3, 2)
+        first_layer(4, 4)
+        first_layer(5, 2)
+        turn_h(3, 4, 5)
+        turn_h(4, 6, 3)
 
-        wd_w = keep.tile([P, N], U16, name="wd_w", align_bytes=64)
-        wd_s = keep.tile([P, N], U8, name="wd_s", align_bytes=64)
-        nc.scalar.copy(wd_w[:].rearrange("k (t p) -> k t p", t=4), w_w[:].bitcast(U16).rearrange("k (p t) -> k t p", t=4))
+        gate_turned = bank(6, [P, HALF, P])
+        for i in range(HALF):
+            nc.tensor.transpose(gate_turned[:, i, :], gate_rows[:, i * P : (i + 1) * P], ident[:])
+        nc.scalar.copy(gate_col[:], gate_turned[:, :, :2])
+
+        held = HALF * N * 4 - 64
+        quantise_h(0, 3)
+        gather_b_scales(0, 3)
+        gather_b_words(0, 1, held)
+        gather_b_words(1, 3)
+        second_layer(0, 7)
+        gather_b_scales(3, 6, held + 1088)
+        quantise_h(3, 6, held + 64)
+        gather_b_words(3, 6, 0)
+        wd_s = sbuf([P, N], U8, "wd_s", held + 576)
         nc.vector.tensor_copy(wd_s[:].rearrange("k (t p) -> k p t", t=4), w_s[:].rearrange("k (p t) -> k p t", t=4))
-        wide_banks = (3, 7, 0, 1)
-        rest_banks = (4, 5)
-        base = []
+        second_layer(1, 1)
+        turn_y(0, 6)
+        second_layer(2, 0)
+        turn_y(1, 7)
+        turn_y(2, 2)
+        wd_w = sbuf([P, N], U16, "wd_w", "y_rows2")
+        nc.scalar.copy(
+            wd_w[:].rearrange("k (t p) -> k t p", t=4), w_w[:].bitcast(U16).rearrange("k (p t) -> k t p", t=4)
+        )
+        scatter("scalar", 2, 0, 2)
+        second_layer(3, 7)
+        second_layer(4, 2)
+        turn_y(3, 1)
+        second_layer(5, 7)
+        turn_y(4, 3)
+        turn_y(5, 4)
+        for first in (0, 2, 4):
+            scatter("vector", 0, first, first + 2)
+            scatter("vector", 1, first, first + 2)
+        scatter("scalar", 2, 2, 4)
+        scatter("scalar", 2, 4, 6)
+        scatter("scalar", 3, 0, 3, "y_rows5")
+        scatter("scalar", 3, 3, 6)
+
+        wide_banks = (5, 6, 2, 7)
+        rest = {0: bank(0, [P, 2, T - BANK]), 1: bank(1, [P, 2, T - BANK])}
+        rest_of = [rest[t // 2][:, t % 2, :] for t in range(4)]
+        wide = {}
         for t in range(4):
-            if t % 2 == 0:
-                rest = bank(rest_banks[t // 2], [P, 2, T - 4 * P])
-            wide = bank(wide_banks[t], [P, 4 * P])
-            for out, toks in ((wide[:], slice(0, 4 * P)), (rest[:, t % 2, :], slice(4 * P, T))):
+            wide[t] = bank(wide_banks[t], [P, BANK])
+            for out, toks in ((wide[t][:], slice(0, BANK)), (rest_of[t], slice(BANK, T))):
                 nc.tensor.matmul_mx(
                     out=out, lhsT=wd_w[:, t * P : (t + 1) * P].bitcast(U8).bitcast(FP4X4),
                     lhsT_scale=wd_s[:, t * P : (t + 1) * P],
                     rhs=x_w[:, toks].bitcast(FP8X4), rhs_scale=x_s[:, toks], start=True, stop=True,
                 )
-            base.append((wide, rest))
 
-        result = [keep.tile([P, 2, T], F32, name="result%d" % u) for u in range(2)]
+        result = [sbuf([P, 2, T], F32, "result%d" % u) for u in range(2)]
         out_rows = out_0.rearrange("(p t) c -> p t c", t=4)
-        out_in = [
-            keep.tile([P, stop - start, 4], BF16, name="out_in%d" % start, align_bytes=64) for start, stop in CHUNKS
-        ]
+        out_in = [sbuf([P, stop - start, 4], BF16, "out_in%d" % start) for start, stop in CHUNKS]
 
         def pair_views(u, c):
             toks = slice(*CHUNKS[c])
             return out_in[c][:, :, 2 * u : 2 * u + 2], result[u][:, :, toks].rearrange("p e j -> p j e")
 
         def add(t, start, stop):
-            wide, rest = base[t]
-            sums = wide[:, start:stop] if stop <= 4 * P else rest[:, t % 2, start - 4 * P : stop - 4 * P]
+            sums = wide[t][:, start:stop] if stop <= BANK else rest_of[t][:, start - BANK : stop - BANK]
             nc.vector.tensor_tensor(result[t // 2][:, t % 2, start:stop], sums, placed[t][:, start:stop], ADD)
 
         for t in range(3):
-            add(t, 0, 4 * P)
-            add(t, 4 * P, T)
+            add(t, 0, BANK)
+            add(t, BANK, T)
             nc.sync.dma_start(out=out_rows[:, t, :], in_=result[t // 2][:, t % 2, :])
-        for c in range(len(CHUNKS)):
+        for c in (0, 1):
             nc.scalar.copy(*pair_views(0, c))
-        for start, stop in CHUNKS:
-            add(3, start, stop)
+        for c in (2, 3):
+            nc.vector.tensor_copy(*pair_views(0, c))
+        for c in (1, 2, 0, 3):
+            add(3, *CHUNKS[c])
         nc.sync.dma_start(out=out_rows[:, 3, :], in_=result[1][:, 1, :])
-
-        out_w = keep.tile([P, T], U32, name="out_w", align_bytes=64)
-        out_s = keep.tile([P, T], U8, name="out_s", align_bytes=64)
-        word_rows = out_1[0].rearrange("p c d -> p (c d)").bitcast(I32)
-        for c in range(len(CHUNKS)):
+        for c in (1, 2):
+            nc.scalar.copy(*pair_views(1, c))
+        for c in (0, 3):
             nc.vector.tensor_copy(*pair_views(1, c))
-        for c in range(len(CHUNKS)):
+
+        out_w = sbuf([P, T], U32, "out_w")
+        out_s = sbuf([P, T], U8, "out_s")
+        word_rows = out_1[0].rearrange("p c d -> p (c d)").bitcast(I32)
+        for c in (0, 3, 1, 2):
             toks = slice(*CHUNKS[c])
             nc.vector.quantize_mx(
                 out=out_w[:, toks].bitcast(FP8X4), scales=out_s[:, toks],
                 in_=out_in[c][:].rearrange("p j d -> p (j d)"),
             )
-            if c % 2:
-                stored = slice(CHUNKS[c - 1][0], toks.stop)
+            if c > 0:
+                stored = slice(0 if c == 1 else toks.start, toks.stop)
                 nc.sync.dma_start(out=word_rows[:, stored], in_=out_w[:, stored].bitcast(I32))
         scale_rows = out_2[0].bitcast(I32)
         for q in range(4):

@@ -1,7 +1,6 @@
 from contextlib import ExitStack
 
 import concourse.mybir as mybir
-from concourse.masks import make_identity
 
 K, T, E, B, H, N = 512, 768, 8, 6, 512, 512
 FLOPS = 2 * K * N * T + 2 * K * H * T + 2 * H * N * T
@@ -23,11 +22,9 @@ POOL = E * H
 PER_COL = 16
 HALF = 3
 WIDE = 1024
-ZERO_SPLIT = 2048
-A_ROW = 0
-B_ROW = 0
 BANK = 512
 CHUNKS = ((0, P), (P, 3 * P), (3 * P, 4 * P), (4 * P, 6 * P))
+LAP = 64
 
 
 def tile_moe_dyl_gelu_kernel(
@@ -44,10 +41,19 @@ def tile_moe_dyl_gelu_kernel(
         def bank(number, shape):
             return psum.tile(shape, F32, name="bank%d" % number)
 
-        def sbuf(shape, dtype, name, tag=None):
-            if isinstance(tag, int):
-                return reuse.tile(shape, dtype, name=name, offset=tag, align_bytes=64)
-            return keep.tile(shape, dtype, name=name, tag=tag or name, align_bytes=64)
+        def sbuf(shape, dtype, name, at=None):
+            if at is not None:
+                return reuse.tile(shape, dtype, name=name, offset=at, align_bytes=64)
+            return keep.tile(shape, dtype, name=name, align_bytes=64)
+
+        words = 4 * N
+        bg4_at = 0
+        bg2_at = bg4_at + 2 * words - LAP
+        gate_at = bg2_at + words - LAP
+        bg1_at = gate_at + 3 * 4 * P
+        bg3_at = bg1_at + words - LAP
+        h_at = bg3_at + words
+        ag0_at = h_at + HALF * 2 * H
 
         tok_list = lists.tile([P, T // PER_COL], U16, name="tok_list")
         a_list = lists.tile([P, B * H // PER_COL], U16, name="a_list")
@@ -61,195 +67,173 @@ def tile_moe_dyl_gelu_kernel(
         wa_s = sbuf([P, POOL], U8, "wa_s")
         wb_w = sbuf([P, POOL], I32, "wb_w")
         wb_s = sbuf([P, POOL], U8, "wb_s")
-        gate_rows = sbuf([P, HALF * P], F32, "gate_rows")
-        gate_col = sbuf([P, HALF, 2], F32, "gate_col")
-        ident = sbuf([P, P], F32, "ident")
+        gate_a = sbuf([P, 3 * P], F32, "gate_a", gate_at)
+        gate_b = sbuf([P, T - P], F32, "gate_b")
 
         def load_words(tile, words, start, stop):
             rows = words[0].rearrange("p c d -> p (c d)").bitcast(I32)
             nc.sync.dma_start(out=tile[:, start:stop], in_=rows[:, start:stop])
 
-        def load_scales(queue, tile, scales, first_row):
+        def load_scales(tile, scales):
             rows = scales[0].bitcast(I32).rearrange("(q r) c -> r q c", r=4)
             for r in range(4):
-                queue.dma_start(out=tile.bitcast(I32)[first_row + r : P : 32, :], in_=rows[r])
+                nc.sync.dma_start(out=tile.bitcast(I32)[r:P:32, :], in_=rows[r])
 
-        nc.gpsimd.memset(wa_s[:, :ZERO_SPLIT].bitcast(I32), 0)
-        nc.vector.memset(wa_s[:, ZERO_SPLIT:].bitcast(I32), 0)
+        def load_spread(name, scales):
+            raw = sbuf([P, H], U8, name)
+            nc.sync.dma_start(out=raw[:].bitcast(I32), in_=scales[0].bitcast(I32).rearrange("b (e c) -> (b e) c", e=E))
+            return raw
+
+        def deal_scales(name, raw):
+            dealt = sbuf([P, H], U8, name)
+            nc.vector.tensor_copy(
+                dealt[:].rearrange("k (t m) -> k m t", t=4), raw[:].rearrange("k (m t) -> k m t", t=4)
+            )
+            return dealt
+
+        def move_scales(dealt, table):
+            for q in (0, 2, 1, 3):
+                nc.sync.dma_start(
+                    out=table[:].bitcast(I32)[32 * q : 32 * q + 4, :], in_=dealt[:].bitcast(I32)[32 * q : 32 * q + 32, :]
+                )
+
         nc.gpsimd.memset(x_s[:, :T].bitcast(I32), 0)
-        nc.vector.memset(wb_s[:].bitcast(I32), 0)
-        nc.gpsimd.memset(gate_rows[:], 0.0)
+        nc.vector.memset(wa_s[:].bitcast(I32), 0)
+        nc.gpsimd.memset(wb_s[:].bitcast(I32), 0)
         nc.gpsimd.memset(w_s[:].bitcast(I32), 0)
-        make_identity(nc, ident[:])
 
+        a_raw = load_spread("a_raw", wa_scales)
+        b_raw = load_spread("b_raw", wb_scales)
         load_words(x_w, x_words, 0, T)
         nc.sync.dma_start(tok_list[:], offs)
+        load_scales(x_s[:, :T], x_scales)
+        load_words(wa_w, wa_words, 0, POOL // 4)
         nc.sync.dma_start(a_list[:], offs2)
-        load_scales(nc.sync, wa_s[:], wa_scales, A_ROW)
-        load_words(wa_w, wa_words, 0, POOL // 2)
-        load_scales(nc.sync, x_s[:, :T], x_scales, 0)
-        load_words(wa_w, wa_words, POOL // 2, POOL)
-        load_words(wb_w, wb_words, 0, POOL // 2)
         nc.sync.dma_start(b_list[:], offs3)
-        nc.sync.dma_start(out=gate_rows[:2, :], in_=gate[0].rearrange("(q c) -> q c", q=2))
-        load_scales(nc.sync, wb_s[:], wb_scales, B_ROW)
-        load_words(wb_w, wb_words, POOL // 2, POOL)
+        move_scales(deal_scales("a_dealt", a_raw), wa_s)
+        load_words(wa_w, wa_words, POOL // 4, POOL)
+        move_scales(deal_scales("b_dealt", b_raw), wb_s)
+        nc.sync.dma_start(out=gate_a[:, :P], in_=gate[:, :P])
+        load_words(wb_w, wb_words, 0, POOL)
         nc.sync.dma_start(out=w_w[:].bitcast(I32), in_=w_words[0].bitcast(I32))
-        load_scales(nc.sync, w_s[:], w_scales, 0)
+        nc.sync.dma_start(out=gate_b[:], in_=gate[:, P:])
+        load_scales(w_s[:], w_scales)
 
-        def gather(name, tag, dtype, window, offsets, start, stop):
-            dst = sbuf([P, stop - start], dtype, name, tag)
-            nc.vector.tensor_copy(dst[:], window.indirect(offsets[:, start // PER_COL : stop // PER_COL]))
+        def gather(name, at, dtype, window, offsets, start, stop, dealt=False):
+            dst = sbuf([P, stop - start], dtype, name, at)
+            view = dst[:].rearrange("k (b t m) -> k b m t", t=4, m=P) if dealt else dst[:]
+            nc.vector.tensor_copy(view, window.indirect(offsets[:, start // PER_COL : stop // PER_COL]))
             return dst
 
         def columns(tiles, m, width):
             first = max(f for f in tiles if f <= m)
             return tiles[first][:, (m - first) * width : (m - first + 1) * width]
 
-        ag_w, ag_s, bg_w, bg_s, h_in, h_w, h_s, h_rows, h_turned, y_rows = {}, {}, {}, {}, {}, {}, {}, {}, {}, {}
-        y = sbuf([P, 4, T], F32, "y")
-        placed = {}
+        ag_w, ag_s, bg_w, bg_s, h_in, h_w, h_s, y, placed = {}, {}, {}, {}, {}, {}, {}, {}, {}
 
-        def gather_a_words(first, last, tag=None):
-            ag_w[first] = gather("ag_w%d" % first, tag, U32, wa_w[:].bitcast(U32), a_list, first * H, last * H)
+        def gather_a_words(first, last, at=None):
+            ag_w[first] = gather("ag_w%d" % first, at, U32, wa_w[:].bitcast(U32), a_list, first * H, last * H, True)
 
-        def gather_a_scales(first, last, tag=None):
-            for f in range(first, last, HALF):
-                ag_s[f] = gather("ag_s%d" % f, tag, U8, wa_s[:], a_list, f * H, (f + HALF) * H)
+        def gather_a_scales(first, last, at=None):
+            ag_s[first] = gather("ag_s%d" % first, at, U8, wa_s[:], a_list, first * H, last * H)
 
-        def gather_b_words(first, last, tag=None):
-            bg_w[first] = gather("bg_w%d" % first, tag, U32, wb_w[:].bitcast(U32), b_list, first * N, last * N)
+        def gather_b_words(first, last, at=None):
+            bg_w[first] = gather("bg_w%d" % first, at, U32, wb_w[:].bitcast(U32), b_list, first * N, last * N, True)
 
-        def gather_b_scales(first, last, tag=None):
-            bg_s[first] = gather("bg_s%d" % first, tag, U8, wb_s[:], b_list, first * N, last * N)
+        def gather_b_scales(first, last, at=None):
+            bg_s[first] = gather("bg_s%d" % first, at, U8, wb_s[:], b_list, first * N, last * N)
 
-        def first_layer(m, number):
+        def product(number, words, scales, moving_words, moving_scales):
+            acc = bank(number, [P, 4, P])
+            for t in range(4):
+                cols = slice(t * P, (t + 1) * P)
+                nc.tensor.matmul_mx(
+                    out=acc[:, t, :], lhsT=words[:, cols].bitcast(FP8X4), lhsT_scale=scales[:, cols],
+                    rhs=moving_words.bitcast(FP8X4), rhs_scale=moving_scales, start=True, stop=True,
+                )
+            return acc
+
+        def first_layer(m, number, group, count):
             slots = slice(m * P, (m + 1) * P)
-            acc = bank(number, [P, H])
-            nc.tensor.matmul_mx(
-                out=acc[:], lhsT=xg_w[:, slots].bitcast(FP8X4), lhsT_scale=xg_s[:, slots],
-                rhs=columns(ag_w, m, H).bitcast(FP8X4), rhs_scale=columns(ag_s, m, H)[A_ROW:, :],
-                start=True, stop=True,
-            )
-            h_rows[m] = sbuf([P, H], BF16, "h_rows%d" % m)
+            acc = product(number, columns(ag_w, m, H), columns(ag_s, m, H), xg_w[:, slots], xg_s[:, slots])
+            if group not in h_in:
+                h_in[group] = sbuf([P, count * 4 * P], BF16, "h_in%d" % group)
             nc.scalar.activation(
-                h_rows[m][:].rearrange("j (u p e) -> j u p e", u=2, e=2),
-                acc[:].rearrange("j (p u e) -> j u p e", u=2, e=2),
-                ACT.Gelu_apprx_tanh,
+                h_in[group][:, (m - group) * 4 * P : (m - group + 1) * 4 * P].rearrange("p (j t) -> p j t", t=4),
+                acc[:].rearrange("p t j -> p j t"), ACT.Gelu_apprx_tanh,
             )
 
-        def turn_h(first, last, number):
-            count = last - first
-            turned = bank(number, [P, count, 2, P])
-            for m in range(first, last):
-                for u in range(2):
-                    nc.tensor.transpose(
-                        turned[:, m - first, u, :], h_rows[m][:].bitcast(F32)[:, u * P : (u + 1) * P], ident[:]
-                    )
-            pair = first - first % HALF
-            if pair not in h_in:
-                h_in[pair] = sbuf([P, 4 * HALF * P], BF16, "h_in%d" % pair)
-            nc.scalar.copy(
-                h_in[pair][:, (first - pair) * 4 * P : (last - pair) * 4 * P]
-                .bitcast(F32).rearrange("p (s j u) -> p s j u", s=count, u=2),
-                turned[:].rearrange("p s u j -> p s j u"),
-            )
-
-        def quantise_h(first, last, tag=None):
-            h_w[first] = sbuf([P, (last - first) * P], U32, "h_w%d" % first)
-            h_s[first] = sbuf([P, (last - first) * P], U8, "h_s%d" % first, tag)
+        def quantise_h(first, last, words_at=None, scales_at=None):
+            h_w[first] = sbuf([P, (last - first) * P], U32, "h_w%d" % first, words_at)
+            h_s[first] = sbuf([P, (last - first) * P], U8, "h_s%d" % first, scales_at)
             nc.vector.quantize_mx(out=h_w[first][:].bitcast(FP8X4), scales=h_s[first][:], in_=h_in[first][:])
 
-        def second_layer(m, number):
-            acc = bank(number, [P, N])
-            nc.tensor.matmul_mx(
-                out=acc[:], lhsT=columns(h_w, m, P).bitcast(FP8X4), lhsT_scale=columns(h_s, m, P),
-                rhs=columns(bg_w, m, N).bitcast(FP8X4), rhs_scale=columns(bg_s, m, N)[B_ROW:, :],
-                start=True, stop=True,
+        def second_layer(m, number, group, count):
+            acc = product(number, columns(bg_w, m, N), columns(bg_s, m, N), columns(h_w, m, P), columns(h_s, m, P))
+            if group not in y:
+                y[group] = sbuf([P, 4, count * P], F32, "y%d" % group)
+            factor = gate_b[:, (m - 1) * P : m * P] if m else gate_a[:, :P]
+            nc.vector.tensor_tensor(
+                y[group][:, :, (m - group) * P : (m - group + 1) * P], acc[:],
+                factor.unsqueeze(1).to_broadcast([P, 4, P]), MULT,
             )
-            y_rows[m] = sbuf([P, 4, P], F32, "y_rows%d" % m)
-            sums = acc[:].rearrange("j (p t) -> j t p", t=4)
-            factor = gate_col[:, m % HALF, m // HALF : m // HALF + 1]
-            nc.scalar.activation(y_rows[m][:], sums, ACT.Copy, scale=factor)
 
-        def turn_y(m, number):
-            turned = bank(number, [P, 4, P])
-            for t in range(4):
-                nc.tensor.transpose(turned[:, t, :], y_rows[m][:, t, :], ident[:])
-            nc.scalar.copy(y[:, :, m * P : (m + 1) * P], turned[:])
-
-        def scatter(engine, t, first, last, tag=None):
+        def scatter(engine, t, first, last):
             if t not in placed:
-                placed[t] = sbuf([P, T], F32, "placed%d" % t, tag)
+                placed[t] = sbuf([P, T], F32, "placed%d" % t)
             window = placed[t][:].indirect(tok_list[:, first * P // PER_COL : last * P // PER_COL])
-            values = y[:, t, first * P : last * P]
+            group = max(f for f in y if f <= first)
+            values = y[group][:, t, (first - group) * P : (last - group) * P]
             if engine == "vector":
                 nc.vector.tensor_copy(window, values)
             else:
                 nc.scalar.activation(window, values, ACT.Copy)
 
         xg_w = gather("xg_w", None, U32, x_w[:].bitcast(U32), tok_list, 0, T)
-        early = 9216
-        gather_a_scales(0, 3)
         xg_s = gather("xg_s", None, U8, x_s[:], tok_list, 0, T)
-        gather_a_words(0, 1, early + 1472)
+        gather_a_scales(0, 3)
+        gather_a_scales(3, 6)
+        gather_a_words(0, 1, ag0_at)
         gather_a_words(1, 3)
-        first_layer(0, 0)
-        gather_a_scales(3, 6, early)
-        gather_a_words(3, 4, early + 1536 + 4096)
-        gather_a_words(4, 6, early + 1536)
-        turn_h(0, 1, 2)
-        first_layer(1, 1)
-        first_layer(2, 3)
-        turn_h(1, 3, 4)
-        first_layer(3, 2)
-        first_layer(4, 4)
-        first_layer(5, 2)
-        turn_h(3, 4, 5)
-        turn_h(4, 6, 3)
-
-        gate_turned = bank(6, [P, HALF, P])
-        for i in range(HALF):
-            nc.tensor.transpose(gate_turned[:, i, :], gate_rows[:, i * P : (i + 1) * P], ident[:])
-        nc.scalar.copy(gate_col[:], gate_turned[:, :, :2])
-
-        held = HALF * N * 4 - 64
+        gather_a_words(3, 4)
+        gather_a_words(4, 6)
+        h_in[HALF] = sbuf([P, HALF * 4 * P], BF16, "h_in3", h_at)
+        for m in range(B):
+            first_layer(m, m, m - m % HALF, HALF)
+        gather_b_scales(0, 1, ag0_at)
         quantise_h(0, 3)
-        gather_b_scales(0, 3)
-        gather_b_words(0, 1, held)
-        gather_b_words(1, 3)
-        second_layer(0, 7)
-        gather_b_scales(3, 6, held + 1088)
-        quantise_h(3, 6, held + 64)
-        gather_b_words(3, 6, 0)
-        wd_s = sbuf([P, N], U8, "wd_s", held + 576)
-        nc.vector.tensor_copy(wd_s[:].rearrange("k (t p) -> k p t", t=4), w_s[:].rearrange("k (p t) -> k p t", t=4))
-        second_layer(1, 1)
-        turn_y(0, 6)
-        second_layer(2, 0)
-        turn_y(1, 7)
-        turn_y(2, 2)
-        wd_w = sbuf([P, N], U16, "wd_w", "y_rows2")
+        wd_s = sbuf([P, N], U8, "wd_s")
+        nc.gpsimd.tensor_copy(wd_s[:].rearrange("k (t p) -> k p t", t=4), w_s[:].rearrange("k (p t) -> k p t", t=4))
+        gather_b_words(0, 1)
+        gather_b_words(1, 2, bg1_at)
+        second_layer(0, 6, 0, 1)
+        gather_b_scales(1, 3, gate_at + LAP)
+        quantise_h(3, 6, None, gate_at + LAP + 2 * N)
+        wd_w = sbuf([P, N], U16, "wd_w", h_at)
         nc.scalar.copy(
             wd_w[:].rearrange("k (t p) -> k t p", t=4), w_w[:].bitcast(U16).rearrange("k (p t) -> k t p", t=4)
         )
-        scatter("scalar", 2, 0, 2)
-        second_layer(3, 7)
-        second_layer(4, 2)
-        turn_y(3, 1)
-        second_layer(5, 7)
-        turn_y(4, 3)
-        turn_y(5, 4)
-        for first in (0, 2, 4):
-            scatter("vector", 0, first, first + 2)
-            scatter("vector", 1, first, first + 2)
-        scatter("scalar", 2, 2, 4)
-        scatter("scalar", 2, 4, 6)
-        scatter("scalar", 3, 0, 3, "y_rows5")
-        scatter("scalar", 3, 3, 6)
+        gather_b_words(2, 3, bg2_at)
+        second_layer(1, 7, 1, 1)
+        gather_b_words(3, 4, bg3_at)
+        second_layer(2, 6, 2, 4)
+        gather_b_scales(3, 6, bg2_at + LAP)
+        gather_b_words(4, 6, bg4_at)
+        for m, number in ((3, 7), (4, 6), (5, 7)):
+            second_layer(m, number, 2, 4)
+        for m in range(2):
+            for t in range(4):
+                scatter("scalar", t, m, m + 1)
+        for t in range(1, 4):
+            scatter("scalar", t, 2, 3)
+        scatter("vector", 0, 2, B)
+        scatter("scalar", 1, HALF, 5)
+        scatter("scalar", 1, 5, B)
+        scatter("scalar", 2, HALF, B)
+        scatter("scalar", 3, HALF, B)
 
-        wide_banks = (5, 6, 2, 7)
-        rest = {0: bank(0, [P, 2, T - BANK]), 1: bank(1, [P, 2, T - BANK])}
+        wide_banks = (0, 1, 2, 3)
+        rest = {0: bank(4, [P, 2, T - BANK]), 1: bank(5, [P, 2, T - BANK])}
         rest_of = [rest[t // 2][:, t % 2, :] for t in range(4)]
         wide = {}
         for t in range(4):
@@ -277,9 +261,7 @@ def tile_moe_dyl_gelu_kernel(
             add(t, 0, BANK)
             add(t, BANK, T)
             nc.sync.dma_start(out=out_rows[:, t, :], in_=result[t // 2][:, t % 2, :])
-        for c in (0, 1):
-            nc.scalar.copy(*pair_views(0, c))
-        for c in (2, 3):
+        for c in range(4):
             nc.vector.tensor_copy(*pair_views(0, c))
         for c in (1, 2, 0, 3):
             add(3, *CHUNKS[c])

@@ -197,26 +197,26 @@ def tile_moe_dyl_gelu_kernel(
         gather_a_words(1, 3)
         gather_a_words(3, 4)
         gather_a_words(4, 6)
-        h_in[HALF] = sbuf([P, HALF * 4 * P], BF16, "h_in3", h_at)
+        h_in[0] = sbuf([P, HALF * 4 * P], BF16, "h_in0", h_at)
         for m in range(B):
             first_layer(m, m, m - m % HALF, HALF)
         gather_b_scales(0, 1, ag0_at)
         quantise_h(0, 3)
-        wd_s = sbuf([P, N], U8, "wd_s")
-        nc.gpsimd.tensor_copy(wd_s[:].rearrange("k (t p) -> k p t", t=4), w_s[:].rearrange("k (p t) -> k p t", t=4))
+        wd_w = sbuf([P, N], U16, "wd_w", h_at)
+        nc.scalar.copy(
+            wd_w[:].rearrange("k (t p) -> k t p", t=4), w_w[:].bitcast(U16).rearrange("k (p t) -> k t p", t=4)
+        )
         gather_b_words(0, 1)
         gather_b_words(1, 2, bg1_at)
         second_layer(0, 6, 0, 1)
         gather_b_scales(1, 3, gate_at + LAP)
         quantise_h(3, 6, None, gate_at + LAP + 2 * N)
-        wd_w = sbuf([P, N], U16, "wd_w", h_at)
-        nc.scalar.copy(
-            wd_w[:].rearrange("k (t p) -> k t p", t=4), w_w[:].bitcast(U16).rearrange("k (p t) -> k t p", t=4)
-        )
         gather_b_words(2, 3, bg2_at)
         second_layer(1, 7, 1, 1)
         gather_b_words(3, 4, bg3_at)
         second_layer(2, 6, 2, 4)
+        wd_s = sbuf([P, N], U8, "wd_s", bg1_at)
+        nc.vector.tensor_copy(wd_s[:].rearrange("k (t p) -> k p t", t=4), w_s[:].rearrange("k (p t) -> k p t", t=4))
         gather_b_scales(3, 6, bg2_at + LAP)
         gather_b_words(4, 6, bg4_at)
         for m, number in ((3, 7), (4, 6), (5, 7)):
@@ -257,24 +257,29 @@ def tile_moe_dyl_gelu_kernel(
             sums = wide[t][:, start:stop] if stop <= BANK else rest_of[t][:, start - BANK : stop - BANK]
             nc.vector.tensor_tensor(result[t // 2][:, t % 2, start:stop], sums, placed[t][:, start:stop], ADD)
 
-        for t in range(3):
+        def add_plane(t):
             add(t, 0, BANK)
             add(t, BANK, T)
             nc.sync.dma_start(out=out_rows[:, t, :], in_=result[t // 2][:, t % 2, :])
-        for c in range(4):
+
+        add_plane(0)
+        add_plane(1)
+        for c in (0, 1):
             nc.vector.tensor_copy(*pair_views(0, c))
-        for c in (1, 2, 0, 3):
+        for c in (2, 3):
+            nc.scalar.copy(*pair_views(0, c))
+        add_plane(2)
+        for c in (3, 0, 1, 2):
             add(3, *CHUNKS[c])
         nc.sync.dma_start(out=out_rows[:, 3, :], in_=result[1][:, 1, :])
-        for c in (1, 2):
-            nc.scalar.copy(*pair_views(1, c))
-        for c in (0, 3):
+        nc.scalar.copy(*pair_views(1, 3))
+        for c in (0, 1, 2):
             nc.vector.tensor_copy(*pair_views(1, c))
 
         out_w = sbuf([P, T], U32, "out_w")
         out_s = sbuf([P, T], U8, "out_s")
         word_rows = out_1[0].rearrange("p c d -> p (c d)").bitcast(I32)
-        for c in (0, 3, 1, 2):
+        for c in range(len(CHUNKS)):
             toks = slice(*CHUNKS[c])
             nc.vector.quantize_mx(
                 out=out_w[:, toks].bitcast(FP8X4), scales=out_s[:, toks],

@@ -50,7 +50,8 @@ def tile_moe_dyl_gelu_kernel(
         bg4_at = 0
         bg2_at = bg4_at + 2 * words - LAP
         gate_at = bg2_at + words - LAP
-        bg1_at = gate_at + 3 * 4 * P
+        bg0_at = gate_at + 4 * P
+        bg1_at = bg0_at + words
         bg3_at = bg1_at + words - LAP
         h_at = bg3_at + words
         ag0_at = h_at + HALF * 2 * H
@@ -67,7 +68,7 @@ def tile_moe_dyl_gelu_kernel(
         wa_s = sbuf([P, POOL], U8, "wa_s")
         wb_w = sbuf([P, POOL], I32, "wb_w")
         wb_s = sbuf([P, POOL], U8, "wb_s")
-        gate_a = sbuf([P, 3 * P], F32, "gate_a", gate_at)
+        gate_a = sbuf([P, P], F32, "gate_a", gate_at)
         gate_b = sbuf([P, T - P], F32, "gate_b")
 
         def load_words(tile, words, start, stop):
@@ -84,16 +85,16 @@ def tile_moe_dyl_gelu_kernel(
             nc.sync.dma_start(out=raw[:].bitcast(I32), in_=scales[0].bitcast(I32).rearrange("b (e c) -> (b e) c", e=E))
             return raw
 
-        def deal_scales(name, raw):
-            dealt = sbuf([P, H], U8, name)
+        def deal_scales(name, raw, at=None):
+            dealt = sbuf([P, H], U8, name, at)
             nc.vector.tensor_copy(
                 dealt[:].rearrange("k (t m) -> k m t", t=4), raw[:].rearrange("k (m t) -> k m t", t=4)
             )
             return dealt
 
-        def move_scales(dealt, table):
+        def move_scales(queue, dealt, table):
             for q in (0, 2, 1, 3):
-                nc.sync.dma_start(
+                queue.dma_start(
                     out=table[:].bitcast(I32)[32 * q : 32 * q + 4, :], in_=dealt[:].bitcast(I32)[32 * q : 32 * q + 32, :]
                 )
 
@@ -110,13 +111,13 @@ def tile_moe_dyl_gelu_kernel(
         load_words(wa_w, wa_words, 0, POOL // 4)
         nc.sync.dma_start(a_list[:], offs2)
         nc.sync.dma_start(b_list[:], offs3)
-        move_scales(deal_scales("a_dealt", a_raw), wa_s)
+        move_scales(nc.sync, deal_scales("a_dealt", a_raw), wa_s)
         load_words(wa_w, wa_words, POOL // 4, POOL)
-        move_scales(deal_scales("b_dealt", b_raw), wb_s)
+        move_scales(nc.gpsimd, deal_scales("b_dealt", b_raw, bg1_at - H // 2), wb_s)
         nc.sync.dma_start(out=gate_a[:, :P], in_=gate[:, :P])
         load_words(wb_w, wb_words, 0, POOL)
-        nc.sync.dma_start(out=w_w[:].bitcast(I32), in_=w_words[0].bitcast(I32))
         nc.sync.dma_start(out=gate_b[:], in_=gate[:, P:])
+        nc.sync.dma_start(out=w_w[:].bitcast(I32), in_=w_words[0].bitcast(I32))
         load_scales(w_s[:], w_scales)
 
         def gather(name, at, dtype, window, offsets, start, stop, dealt=False):
@@ -200,17 +201,16 @@ def tile_moe_dyl_gelu_kernel(
         h_in[0] = sbuf([P, HALF * 4 * P], BF16, "h_in0", h_at)
         for m in range(B):
             first_layer(m, m, m - m % HALF, HALF)
-        gather_b_scales(0, 1, ag0_at)
         quantise_h(0, 3)
+        gather_b_scales(0, 3, ag0_at)
         wd_w = sbuf([P, N], U16, "wd_w", h_at)
         nc.scalar.copy(
             wd_w[:].rearrange("k (t p) -> k t p", t=4), w_w[:].bitcast(U16).rearrange("k (p t) -> k t p", t=4)
         )
-        gather_b_words(0, 1)
+        gather_b_words(0, 1, bg0_at)
         gather_b_words(1, 2, bg1_at)
         second_layer(0, 6, 0, 1)
-        gather_b_scales(1, 3, gate_at + LAP)
-        quantise_h(3, 6, None, gate_at + LAP + 2 * N)
+        quantise_h(3, 6, None, gate_at + LAP)
         gather_b_words(2, 3, bg2_at)
         second_layer(1, 7, 1, 1)
         gather_b_words(3, 4, bg3_at)
@@ -227,10 +227,11 @@ def tile_moe_dyl_gelu_kernel(
         for t in range(1, 4):
             scatter("scalar", t, 2, 3)
         scatter("vector", 0, 2, B)
+        scatter("vector", 3, 5, B)
         scatter("scalar", 1, HALF, 5)
         scatter("scalar", 1, 5, B)
         scatter("scalar", 2, HALF, B)
-        scatter("scalar", 3, HALF, B)
+        scatter("scalar", 3, HALF, 5)
 
         wide_banks = (0, 1, 2, 3)
         rest = {0: bank(4, [P, 2, T - BANK]), 1: bank(5, [P, 2, T - BANK])}

@@ -48,12 +48,12 @@ def tile_moe_dyl_gelu_kernel(
 
         words = 4 * N
         bg4_at = 0
-        bg2_at = bg4_at + 2 * words - LAP
+        bg2_at = bg4_at + words - LAP
         gate_at = bg2_at + words - LAP
-        bg0_at = gate_at + 4 * P
-        bg1_at = bg0_at + words
+        bg1_at = gate_at + 3 * 4 * P
         bg3_at = bg1_at + words - LAP
-        h_at = bg3_at + words
+        bg5_at = bg3_at + words - LAP
+        h_at = bg5_at + words
         ag0_at = h_at + HALF * 2 * H
 
         tok_list = lists.tile([P, T // PER_COL], U16, name="tok_list")
@@ -68,7 +68,7 @@ def tile_moe_dyl_gelu_kernel(
         wa_s = sbuf([P, POOL], U8, "wa_s")
         wb_w = sbuf([P, POOL], I32, "wb_w")
         wb_s = sbuf([P, POOL], U8, "wb_s")
-        gate_a = sbuf([P, P], F32, "gate_a", gate_at)
+        gate_a = sbuf([P, 3 * P], F32, "gate_a", gate_at)
         gate_b = sbuf([P, T - P], F32, "gate_b")
 
         def load_words(tile, words, start, stop):
@@ -85,16 +85,16 @@ def tile_moe_dyl_gelu_kernel(
             nc.sync.dma_start(out=raw[:].bitcast(I32), in_=scales[0].bitcast(I32).rearrange("b (e c) -> (b e) c", e=E))
             return raw
 
-        def deal_scales(name, raw, at=None):
-            dealt = sbuf([P, H], U8, name, at)
+        def deal_scales(name, raw):
+            dealt = sbuf([P, H], U8, name)
             nc.vector.tensor_copy(
                 dealt[:].rearrange("k (t m) -> k m t", t=4), raw[:].rearrange("k (m t) -> k m t", t=4)
             )
             return dealt
 
-        def move_scales(queue, dealt, table):
+        def move_scales(dealt, table):
             for q in (0, 2, 1, 3):
-                queue.dma_start(
+                nc.sync.dma_start(
                     out=table[:].bitcast(I32)[32 * q : 32 * q + 4, :], in_=dealt[:].bitcast(I32)[32 * q : 32 * q + 32, :]
                 )
 
@@ -111,9 +111,9 @@ def tile_moe_dyl_gelu_kernel(
         load_words(wa_w, wa_words, 0, POOL // 4)
         nc.sync.dma_start(a_list[:], offs2)
         nc.sync.dma_start(b_list[:], offs3)
-        move_scales(nc.sync, deal_scales("a_dealt", a_raw), wa_s)
+        move_scales(deal_scales("a_dealt", a_raw), wa_s)
         load_words(wa_w, wa_words, POOL // 4, POOL)
-        move_scales(nc.gpsimd, deal_scales("b_dealt", b_raw, bg1_at - H // 2), wb_s)
+        move_scales(deal_scales("b_dealt", b_raw), wb_s)
         nc.sync.dma_start(out=gate_a[:, :P], in_=gate[:, :P])
         load_words(wb_w, wb_words, 0, POOL)
         nc.sync.dma_start(out=gate_b[:], in_=gate[:, P:])
@@ -144,19 +144,19 @@ def tile_moe_dyl_gelu_kernel(
         def gather_b_scales(first, last, at=None):
             bg_s[first] = gather("bg_s%d" % first, at, U8, wb_s[:], b_list, first * N, last * N)
 
-        def product(number, words, scales, moving_words, moving_scales):
-            acc = bank(number, [P, 4, P])
-            for t in range(4):
+        def product(number, planes, words, scales, moving_words, moving_scales):
+            acc = bank(number, [P, len(planes), P])
+            for t in planes:
                 cols = slice(t * P, (t + 1) * P)
                 nc.tensor.matmul_mx(
-                    out=acc[:, t, :], lhsT=words[:, cols].bitcast(FP8X4), lhsT_scale=scales[:, cols],
+                    out=acc[:, t - planes.start, :], lhsT=words[:, cols].bitcast(FP8X4), lhsT_scale=scales[:, cols],
                     rhs=moving_words.bitcast(FP8X4), rhs_scale=moving_scales, start=True, stop=True,
                 )
             return acc
 
         def first_layer(m, number, group, count):
             slots = slice(m * P, (m + 1) * P)
-            acc = product(number, columns(ag_w, m, H), columns(ag_s, m, H), xg_w[:, slots], xg_s[:, slots])
+            acc = product(number, range(4), columns(ag_w, m, H), columns(ag_s, m, H), xg_w[:, slots], xg_s[:, slots])
             if group not in h_in:
                 h_in[group] = sbuf([P, count * 4 * P], BF16, "h_in%d" % group)
             nc.scalar.activation(
@@ -169,14 +169,16 @@ def tile_moe_dyl_gelu_kernel(
             h_s[first] = sbuf([P, (last - first) * P], U8, "h_s%d" % first, scales_at)
             nc.vector.quantize_mx(out=h_w[first][:].bitcast(FP8X4), scales=h_s[first][:], in_=h_in[first][:])
 
-        def second_layer(m, number, group, count):
-            acc = product(number, columns(bg_w, m, N), columns(bg_s, m, N), columns(h_w, m, P), columns(h_s, m, P))
+        def second_layer(m, number, group, count, planes=range(4)):
+            acc = product(
+                number, planes, columns(bg_w, m, N), columns(bg_s, m, N), columns(h_w, m, P), columns(h_s, m, P)
+            )
             if group not in y:
                 y[group] = sbuf([P, 4, count * P], F32, "y%d" % group)
             factor = gate_b[:, (m - 1) * P : m * P] if m else gate_a[:, :P]
             nc.vector.tensor_tensor(
-                y[group][:, :, (m - group) * P : (m - group + 1) * P], acc[:],
-                factor.unsqueeze(1).to_broadcast([P, 4, P]), MULT,
+                y[group][:, planes.start : planes.stop, (m - group) * P : (m - group + 1) * P], acc[:],
+                factor.unsqueeze(1).to_broadcast([P, len(planes), P]), MULT,
             )
 
         def scatter(engine, t, first, last):
@@ -201,37 +203,40 @@ def tile_moe_dyl_gelu_kernel(
         h_in[0] = sbuf([P, HALF * 4 * P], BF16, "h_in0", h_at)
         for m in range(B):
             first_layer(m, m, m - m % HALF, HALF)
+        gather_b_scales(0, 1, ag0_at)
         quantise_h(0, 3)
-        gather_b_scales(0, 3, ag0_at)
         wd_w = sbuf([P, N], U16, "wd_w", h_at)
         nc.scalar.copy(
             wd_w[:].rearrange("k (t p) -> k t p", t=4), w_w[:].bitcast(U16).rearrange("k (p t) -> k t p", t=4)
         )
-        gather_b_words(0, 1, bg0_at)
+        gather_b_words(0, 1)
         gather_b_words(1, 2, bg1_at)
-        second_layer(0, 6, 0, 1)
-        quantise_h(3, 6, None, gate_at + LAP)
+        second_layer(0, 6, 0, 1, range(0, 2))
+        second_layer(0, 7, 0, 1, range(2, 4))
+        gather_b_scales(1, 3, gate_at + LAP)
+        quantise_h(3, 6, None, gate_at + LAP + 2 * N)
         gather_b_words(2, 3, bg2_at)
-        second_layer(1, 7, 1, 1)
+        second_layer(1, 0, 1, 1)
         gather_b_words(3, 4, bg3_at)
-        second_layer(2, 6, 2, 4)
-        wd_s = sbuf([P, N], U8, "wd_s", bg1_at)
-        nc.vector.tensor_copy(wd_s[:].rearrange("k (t p) -> k p t", t=4), w_s[:].rearrange("k (p t) -> k p t", t=4))
+        second_layer(2, 6, 2, 1)
+        wd_s = sbuf([P, N], U8, "wd_s")
+        nc.gpsimd.tensor_copy(wd_s[:].rearrange("k (t p) -> k p t", t=4), w_s[:].rearrange("k (p t) -> k p t", t=4))
         gather_b_scales(3, 6, bg2_at + LAP)
-        gather_b_words(4, 6, bg4_at)
-        for m, number in ((3, 7), (4, 6), (5, 7)):
-            second_layer(m, number, 2, 4)
-        for m in range(2):
+        gather_b_words(4, 5, bg4_at)
+        second_layer(3, 7, HALF, HALF)
+        gather_b_words(5, 6, bg5_at)
+        second_layer(4, 6, HALF, HALF)
+        second_layer(5, 7, HALF, HALF)
+        for m in range(HALF):
             for t in range(4):
                 scatter("scalar", t, m, m + 1)
-        for t in range(1, 4):
-            scatter("scalar", t, 2, 3)
-        scatter("vector", 0, 2, B)
-        scatter("vector", 3, 5, B)
-        scatter("scalar", 1, HALF, 5)
-        scatter("scalar", 1, 5, B)
-        scatter("scalar", 2, HALF, B)
-        scatter("scalar", 3, HALF, 5)
+        for t in (0, 1):
+            scatter("vector", t, 3, 4)
+        for t in (2, 3):
+            scatter("scalar", t, 3, 4)
+        scatter("vector", 0, 4, B)
+        for t in (1, 2, 3):
+            scatter("scalar", t, 4, B)
 
         wide_banks = (0, 1, 2, 3)
         rest = {0: bank(4, [P, 2, T - BANK]), 1: bank(5, [P, 2, T - BANK])}
@@ -246,41 +251,37 @@ def tile_moe_dyl_gelu_kernel(
                     rhs=x_w[:, toks].bitcast(FP8X4), rhs_scale=x_s[:, toks], start=True, stop=True,
                 )
 
-        result = [sbuf([P, 2, T], F32, "result%d" % u) for u in range(2)]
+        result = sbuf([P, 4, T], F32, "result")
         out_rows = out_0.rearrange("(p t) c -> p t c", t=4)
         out_in = [sbuf([P, stop - start, 4], BF16, "out_in%d" % start) for start, stop in CHUNKS]
 
-        def pair_views(u, c):
+        def rounding(c):
             toks = slice(*CHUNKS[c])
-            return out_in[c][:, :, 2 * u : 2 * u + 2], result[u][:, :, toks].rearrange("p e j -> p j e")
+            return (
+                out_in[c][:].rearrange("p (g i) t -> p g t i", i=4),
+                result[:, :, toks].rearrange("p t (g i) -> p g t i", i=4),
+            )
 
         def add(t, start, stop):
             sums = wide[t][:, start:stop] if stop <= BANK else rest_of[t][:, start - BANK : stop - BANK]
-            nc.vector.tensor_tensor(result[t // 2][:, t % 2, start:stop], sums, placed[t][:, start:stop], ADD)
+            nc.vector.tensor_tensor(result[:, t, start:stop], sums, placed[t][:, start:stop], ADD)
 
-        def add_plane(t):
+        for t in range(3):
             add(t, 0, BANK)
             add(t, BANK, T)
-            nc.sync.dma_start(out=out_rows[:, t, :], in_=result[t // 2][:, t % 2, :])
-
-        add_plane(0)
-        add_plane(1)
-        for c in (0, 1):
-            nc.vector.tensor_copy(*pair_views(0, c))
-        for c in (2, 3):
-            nc.scalar.copy(*pair_views(0, c))
-        add_plane(2)
-        for c in (3, 0, 1, 2):
+            nc.sync.dma_start(out=out_rows[:, t, :], in_=result[:, t, :])
+        for c in (1, 2, 0, 3):
             add(3, *CHUNKS[c])
-        nc.sync.dma_start(out=out_rows[:, 3, :], in_=result[1][:, 1, :])
-        nc.scalar.copy(*pair_views(1, 3))
-        for c in (0, 1, 2):
-            nc.vector.tensor_copy(*pair_views(1, c))
+        nc.sync.dma_start(out=out_rows[:, 3, :], in_=result[:, 3, :])
+        for c in (1, 2):
+            nc.scalar.copy(*rounding(c))
+        for c in (0, 3):
+            nc.vector.tensor_copy(*rounding(c))
 
         out_w = sbuf([P, T], U32, "out_w")
         out_s = sbuf([P, T], U8, "out_s")
         word_rows = out_1[0].rearrange("p c d -> p (c d)").bitcast(I32)
-        for c in range(len(CHUNKS)):
+        for c in (0, 3, 1, 2):
             toks = slice(*CHUNKS[c])
             nc.vector.quantize_mx(
                 out=out_w[:, toks].bitcast(FP8X4), scales=out_s[:, toks],

@@ -68,7 +68,7 @@ def tile_moe_dyl_gelu_kernel(
         wa_s = sbuf([P, POOL], U8, "wa_s")
         wb_w = sbuf([P, POOL], I32, "wb_w")
         wb_s = sbuf([P, POOL], U8, "wb_s")
-        gate_a = sbuf([P, 3 * P], F32, "gate_a", gate_at)
+        gate_a = sbuf([P, P], F32, "gate_a", gate_at)
         gate_b = sbuf([P, T - P], F32, "gate_b")
 
         def load_words(tile, words, start, stop):
@@ -114,7 +114,7 @@ def tile_moe_dyl_gelu_kernel(
         move_scales(deal_scales("a_dealt", a_raw), wa_s)
         load_words(wa_w, wa_words, POOL // 4, POOL)
         move_scales(deal_scales("b_dealt", b_raw), wb_s)
-        nc.sync.dma_start(out=gate_a[:, :P], in_=gate[:, :P])
+        nc.sync.dma_start(out=gate_a[:], in_=gate[:, :P])
         load_words(wb_w, wb_words, 0, POOL)
         nc.sync.dma_start(out=gate_b[:], in_=gate[:, P:])
         nc.sync.dma_start(out=w_w[:].bitcast(I32), in_=w_words[0].bitcast(I32))
@@ -160,8 +160,8 @@ def tile_moe_dyl_gelu_kernel(
             if group not in h_in:
                 h_in[group] = sbuf([P, count * 4 * P], BF16, "h_in%d" % group)
             nc.scalar.activation(
-                h_in[group][:, (m - group) * 4 * P : (m - group + 1) * 4 * P].rearrange("p (j t) -> p j t", t=4),
-                acc[:].rearrange("p t j -> p j t"), ACT.Gelu_apprx_tanh,
+                h_in[group][:, (m - group) * 4 * P : (m - group + 1) * 4 * P].rearrange("p (g i t) -> p g t i", i=4, t=4),
+                acc[:].rearrange("p t (g i) -> p g t i", i=4), ACT.Gelu_apprx_tanh,
             )
 
         def quantise_h(first, last, words_at=None, scales_at=None):
@@ -175,7 +175,7 @@ def tile_moe_dyl_gelu_kernel(
             )
             if group not in y:
                 y[group] = sbuf([P, 4, count * P], F32, "y%d" % group)
-            factor = gate_b[:, (m - 1) * P : m * P] if m else gate_a[:, :P]
+            factor = gate_b[:, (m - 1) * P : m * P] if m else gate_a[:]
             nc.vector.tensor_tensor(
                 y[group][:, planes.start : planes.stop, (m - group) * P : (m - group + 1) * P], acc[:],
                 factor.unsqueeze(1).to_broadcast([P, len(planes), P]), MULT,
@@ -205,22 +205,22 @@ def tile_moe_dyl_gelu_kernel(
             first_layer(m, m, m - m % HALF, HALF)
         gather_b_scales(0, 1, ag0_at)
         quantise_h(0, 3)
-        wd_w = sbuf([P, N], U16, "wd_w", h_at)
-        nc.scalar.copy(
-            wd_w[:].rearrange("k (t p) -> k t p", t=4), w_w[:].bitcast(U16).rearrange("k (p t) -> k t p", t=4)
+        wd_w = sbuf([P, 2 * N], U8, "wd_w", h_at)
+        nc.gpsimd.tensor_copy(
+            wd_w[:].rearrange("k (t p d) -> k t p d", t=4, d=2), w_w[:].rearrange("k (p t d) -> k t p d", t=4, d=2)
         )
+        wd_s = sbuf([P, N], U8, "wd_s", h_at + 2 * N)
+        nc.gpsimd.tensor_copy(wd_s[:].rearrange("k (t p) -> k t p", t=4), w_s[:].rearrange("k (p t) -> k t p", t=4))
         gather_b_words(0, 1)
         gather_b_words(1, 2, bg1_at)
         second_layer(0, 6, 0, 1, range(0, 2))
         second_layer(0, 7, 0, 1, range(2, 4))
-        gather_b_scales(1, 3, gate_at + LAP)
-        quantise_h(3, 6, None, gate_at + LAP + 2 * N)
+        gather_b_scales(1, 3, gate_at + 4 * P - LAP)
+        quantise_h(3, 6, None, gate_at + LAP)
         gather_b_words(2, 3, bg2_at)
         second_layer(1, 0, 1, 1)
         gather_b_words(3, 4, bg3_at)
         second_layer(2, 6, 2, 1)
-        wd_s = sbuf([P, N], U8, "wd_s")
-        nc.gpsimd.tensor_copy(wd_s[:].rearrange("k (t p) -> k p t", t=4), w_s[:].rearrange("k (p t) -> k p t", t=4))
         gather_b_scales(3, 6, bg2_at + LAP)
         gather_b_words(4, 5, bg4_at)
         second_layer(3, 7, HALF, HALF)
@@ -246,7 +246,7 @@ def tile_moe_dyl_gelu_kernel(
             wide[t] = bank(wide_banks[t], [P, BANK])
             for out, toks in ((wide[t][:], slice(0, BANK)), (rest_of[t], slice(BANK, T))):
                 nc.tensor.matmul_mx(
-                    out=out, lhsT=wd_w[:, t * P : (t + 1) * P].bitcast(U8).bitcast(FP4X4),
+                    out=out, lhsT=wd_w[:, 2 * t * P : 2 * (t + 1) * P].bitcast(FP4X4),
                     lhsT_scale=wd_s[:, t * P : (t + 1) * P],
                     rhs=x_w[:, toks].bitcast(FP8X4), rhs_scale=x_s[:, toks], start=True, stop=True,
                 )

@@ -199,7 +199,8 @@ def tile_moe_dyl_gelu_kernel(
         gather_a_words(0, 1, ag0_at)
         gather_a_words(1, 3)
         gather_a_words(3, 4)
-        gather_a_words(4, 6)
+        gather_a_words(4, 5)
+        gather_a_words(5, 6)
         h_in[0] = sbuf([P, HALF * 4 * P], BF16, "h_in0", h_at)
         for m in range(B):
             first_layer(m, m, m - m % HALF, HALF)
@@ -234,8 +235,10 @@ def tile_moe_dyl_gelu_kernel(
             scatter("vector", t, 3, 4)
         for t in (2, 3):
             scatter("scalar", t, 3, 4)
+        scatter("scalar", 1, 4, 5)
         scatter("vector", 0, 4, B)
-        for t in (1, 2, 3):
+        scatter("vector", 1, 5, B)
+        for t in (2, 3):
             scatter("scalar", t, 4, B)
 
         wide_banks = (0, 1, 2, 3)

from contextlib import ExitStack

import concourse.mybir as mybir

K, T, E, B, H, N = 512, 768, 8, 6, 512, 512
FLOPS = 2 * K * N * T + 2 * K * H * T + 2 * H * N * T

F32 = mybir.dt.float32
BF16 = mybir.dt.bfloat16
I32 = mybir.dt.int32
U32 = mybir.dt.uint32
U16 = mybir.dt.uint16
U8 = mybir.dt.uint8
FP8X4 = mybir.dt.float8_e4m3fn_x4
FP4X4 = mybir.dt.float4_e2m1fn_x4
ACT = mybir.ActivationFunctionType
ADD = mybir.AluOpType.add
MULT = mybir.AluOpType.mult

P = 128
POOL = E * H
PER_COL = 16
HALF = 3
WIDE = 1024
BANK = 512
CHUNKS = ((0, P), (P, 3 * P), (3 * P, 4 * P), (4 * P, 6 * P))
LAP = 64


def tile_moe_dyl_gelu_kernel(
    tc, x_words, x_scales, w_words, w_scales, wa_words, wa_scales, wb_words, wb_scales,
    gate, offs, offs2, offs3, out_0, out_1, out_2,
):
    nc = tc.nc
    with ExitStack() as ctx:
        lists = ctx.enter_context(tc.tile_pool(name="lists", bufs=1))
        keep = ctx.enter_context(tc.tile_pool(name="keep", bufs=1))
        reuse = ctx.enter_context(tc.tile_pool(name="reuse", bufs=1))
        psum = ctx.enter_context(tc.psum_pool(name="psum", bufs=1))

        def bank(number, shape):
            return psum.tile(shape, F32, name="bank%d" % number)

        def sbuf(shape, dtype, name, at=None):
            if at is not None:
                return reuse.tile(shape, dtype, name=name, offset=at, align_bytes=64)
            return keep.tile(shape, dtype, name=name, align_bytes=64)

        words = 4 * N
        bg4_at = 0
        bg2_at = bg4_at + words - LAP
        gate_at = bg2_at + words - LAP
        bg1_at = gate_at + 3 * 4 * P
        bg3_at = bg1_at + words - LAP
        bg5_at = bg3_at + words - LAP
        h_at = bg5_at + words
        ag0_at = h_at + HALF * 2 * H

        tok_list = lists.tile([P, T // PER_COL], U16, name="tok_list")
        a_list = lists.tile([P, B * H // PER_COL], U16, name="a_list")
        b_list = lists.tile([P, B * N // PER_COL], U16, name="b_list")

        x_w = sbuf([P, WIDE], I32, "x_w")
        x_s = sbuf([P, WIDE], U8, "x_s")
        w_w = sbuf([P, 2 * N], U8, "w_w")
        w_s = sbuf([P, N], U8, "w_s")
        wa_w = sbuf([P, POOL], I32, "wa_w")
        wa_s = sbuf([P, POOL], U8, "wa_s")
        wb_w = sbuf([P, POOL], I32, "wb_w")
        wb_s = sbuf([P, POOL], U8, "wb_s")
        gate_a = sbuf([P, P], F32, "gate_a", gate_at)
        gate_b = sbuf([P, T - P], F32, "gate_b")

        def load_words(tile, words, start, stop):
            rows = words[0].rearrange("p c d -> p (c d)").bitcast(I32)
            nc.sync.dma_start(out=tile[:, start:stop], in_=rows[:, start:stop])

        def load_scales(tile, scales):
            rows = scales[0].bitcast(I32).rearrange("(q r) c -> r q c", r=4)
            for r in range(4):
                nc.sync.dma_start(out=tile.bitcast(I32)[r:P:32, :], in_=rows[r])

        def load_spread(name, scales):
            raw = sbuf([P, H], U8, name)
            nc.sync.dma_start(out=raw[:].bitcast(I32), in_=scales[0].bitcast(I32).rearrange("b (e c) -> (b e) c", e=E))
            return raw

        def deal_scales(name, raw):
            dealt = sbuf([P, H], U8, name)
            nc.vector.tensor_copy(
                dealt[:].rearrange("k (t m) -> k m t", t=4), raw[:].rearrange("k (m t) -> k m t", t=4)
            )
            return dealt

        def move_scales(dealt, table):
            for q in (0, 2, 1, 3):
                nc.sync.dma_start(
                    out=table[:].bitcast(I32)[32 * q : 32 * q + 4, :], in_=dealt[:].bitcast(I32)[32 * q : 32 * q + 32, :]
                )

        nc.gpsimd.memset(x_s[:, :T].bitcast(I32), 0)
        nc.vector.memset(wa_s[:].bitcast(I32), 0)
        nc.gpsimd.memset(wb_s[:].bitcast(I32), 0)
        nc.gpsimd.memset(w_s[:].bitcast(I32), 0)

        a_raw = load_spread("a_raw", wa_scales)
        b_raw = load_spread("b_raw", wb_scales)
        load_words(x_w, x_words, 0, T)
        nc.sync.dma_start(tok_list[:], offs)
        load_scales(x_s[:, :T], x_scales)
        load_words(wa_w, wa_words, 0, POOL // 4)
        nc.sync.dma_start(a_list[:], offs2)
        nc.sync.dma_start(b_list[:], offs3)
        move_scales(deal_scales("a_dealt", a_raw), wa_s)
        load_words(wa_w, wa_words, POOL // 4, POOL)
        move_scales(deal_scales("b_dealt", b_raw), wb_s)
        nc.sync.dma_start(out=gate_a[:], in_=gate[:, :P])
        load_words(wb_w, wb_words, 0, POOL)
        nc.sync.dma_start(out=gate_b[:], in_=gate[:, P:])
        nc.sync.dma_start(out=w_w[:].bitcast(I32), in_=w_words[0].bitcast(I32))
        load_scales(w_s[:], w_scales)

        def gather(name, at, dtype, window, offsets, start, stop, dealt=False):
            dst = sbuf([P, stop - start], dtype, name, at)
            view = dst[:].rearrange("k (b t m) -> k b m t", t=4, m=P) if dealt else dst[:]
            nc.vector.tensor_copy(view, window.indirect(offsets[:, start // PER_COL : stop // PER_COL]))
            return dst

        def columns(tiles, m, width):
            first = max(f for f in tiles if f <= m)
            return tiles[first][:, (m - first) * width : (m - first + 1) * width]

        ag_w, ag_s, bg_w, bg_s, h_in, h_w, h_s, y, placed = {}, {}, {}, {}, {}, {}, {}, {}, {}

        def gather_a_words(first, last, at=None):
            ag_w[first] = gather("ag_w%d" % first, at, U32, wa_w[:].bitcast(U32), a_list, first * H, last * H, True)

        def gather_a_scales(first, last, at=None):
            ag_s[first] = gather("ag_s%d" % first, at, U8, wa_s[:], a_list, first * H, last * H)

        def gather_b_words(first, last, at=None):
            bg_w[first] = gather("bg_w%d" % first, at, U32, wb_w[:].bitcast(U32), b_list, first * N, last * N, True)

        def gather_b_scales(first, last, at=None):
            bg_s[first] = gather("bg_s%d" % first, at, U8, wb_s[:], b_list, first * N, last * N)

        def product(number, planes, words, scales, moving_words, moving_scales):
            acc = bank(number, [P, len(planes), P])
            for t in planes:
                cols = slice(t * P, (t + 1) * P)
                nc.tensor.matmul_mx(
                    out=acc[:, t - planes.start, :], lhsT=words[:, cols].bitcast(FP8X4), lhsT_scale=scales[:, cols],
                    rhs=moving_words.bitcast(FP8X4), rhs_scale=moving_scales, start=True, stop=True,
                )
            return acc

        def first_layer(m, number, group, count):
            slots = slice(m * P, (m + 1) * P)
            acc = product(number, range(4), columns(ag_w, m, H), columns(ag_s, m, H), xg_w[:, slots], xg_s[:, slots])
            if group not in h_in:
                h_in[group] = sbuf([P, count * 4 * P], BF16, "h_in%d" % group)
            nc.scalar.activation(
                h_in[group][:, (m - group) * 4 * P : (m - group + 1) * 4 * P].rearrange("p (g i t) -> p g t i", i=4, t=4),
                acc[:].rearrange("p t (g i) -> p g t i", i=4), ACT.Gelu_apprx_tanh,
            )

        def quantise_h(first, last, words_at=None, scales_at=None):
            h_w[first] = sbuf([P, (last - first) * P], U32, "h_w%d" % first, words_at)
            h_s[first] = sbuf([P, (last - first) * P], U8, "h_s%d" % first, scales_at)
            nc.vector.quantize_mx(out=h_w[first][:].bitcast(FP8X4), scales=h_s[first][:], in_=h_in[first][:])

        def second_layer(m, number, group, count, planes=range(4)):
            acc = product(
                number, planes, columns(bg_w, m, N), columns(bg_s, m, N), columns(h_w, m, P), columns(h_s, m, P)
            )
            if group not in y:
                y[group] = sbuf([P, 4, count * P], F32, "y%d" % group)
            factor = gate_b[:, (m - 1) * P : m * P] if m else gate_a[:]
            nc.vector.tensor_tensor(
                y[group][:, planes.start : planes.stop, (m - group) * P : (m - group + 1) * P], acc[:],
                factor.unsqueeze(1).to_broadcast([P, len(planes), P]), MULT,
            )

        def scatter(engine, t, first, last):
            if t not in placed:
                placed[t] = sbuf([P, T], F32, "placed%d" % t)
            window = placed[t][:].indirect(tok_list[:, first * P // PER_COL : last * P // PER_COL])
            group = max(f for f in y if f <= first)
            values = y[group][:, t, (first - group) * P : (last - group) * P]
            if engine == "vector":
                nc.vector.tensor_copy(window, values)
            else:
                nc.scalar.activation(window, values, ACT.Copy)

        xg_w = gather("xg_w", None, U32, x_w[:].bitcast(U32), tok_list, 0, T)
        xg_s = gather("xg_s", None, U8, x_s[:], tok_list, 0, T)
        gather_a_scales(0, 3)
        gather_a_scales(3, 6)
        gather_a_words(0, 1, ag0_at)
        gather_a_words(1, 3)
        gather_a_words(3, 4)
        gather_a_words(4, 5)
        gather_a_words(5, 6)
        h_in[0] = sbuf([P, HALF * 4 * P], BF16, "h_in0", h_at)
        for m in range(B):
            first_layer(m, m, m - m % HALF, HALF)
        gather_b_scales(0, 1, ag0_at)
        quantise_h(0, 3)
        wd_w = sbuf([P, 2 * N], U8, "wd_w", h_at)
        nc.gpsimd.tensor_copy(
            wd_w[:].rearrange("k (t p d) -> k t p d", t=4, d=2), w_w[:].rearrange("k (p t d) -> k t p d", t=4, d=2)
        )
        wd_s = sbuf([P, N], U8, "wd_s", h_at + 2 * N)
        nc.gpsimd.tensor_copy(wd_s[:].rearrange("k (t p) -> k t p", t=4), w_s[:].rearrange("k (p t) -> k t p", t=4))
        gather_b_words(0, 1)
        gather_b_words(1, 2, bg1_at)
        second_layer(0, 6, 0, 1, range(0, 2))
        second_layer(0, 7, 0, 1, range(2, 4))
        gather_b_scales(1, 3, gate_at + 4 * P - LAP)
        quantise_h(3, 6, None, gate_at + LAP)
        gather_b_words(2, 3, bg2_at)
        second_layer(1, 0, 1, 1)
        gather_b_words(3, 4, bg3_at)
        second_layer(2, 6, 2, 1)
        gather_b_scales(3, 6, bg2_at + LAP)
        gather_b_words(4, 5, bg4_at)
        second_layer(3, 7, HALF, HALF)
        gather_b_words(5, 6, bg5_at)
        second_layer(4, 6, HALF, HALF)
        second_layer(5, 7, HALF, HALF)
        for m in range(HALF):
            for t in range(4):
                scatter("scalar", t, m, m + 1)
        for t in (0, 1):
            scatter("vector", t, 3, 4)
        for t in (2, 3):
            scatter("scalar", t, 3, 4)
        scatter("scalar", 1, 4, 5)
        scatter("vector", 0, 4, B)
        scatter("vector", 1, 5, B)
        for t in (2, 3):
            scatter("scalar", t, 4, B)

        wide_banks = (0, 1, 2, 3)
        rest = {0: bank(4, [P, 2, T - BANK]), 1: bank(5, [P, 2, T - BANK])}
        rest_of = [rest[t // 2][:, t % 2, :] for t in range(4)]
        wide = {}
        for t in range(4):
            wide[t] = bank(wide_banks[t], [P, BANK])
            for out, toks in ((wide[t][:], slice(0, BANK)), (rest_of[t], slice(BANK, T))):
                nc.tensor.matmul_mx(
                    out=out, lhsT=wd_w[:, 2 * t * P : 2 * (t + 1) * P].bitcast(FP4X4),
                    lhsT_scale=wd_s[:, t * P : (t + 1) * P],
                    rhs=x_w[:, toks].bitcast(FP8X4), rhs_scale=x_s[:, toks], start=True, stop=True,
                )

        result = sbuf([P, 4, T], F32, "result")
        out_rows = out_0.rearrange("(p t) c -> p t c", t=4)
        out_in = [sbuf([P, stop - start, 4], BF16, "out_in%d" % start) for start, stop in CHUNKS]

        def rounding(c):
            toks = slice(*CHUNKS[c])
            return (
                out_in[c][:].rearrange("p (g i) t -> p g t i", i=4),
                result[:, :, toks].rearrange("p t (g i) -> p g t i", i=4),
            )

        def add(t, start, stop):
            sums = wide[t][:, start:stop] if stop <= BANK else rest_of[t][:, start - BANK : stop - BANK]
            nc.vector.tensor_tensor(result[:, t, start:stop], sums, placed[t][:, start:stop], ADD)

        for t in range(3):
            add(t, 0, BANK)
            add(t, BANK, T)
            nc.sync.dma_start(out=out_rows[:, t, :], in_=result[:, t, :])
        for c in (1, 2, 0, 3):
            add(3, *CHUNKS[c])
        nc.sync.dma_start(out=out_rows[:, 3, :], in_=result[:, 3, :])
        for c in (1, 2):
            nc.scalar.copy(*rounding(c))
        for c in (0, 3):
            nc.vector.tensor_copy(*rounding(c))

        out_w = sbuf([P, T], U32, "out_w")
        out_s = sbuf([P, T], U8, "out_s")
        word_rows = out_1[0].rearrange("p c d -> p (c d)").bitcast(I32)
        for c in (0, 3, 1, 2):
            toks = slice(*CHUNKS[c])
            nc.vector.quantize_mx(
                out=out_w[:, toks].bitcast(FP8X4), scales=out_s[:, toks],
                in_=out_in[c][:].rearrange("p j d -> p (j d)"),
            )
            if c > 0:
                stored = slice(0 if c == 1 else toks.start, toks.stop)
                nc.sync.dma_start(out=word_rows[:, stored], in_=out_w[:, stored].bitcast(I32))
        scale_rows = out_2[0].bitcast(I32)
        for q in range(4):
            queue = nc.scalar if q % 2 else nc.sync
            queue.dma_start(out=scale_rows[4 * q : 4 * q + 4, :], in_=out_s[:].bitcast(I32)[32 * q : 32 * q + 4, :])
